import numpy as np, ml_dtypes
CORES = [83,85,87,115,117,119]
N = 6
import mx_ref
BF = ml_dtypes.bfloat16
def f(rng, *shape):
    return mx_ref.flush((rng.standard_normal(shape, dtype=np.float32) * np.exp2(rng.integers(-2, 3, shape[:-1] + (1,)))).astype(BF))
def wide(rng, *shape, cols=0):
    v = rng.standard_normal(shape, dtype=np.float32) * np.exp2(rng.integers(-12, 13, shape)).astype(np.float32)
    if cols: v *= np.repeat(np.exp2(rng.integers(-cols, cols + 1, shape[:-2] + (1, shape[-1] // 4))) * (rng.random(shape[:-2] + (1, shape[-1] // 4)) > 0.0625), 4, axis=-1).astype(np.float32)
    return mx_ref.flush(v.astype(BF))
def cols(t, e):
    v = np.concatenate([t.reshape(128, -1, 4), np.zeros((128, 1, 4), BF)], axis=1)
    return np.ascontiguousarray(v[:, e]).reshape(128, -1)
def tile(rs):
    return np.stack(rs, axis=2).reshape(128, -1).astype(BF)
def cut(t, i, w=512):
    return t[:, w * i:w * i + w]
def decode(q):
    o = []
    for b in range(4):
        e = np.zeros((128, 128, 4), np.float32); e[np.arange(128), np.arange(128), b] = 1
        o.append(mx_ref.matmul(mx_ref.quantize(e.reshape(128, 512).astype(BF)), q))
    return np.stack(o, axis=2).reshape(128, -1)
T, CK = 384, 96
def gates(g):
    t = np.zeros((128, 512), BF); t[:, :4 * N] = g
    return np.stack([t] * N)
def plus(g):
    return np.maximum(np.abs(g.astype(np.float32)), np.float32(0.0625)).astype(BF)
def apart(rng):
    g = np.zeros((128, 4 * N), BF)
    for e in range(N): g[8 * e:8 * e + 8, 4 * e:4 * e + 4] = plus(f(rng, 8, 4))
    return g
def setup_inputs(rng):
    return {"x": f(rng, N, 128, 4 * T), "wg": gates(f(rng, 128, 4 * N)), "w1": f(rng, N, 128, 2048)}
def setup_inputs_alike(rng):
    d = setup_inputs(rng); d["wg"] = gates(np.tile(f(rng, 128, 4), (1, N))); return d
def setup_inputs_ties(rng):
    d = setup_inputs(rng); d["wg"] = gates(plus(f(rng, 128, 4 * N))); d["x"] = -plus(d["x"])
    for s in range(N):
        k = rng.permutation(np.arange(T) // 5 if s % 2 else np.arange(T) % (T // (CK + 1)))
        d["x"][s] = d["x"][s].reshape(128, T, 4)[:, k].reshape(128, -1)
    return d
def setup_inputs_split(rng):
    d = setup_inputs(rng); g = apart(rng)
    v = d["x"].astype(np.float32).reshape(N, 128, T, 4)
    for s in range(N):
        p = rng.permutation(T)
        for e in range(N):
            sign = np.full((1, T, 1), -1, np.float32); sign[:, p[(e * CK + np.arange(CK)) % T]] = 1
            v[s, 8 * e:8 * e + 8] = np.abs(v[s, 8 * e:8 * e + 8]) * sign
    d["x"] = v.reshape(N, 128, 4 * T).astype(BF); d["wg"] = gates(g); return d
def setup_inputs_zeros(rng):
    d = setup_inputs(rng); g = apart(rng)
    v = d["x"].astype(np.float32).reshape(N, 128, T, 4)
    for s in range(N):
        for e in range(N):
            p = rng.permutation(T); u = np.abs(v[s, 8 * e:8 * e + 8])
            u[:, p[CK // 2:CK // 2 + CK]] = np.where(rng.random((8, CK, 4)) < 0.5, np.float32(-0.0), np.float32(0.0))
            u[:, p[CK // 2 + CK:]] *= np.float32(-1)
            v[s, 8 * e:8 * e + 8] = u
    d["x"] = v.reshape(N, 128, 4 * T).astype(BF); d["wg"] = gates(g); return d
def setup_inputs_spread(rng):
    d = setup_inputs(rng); d["x"] = wide(rng, N, 128, 4 * T, cols=6); return d
def check_inputs(d):
    b = []
    g = d["wg"].astype(np.float32)
    if (g != g[0]).any() or (g[:, :, 4 * N:] != 0).any(): b.append("wg")
    return b
def reference(x, wg, w1):
    took = []
    for s in range(N):
        z = mx_ref.matmul(mx_ref.quantize(wg[s]), mx_ref.quantize(x[s])) + np.float32(0.0)
        took.append([np.argsort(-z[e], kind="stable")[:CK] for e in range(N)])
    y = np.zeros((N, 128, T, 4), np.float32)
    for e in range(N):
        q = mx_ref.quantize(np.concatenate([cols(x[s], took[s][e]) for s in range(N)], axis=1))
        rs = [np.maximum(mx_ref.matmul(mx_ref.quantize(np.ascontiguousarray(cut(w1[e], i))), q), np.float32(0.0)) * np.float32(0.05) for i in range(4)]
        v = decode(mx_ref.quantize(tile(rs))).reshape(128, N, CK, 4)
        for s in range(N): y[s][:, took[s][e]] += v[:, s]
    return {"y": y.reshape(N, 128, 4 * T)}

@@ -1,0 +1,563 @@
+from concourse.bass import DstId, RemoteDMATransfer
+from concourse.mybir import dt, AluOpType, ActivationFunctionType
+
+OP = AluOpType
+AF = ActivationFunctionType
+NT, CK, N = 384, 96, 6
+BIG = 1e29
+F8, U8, F32, BF, U16, I32 = "float8_e4m3fn_x4", "uint8", "float32", "bfloat16", "uint16", "int32"
+
+FAR0, NEAR0, OWN0, ALLC = 0, 3 * CK, 5 * CK, 5 * CK + 128
+HALF = NT // 2
+NP = CK * (N - 1)
+ROUNDS = ({"k": "1", "W": 32, "NS": 5, "bank": 0}, {"k": "2", "W": 64, "NS": 3, "bank": 2})
+
+SHAPES = {
+    BF: {"xsb": 4 * NT, "wgs": 32, "wga1": 512, "wga2": 512, "w1s": 2048, "ones": 512, "et": 2048, "reset1": NT, "reset2": NT,
+         "reset4": NP, "xt": 4 * ALLC, "rt": 4 * ALLC},
+    F8: {"qx": NT, "qg1": 128, "qg2": 128, "qw": 512, "qe": 512, "ct": ALLC, "rxn": 192, "rxf": 288, "rc": ALLC, "bkn": 192, "bkf": 288},
+    U8: {"px": NT, "pg1": 128, "pg2": 128, "pw": 512, "pe": 512, "cs": ALLC, "rxns": 192, "rxfs": 288, "rs": ALLC, "bkns": 192, "bkfs": 288},
+    I32: {"pi": 2, "pci": 8},
+    U16: {"offw": 64, "off4": 144, "off16": 36, "offc": 216},
+    F32: {"pc": 8, "offwf": 64, "k1": NT, "k2": NT, "im4": 32, "im16": 32, "k4s": CK, "k16s": CK, "k4": NP, "cut1": 12, "cut2": 6,
+          "slots": 576, "mask4": 32, "mask16": 32, "rr4": CK, "rr16": CK, "mcol": 4, "v2": 6, "offf": 36,
+          "cl": NP + NT, "cm": NP + NT, "cq": NP + NT, "aa": 8 + 4 * 576, "yy": 4 * NT},
+}
+for R in ROUNDS:
+    k, n, ns = R["k"], NT // R["W"], R["NS"]
+    R["n"] = n
+    SHAPES[BF].update({"cmp" + k: n * NT, "sums" + k: (n - ns) * HALF, "eqw" + k: NT, "corr" + k: NT})
+    SHAPES[U16].update({"offr" + k: n})
+    SHAPES[F32].update({"m3" + k: NT, "rr" + k: NT, "md" + k: NT, "sc" + k: NT, "acc" + k: ns, "accb" + k: ns, "accc" + k: ns, "rk" + k: ns, "rkb" + k: ns,
+                        "first" + k: n, "tok" + k: 16 * n, "tokf" + k: 16 * n, "win" + k: NT, "t1" + k: CK, "wa" + k: CK, "t2" + k: CK, "s4" + k: CK,
+                        "wb" + k: CK, "t3" + k: CK, "s16" + k: CK})
+SCRATCH = {name: ("sbuf", [128, n], kind) for kind in SHAPES for name, n in SHAPES[kind].items()}
+SCRATCH["pp"] = ("psum", [128, 4096], F32)
+SEMAPHORES = ["sv", "sa", "sten", "sp", "ldx", "ldx2", "ldg", "ldw", "sty", "sty2", "loc", "dn", "df", "rn", "rf"]
+
+
+def rank_program(g, core, T, topo):
+    me = T.rank_of(core)
+    if me is None:
+        return
+    cores = list(T.cores)
+
+    def far_of(r):
+        return [k for k in range(N) if topo.chip(cores[k]) != topo.chip(cores[r])]
+
+    def near_of(r):
+        return [k for k in range(N) if k != r and topo.chip(cores[k]) == topo.chip(cores[r])]
+
+    far, near = far_of(me), near_of(me)
+    order = far + near + [me]
+    idx = {e: i for i, e in enumerate(order)}
+    pos = {e: CK * idx[e] for e in order}
+
+    Q = {"v": (g.vector, "sv"), "a": (g.scalar, "sa"), "t": (g.tensor, "sten"), "p": (g, "sp"), "s": (g.sync, None)}
+    count = {"sv": 0, "sa": 0, "sten": 0, "sp": 0}
+    seen = {}
+
+    def need(q, deps):
+        for d in deps:
+            if d is not None and seen.get((q, d[0]), 0) < d[1]:
+                Q[q][0].wait_ge(T.sem[d[0]], d[1])
+                seen[(q, d[0])] = d[1]
+
+    def done(q, ins):
+        s = Q[q][1]
+        ins.then_inc(T.sem[s], 1)
+        count[s] += 1
+        if q == "p":
+            need("p", [(s, count[s])])
+        return (s, count[s])
+
+    V, A, TE = g.vector, g.scalar, g.tensor
+
+    g.sync.dma_start(T.xsb[:, 0:4 * HALF], T.x[:, 0:4 * HALF]).then_inc(T.sem["ldx"], 16)
+    g.scalar.dma_start(T.wgs[:], T.wg[:, 0:32]).then_inc(T.sem["ldg"], 16)
+    g.sync.dma_start(T.xsb[:, 4 * HALF:4 * NT], T.x[:, 4 * HALF:4 * NT]).then_inc(T.sem["ldx2"], 16)
+    g.sync.dma_start(T.w1s[:], T.w1[:]).then_inc(T.sem["ldw"], 16)
+    LDX, LDX2, LDG, LDW = ("ldx", 16), ("ldx2", 16), ("ldg", 16), ("ldw", 16)
+
+    def iota(name, pattern, base=0, cm=0):
+        if name == "pi":
+            return done("p", g.iota(T.pi[:], pattern, base, cm))
+        return done("p", g.iota(T[name][:], pattern, base, cm, allow_small_or_imprecise_dtypes=True))
+
+    c_pi = iota("pi", [[0, 2]], 0, 1)
+    c_k = {"1": iota("k1", [[0, 12], [1, 32]])}
+    c_im4 = iota("im4", [[0, 2], [1, 4], [0, 4]])
+    c_im16 = iota("im16", [[0, 2], [1, 16]])
+    c_k4s = iota("k4s", [[0, 24], [1, 4]])
+    c_k16s = iota("k16s", [[0, 6], [1, 16]])
+    c_cut = {"1": iota("cut1", [[32, 12]], 32)}
+    c_k["2"] = iota("k2", [[0, 6], [1, 64]])
+    c_tokf = {"1": iota("tokf1", [[32, 12], [1, 16]]), "2": iota("tokf2", [[64, 6], [1, 16]])}
+    c_cut["2"] = iota("cut2", [[64, 6]], 64)
+    c_slots = iota("slots", [[1, 576]], 1)
+    c_k4 = iota("k4", [[0, NP // 4], [1, 4]])
+
+    for i in range(4):
+        done("v", V.memset(T.offwf[:, 8 * i:8 * i + 8], float(4 * order[i])))
+    for i in (4, 5):
+        c_offwf = done("v", V.memset(T.offwf[:, 16 * i - 32:16 * i - 16], float(4 * order[i])))
+    c_ones = done("v", V.memset(T.ones[:], 1.0))
+    P3, P15, W31, W63, H16, H48, PM = range(7)
+    need("v", [c_pi])
+    for k, m in enumerate((3, 15, 31, 63, 16, 48)):
+        done("v", V.tensor_scalar(T.pci[:, k:k + 1], T.pi[:, 0:1], m, None, OP.bitwise_and))
+    done("v", V.tensor_scalar(T.pci[:, PM:PM + 1], T.pi[:, 0:1], 15, 2, OP.bitwise_and, OP.logical_shift_right))
+    d = done("v", V.tensor_scalar(T.pci[:, 7:8], T.pi[:, 0:1], 0, None, OP.bitwise_and))
+    c_win = [done("v", V.memset(T[w][:, 0:CK], 0.0)) for w in ("win1", "win2")][-1]
+    need("v", [d])
+    c_pc = done("v", V.tensor_copy(T.pc[:], T.pci[:]))
+    c_v2 = done("v", V.memset(T.v2[:], 0.0))
+
+    def pcol(k, lo=0, hi=128):
+        return T.pc[lo:hi, k:k + 1]
+
+    need("v", [c_offwf, c_pc])
+    c_offw = done("v", V.tensor_scalar(T.offw[:], T.offwf[:], pcol(P3), None, OP.add))
+    c_m3 = {}
+
+    def m3(k, col):
+        need("v", [c_k[k]])
+        c_m3[k] = done("v", V.tensor_scalar(T["m3" + k][:], T["k" + k][:], pcol(col), -BIG, OP.not_equal, OP.mult))
+
+    m3("1", W31)
+    c_xpad = done("v", V.memset(T.xt[:, 4 * (OWN0 + CK):4 * ALLC], 0.0))
+    c_aa = done("v", V.memset(T.aa[:, 0:4], 0.0))
+
+    c_reset, c_rr, c_tok, a_wga = {}, {}, {}, {}
+
+    def reset(k):
+        need("a", [c_k[k]])
+        c_reset[k] = done("a", A.activation(T["reset" + k][:], T["k" + k][:], AF.Sign))
+
+    def rr(k):
+        need("a", [c_reset[k]])
+        c_rr[k] = done("a", A.activation(T["rr" + k][:], T["reset" + k][:], AF.Copy, bias=-BIG, scale=BIG))
+
+    def tokens(k, col):
+        need("a", [c_tokf[k], c_pc])
+        c_tok[k] = done("a", A.activation(T["tok" + k][:], T["tokf" + k][:], AF.Identity, bias=pcol(col)))
+
+    def gates(k, lo):
+        need("a", [c_offw, LDG])
+        a_wga[k] = done("a", A.activation(T["wga" + k][:], T.wgs[:, 0:32].indirect(T.offw[:, lo:lo + 32]), AF.Copy))
+
+    reset("1")
+    gates("1", 0)
+    rr("1")
+    gates("2", 32)
+    tokens("1", H16)
+    reset("2")
+    tokens("2", H48)
+
+    need("p", [c_ones])
+
+    def one_tile(b):
+        return done("p", g.affine_select(T.et[:, 512 * b:512 * b + 512], T.ones[:], [[-1, 512]], OP.is_equal, 0.0, b, 4))
+
+    c_et = [one_tile(0), one_tile(1)]
+
+    need("v", [a_wga["1"]])
+    done("v", V.quantize_mx(T.qg1[:], T.pg1[:], T.wga1[:]))
+    need("v", [LDX])
+    done("v", V.quantize_mx(T.qx[:, 0:HALF], T.px[:, 0:HALF], T.xsb[:, 0:4 * HALF]))
+    need("v", [c_im4, c_im16, c_k4s, c_k16s])
+    done("v", V.tensor_scalar(T.mask4[:], T.im4[:], pcol(P3), -BIG, OP.not_equal, OP.mult))
+    done("v", V.tensor_scalar(T.mask16[:], T.im16[:], pcol(P15), -BIG, OP.not_equal, OP.mult))
+    done("v", V.tensor_scalar(T.mcol[:], T.k4s[:, 0:4], pcol(PM), 4.0, OP.is_equal, OP.mult))
+    done("v", V.tensor_scalar(T.rr4[:], T.k4s[:], 0.0, -BIG, OP.is_equal, OP.mult))
+    c_lists = done("v", V.tensor_scalar(T.rr16[:], T.k16s[:], 0.0, -BIG, OP.is_equal, OP.mult))
+    need("v", [LDX2])
+    v_qx = done("v", V.quantize_mx(T.qx[:, HALF:NT], T.px[:, HALF:NT], T.xsb[:, 4 * HALF:4 * NT]))
+    m3("2", W63)
+    need("v", [a_wga["2"]])
+    v_qg2 = done("v", V.quantize_mx(T.qg2[:], T.pg2[:], T.wga2[:]))
+    t_z = {}
+    for R, dep in zip(ROUNDS, (v_qx, v_qg2)):
+        k = R["k"]
+        need("t", [dep])
+        t_z[k] = [done("t", TE.matmul_mx(T.pp[:, 512 * b:512 * b + NT], T["qg" + k][:], T["pg" + k][:], T.qx[:], T.px[:], True, True)) for b in (R["bank"], R["bank"] + 1)]
+
+    def z(R, other, lo=0, hi=NT):
+        o = 512 * (R["bank"] + other)
+        return T.pp[:, o + lo:o + hi]
+
+    v_sc = {}
+
+    def own_mask(R, lo, hi):
+        k = R["k"]
+        need("v", [t_z[k][0], c_m3[k]])
+        return done("v", V.tensor_tensor(T["md" + k][:, lo:hi], z(R, 0, lo, hi), T["m3" + k][:, lo:hi], OP.add))
+
+    def own_scan(R, lo, hi, dep):
+        k = R["k"]
+        need("v", [dep, c_rr[k]])
+        v_sc[k + str(lo)] = done("v", V.tensor_tensor_scan(T["sc" + k][:, lo:hi], T["rr" + k][:, lo:hi], T["md" + k][:, lo:hi], 0.0, OP.add, OP.max))
+
+    a_acc = {}
+
+    def scalar_ranks(R):
+        k, W, ns = R["k"], R["W"], R["NS"]
+        need("a", [t_z[k][1], v_sc[k + "0"]])
+        cmp, signs = T["cmp" + k], []
+        for q in range(ns + 1):
+            if q < ns:
+                signs.append(done("a", A.activation(cmp[:, NT * q:NT * q + NT], z(R, 1), AF.Sign, bias=T["sc" + k][:, W * q + W - 1:W * q + W], scale=-1.0)))
+            if q:
+                j, c = q - 1, NT * (q - 1)
+                lower, higher = cmp[:, c:c + W * q], cmp[:, c + W * q:c + NT]
+                need("a", [signs[j]])
+                done("a", A.activation(lower, lower, AF.Relu, accum_out=T["acc" + k][:, j:j + 1]))
+                a_acc[k] = done("a", A.activation(higher, higher, AF.Relu, scale=-1.0, accum_out=T["accb" + k][:, j:j + 1]))
+
+    v_eq = {}
+
+    def vector_ranks(R, fill):
+        k, W, ns, n = R["k"], R["W"], R["NS"], R["n"]
+        cmp, sc, corr, first, offr = T["cmp" + k], T["sc" + k], T["corr" + k], T["first" + k], T["offr" + k]
+        s0 = W * ns
+
+        def total(q, deps):
+            o, c = HALF * (q - ns), NT * q
+            need("v", deps)
+            return done("v", V.tensor_tensor_scan(T["sums" + k][:, o:o + HALF], cmp[:, c:c + HALF], cmp[:, c + HALF:c + NT], first[:, q:q + 1], OP.add, OP.add))
+
+        need("v", [v_sc[k + str(s0)]])
+        v_eq[k] = done("v", V.tensor_tensor(T["eqw" + k][:], z(R, 0), sc[:], OP.is_equal))
+        late = []
+        for q in range(ns, n):
+            s = sc[:, W * q + W - 1:W * q + W]
+            cut, c = W * q + W, NT * q
+            d = done("v", V.tensor_scalar(cmp[:, c:c + cut], z(R, 0, 0, cut), s, None, OP.is_ge))
+            if cut < NT:
+                d = done("v", V.tensor_scalar(cmp[:, c + cut:c + NT], z(R, 0, cut, NT), s, None, OP.is_gt))
+            late.append((q, d))
+            if q == ns:
+                need("v", [v_eq[k], c_reset[k]])
+                v_corr = done("v", V.tensor_tensor_scan(corr[:], T["reset" + k][:], T["eqw" + k][:], 0.0, OP.mult, OP.add))
+            elif q == ns + 1:
+                need("v", [v_corr, c_cut[k]])
+                v_first = done("v", V.tensor_scalar(first[:], corr[:, W - 1:NT:W], -1.0, -float(HALF), OP.mult, OP.add))
+                v_k = done("v", V.tensor_tensor(T["rkb" + k][:], T["cut" + k][:, 0:ns], corr[:, W - 1:s0:W], OP.subtract))
+            else:
+                j, d = late.pop(0)
+                total(j, [d, v_first])
+        j, d = late.pop(0)
+        total(j, [d, v_first])
+        need("v", [a_acc[k], v_k])
+        d0 = done("v", V.tensor_tensor(T["accc" + k][:], T["accb" + k][:], T["acc" + k][:], OP.subtract))
+        j, d = late.pop(0)
+        v_sum = total(j, [d])
+        need("v", [d0])
+        d0 = done("v", V.tensor_tensor(T["rk" + k][:], T["accc" + k][:], T["rkb" + k][:], OP.add))
+        need("v", [v_sum])
+        done("v", V.tensor_scalar(offr[:, ns:n], T["sums" + k][:, HALF - 1:HALF * (n - ns):HALF], float(HALF), None, OP.add))
+        need("v", [d0])
+        v_offr = done("v", V.tensor_copy(offr[:, 0:ns], T["rk" + k][:]))
+        fill()
+        need("v", [v_offr, c_tok[k], c_win])
+        return done("v", V.tensor_copy(T["win" + k][:, 0:NT].indirect(offr[:, 0:n]), T["tok" + k][:]))
+
+    v_t3, v_s16, off = {}, {}, {}
+
+    def lists(R, v_win, fill):
+        k = R["k"]
+        t1 = T["t1" + k]
+        fill()
+        need("v", [v_win, c_lists])
+        d = done("v", V.transpose(t1[:], T["win" + k][:, 0:CK]))
+        fill()
+        need("v", [d])
+        if k == "1":
+            pair = [(t1[:, 32 * u:32 * u + 1], t1[:, 32 * u + 16:32 * u + 17]) for u in range(3)]
+        else:
+            for b in (0, 64):
+                d = done("v", V.tensor_tensor(T.v2[b:b + 32, :], t1[b:b + 32, 0:CK:16], t1[b + 32:b + 64, 0:CK:16], OP.add))
+            pair = [(T.v2[:, 2 * u:2 * u + 1], T.v2[:, 2 * u + 1:2 * u + 2]) for u in range(3)]
+            fill()
+            need("v", [d, c_v2])
+
+        def under(w, mask, u):
+            return done("v", V.tensor_scalar(T[w + k][:, 32 * u:32 * u + 32], T[mask][:], pair[u][0], pair[u][1], OP.add, OP.add))
+
+        d = [under("wa", "mask4", u) for u in range(3)][-1]
+        under("wb", "mask16", 0)
+        need("v", [d])
+        d = done("v", V.transpose(T["t2" + k][:], T["wa" + k][:]))
+        under("wb", "mask16", 1)
+        need("v", [d])
+        d = done("v", V.tensor_tensor_scan(T["s4" + k][:], T.rr4[:], T["t2" + k][:], 0.0, OP.add, OP.max))
+        e = under("wb", "mask16", 2)
+        need("v", [d])
+
+        def offsets(i, block, blocks):
+            for b in blocks:
+                off[i] = done("v", V.tensor_scalar(T.off4[32 * b:32 * b + 32, 24 * i:24 * i + 24], T["s4" + k][32 * block:32 * block + 32, 3:CK:4], 4.0, pcol(P3, 32 * b, 32 * b + 32), OP.mult, OP.add))
+
+        def upper(lo, hi):
+            need("v", [off[hi - 1]])
+            d = done("v", V.tensor_copy(T.off4[64:128, 24 * lo:24 * hi], T.off4[0:64, 24 * lo:24 * hi]))
+            for i in range(lo, hi):
+                off[i] = d
+
+        if k == "1":
+            offsets(0, 0, range(4))
+            offsets(1, 1, (0, 1))
+            offsets(2, 2, (0, 1))
+            offsets(3, 3, (0, 1))
+        else:
+            offsets(4, 0, (0, 1))
+            offsets(5, 2, (0, 1))
+        need("v", [e])
+        v_t3[k] = done("v", V.transpose(T["t3" + k][:], T["wb" + k][:]))
+        if k == "1":
+            upper(1, 4)
+        else:
+            upper(4, 6)
+
+    def singles(k):
+        need("v", [v_t3[k]])
+        v_s16[k] = done("v", V.tensor_tensor_scan(T["s16" + k][:], T.rr16[:], T["t3" + k][:], 0.0, OP.add, OP.max))
+
+    def gather(q, e):
+        i = idx[e]
+        out = T.xt[:, 4 * pos[e]:4 * pos[e] + 4 * CK]
+        win = T.xsb[:, 0:4 * NT].indirect(T.off4[:, 24 * i:24 * i + 24])
+        need(q, [off[i], LDX, LDX2])
+        return done(q, A.activation(out, win, AF.Copy) if q == "a" else V.tensor_copy(out, win))
+
+    def pack(lo, hi, deps, src, qc, qs):
+        need("v", deps)
+        return done("v", V.quantize_mx(T[qc][:, lo:hi], T[qs][:, lo:hi], T[src][:, 4 * lo:4 * hi]))
+
+    local = [0]
+
+    def lanes(isfar, bits, i):
+        if not isfar:
+            return (8 + 4 * i, 12 + 4 * i)
+        return (2 * i, 2 * i + 2) if bits else ((6, 7), (7, 8), (0, 4))[i]
+
+    def arrivals(isfar):
+        n = 0
+        for r in (far if isfar else near):
+            i = (far_of(r) if isfar else near_of(r)).index(me)
+            for bits in (True, False):
+                lo, hi = lanes(isfar, bits, i)
+                n += hi - lo
+        return n
+
+    def send(isfar, dep, codes, planes, dcodes, dplanes, rsem):
+        need("p", [dep])
+        for bits, sname, dname in ((True, codes, dcodes), (False, planes, dplanes)):
+            tr = []
+            for i, r in enumerate(far if isfar else near):
+                lo, hi = lanes(isfar, bits, i)
+                es = topo.engines(core, cores[r])[lo:hi]
+                there = (far_of(r) if isfar else near_of(r)).index(me) * CK
+                src = T[sname][:, pos[r]:pos[r] + CK]
+                dst = T[dname][:, there:there + CK]
+                if bits:
+                    src, dst = src.bitcast(dt.uint8), dst.bitcast(dt.uint8)
+                ad = topo.addr(cores[r])
+                tr.append(RemoteDMATransfer(dst_ids=[DstId(rid=ad[0], pnc=ad[1])], dma_engine_mask=sum(1 << k for k in es), remote_sem=T.sem[rsem], src=src, dst=dst))
+                local[0] += len(es)
+            g.remote_dma_fused(tr, local_sem=T.sem["loc"])
+
+    DF, DN, RF, RN = ("df", arrivals(True)), ("dn", arrivals(False)), ("rf", arrivals(True)), ("rn", arrivals(False))
+
+    def qweight(i):
+        need("v", [LDW])
+        return done("v", V.quantize_mx(T.qw[:, 128 * i:128 * i + 128], T.pw[:, 128 * i:128 * i + 128], T.w1s[:, 512 * i:512 * i + 512]))
+
+    def qunpack(i):
+        need("v", [c_et[i]])
+        return done("v", V.quantize_mx(T.qe[:, 128 * i:128 * i + 128], T.pe[:, 128 * i:128 * i + 128], T.et[:, 512 * i:512 * i + 512]))
+
+    def filler(steps):
+        steps = list(steps)
+
+        def fill(n=1):
+            for _ in range(min(n, len(steps))):
+                steps.pop(0)()
+        return fill
+
+    R1, R2 = ROUNDS
+    s1, s2 = R1["W"] * R1["NS"], R2["W"] * R2["NS"]
+    d1, d2 = own_mask(R1, 0, s1), own_mask(R1, s1, NT)
+    own_scan(R1, 0, s1, d1)
+    own_scan(R1, s1, NT, d2)
+    scalar_ranks(R1)
+    rr("2")
+    need("a", [c_k4])
+    c_r4 = done("a", A.activation(T.reset4[:], T.k4[:], AF.Sign))
+    c_cl = done("a", A.activation(T.cl[:, NP:NP + NT], T.k1[:], AF.Copy, scale=0.0))
+    md2 = []
+    fill = filler([lambda lo=lo: md2.append(own_mask(R2, lo, lo + 96)) for lo in range(0, NT, 96)])
+    v_win = vector_ranks(R1, fill)
+    lists(R1, v_win, fill)
+    for e in far[:2]:
+        a_gf = gather("a", e)
+    fill(4)
+    v_gf = gather("v", far[2])
+    v_qfar = pack(FAR0, NEAR0, [a_gf, v_gf], "xt", "ct", "cs")
+    send(True, v_qfar, "ct", "cs", "rxf", "rxfs", "df")
+    c_et += [one_tile(2), one_tile(3)]
+
+    own_scan(R2, 0, s2, md2[-1])
+    own_scan(R2, s2, NT, md2[-1])
+    singles("1")
+    scalar_ranks(R2)
+    a_gn = gather("a", near[0])
+
+    def spread(i):
+        k, block = ("1", i) if i < 4 else ("2", 2 * (i - 4))
+        need("a", [v_s16[k]])
+        for b in (0, 1):
+            d = done("a", A.activation(T.offf[32 * b:32 * b + 32, 6 * i:6 * i + 6], T["s16" + k][32 * block:32 * block + 32, 15:CK:16], AF.Copy))
+        return d
+
+    for i in range(4):
+        spread(i)
+    v_qw = []
+    fill = filler([lambda i=i: v_qw.append(qweight(i)) for i in range(4)])
+    fill()
+    v_win = vector_ranks(R2, fill)
+    lists(R2, v_win, fill)
+    v_gn = gather("v", near[1])
+    fill(4)
+    singles("2")
+    v_qnear = pack(NEAR0, OWN0, [a_gn, v_gn], "xt", "ct", "cs")
+    send(False, v_qnear, "ct", "cs", "rxn", "rxns", "dn")
+
+    def products(stat, plane, codes, planes, lo, hi, bank, deps):
+        need("t", deps)
+        r = []
+        for i in range(4):
+            c = slice(128 * i, 128 * i + 128)
+            o = 512 * (bank + i)
+            r.append(done("t", TE.matmul_mx(T.pp[:, o:o + hi - lo], T[stat][:, c], T[plane][:, c], T[codes][:, lo:hi], T[planes][:, lo:hi], True, True)))
+        return r
+
+    def relus(lo, hi, bank, deps):
+        for i in range(4):
+            need("a", [deps[i]])
+            o = 512 * (bank + i)
+            d = done("a", A.activation(T.rt[:, 4 * lo + i:4 * hi:4], T.pp[:, o:o + hi - lo], AF.Relu, scale=0.05))
+        return d
+
+    def slot(e):
+        return 4 * (1 + CK * e)
+
+    def unpack(q, e0, n, bank, col, b, dep):
+        need(q, [dep])
+        o = 512 * (bank + b) + col
+        out, src = T.aa[:, slot(e0) + b:slot(e0) + 4 * n:4], T.pp[:, o:o + n]
+        return done(q, V.tensor_copy(out, src) if q == "v" else A.activation(out, src, AF.Copy))
+
+    table = T.cl[:, NP:NP + NT]
+    tk = {"last": None}
+
+    def tab(k):
+        e = (k + 1) // 2
+        o16 = T.off16[:, 6 * idx[e]:6 * idx[e] + 6]
+        if k % 2:
+            need("a", [tk["last"], v_o16])
+            tk["last"] = done("a", A.activation(T.cl[:, CK * (e - 1):CK * e], table.indirect(o16), AF.Copy))
+            if e == N - 1:
+                mask(0, NP)
+        else:
+            need("v", [tk["last"]])
+            tk["last"] = done("v", V.tensor_copy(table.indirect(o16), T.slots[:, CK * e:CK * e + CK]))
+
+    def mask(lo, hi):
+        need("a", [tk["last"], c_lists])
+        for m in range(4):
+            tk[lo] = done("a", A.activation(T.cm[:, lo + m:hi:4], T.cl[:, lo + m:hi:4], AF.Copy, scale=T.mcol[:, m:m + 1]))
+
+    def wrap(lo, hi):
+        need("v", [tk[lo], c_r4])
+        d = done("v", V.tensor_tensor_scan(T.cq[:, lo:hi], T.reset4[:, 0:hi - lo], T.cm[:, lo:hi], 0.0, OP.mult, OP.add))
+        need("v", [d])
+        return done("v", V.tensor_scalar(T.offc[:, lo // 4:hi // 4], T.cq[:, lo + 3:hi:4], pcol(P3), None, OP.add))
+
+    p_far = products("qw", "pw", "rxf", "rxfs", 0, 288, 4, [DF, v_qw[-1]])
+    a_far = relus(FAR0, NEAR0, 4, p_far)
+    spread(4)
+    d = spread(5)
+    need("a", [d])
+    a_offf = done("a", A.activation(T.offf[64:128, :], T.offf[0:64, :], AF.Copy))
+    a_go = gather("a", me)
+    v_rfar = pack(FAR0, NEAR0, [a_far], "rt", "rc", "rs")
+    send(True, v_rfar, "rc", "rs", "bkf", "bkfs", "rf")
+
+    need("v", [a_offf])
+    v_o16 = done("v", V.tensor_copy(T.off16[:], T.offf[:]))
+    qunpack(0)
+    need("v", [v_o16, c_cl, c_slots])
+    tab(0)
+    v_qown = pack(OWN0, ALLC, [a_go, c_xpad], "xt", "ct", "cs")
+    tab(1)
+    p_own = products("qw", "pw", "ct", "cs", OWN0, ALLC, 0, [v_qown, v_eq["2"], a_acc["2"], v_win])
+    a_own = relus(OWN0, ALLC, 0, p_own)
+    tab(2)
+    tab(3)
+    qunpack(1)
+    v_rown = pack(OWN0, ALLC, [a_own], "rt", "rc", "rs")
+    tab(4)
+    p_near = products("qw", "pw", "rxn", "rxns", 0, 192, 4, [DN, a_far])
+    a_near = relus(NEAR0, OWN0, 4, p_near)
+    qunpack(2)
+    v_qe = qunpack(3)
+    v_rnear = pack(NEAR0, OWN0, [a_near], "rt", "rc", "rs")
+    send(False, v_rnear, "rc", "rs", "bkn", "bkns", "rn")
+    for k in range(5, 2 * N - 1):
+        tab(k)
+    mask(NP, NP + NT)
+
+    u_own = products("qe", "pe", "rc", "rs", OWN0, ALLC, 0, [v_rown, v_qe, a_own])
+    d_own = [unpack("a", me, CK, 0, 0, b, u_own[b]) for b in range(4)]
+    v_prev = wrap(0, NP)
+    v_last = wrap(NP, NP + NT)
+
+    u_near = products("qe", "pe", "bkn", "bkns", 0, 192, 4, [RN, a_near])
+    d_near = [unpack("a", near[i], CK, 4, CK * i, b, u_near[b]) for b in range(4) for i in range(2)]
+    u_far = products("qe", "pe", "bkf", "bkfs", 0, 288, 0, [RF, d_own[-1]])
+
+    def chain(e, deps):
+        need("v", deps + [v_prev, c_aa])
+        o = 24 * (e - 1)
+        s = slice(slot(e), slot(e) + 4 * CK)
+        return done("v", V.tensor_tensor(T.aa[:, s], T.aa[:, 0:slot(e)].indirect(T.offc[:, o:o + 24]), T.aa[:, s], OP.add))
+
+    dlast = [d_own[-1], d_near[-1]]
+    step = None
+    if far[0] != 0:
+        for e in (1, 2):
+            step = chain(e, dlast + [step])
+    d1 = [unpack("v", far[0], 3 * CK, 0, 0, b, u_far[b]) for b in (0, 1)][-1]
+    d2 = [unpack("a", far[0], 3 * CK, 0, 0, b, u_far[b]) for b in (2, 3)][-1]
+    for e in range(1 if far[0] == 0 else 3, N):
+        step = chain(e, dlast + [d1, d2, step])
+
+    win = T.aa[:, 0:slot(N)]
+    for q, quarters in (("v", (0, 1)), ("a", (2, 3))):
+        need(q, [step, v_last])
+        r = []
+        for k in quarters:
+            o = NP // 4 + 24 * k
+            out, src = T.yy[:, NT * k:NT * k + NT], win.indirect(T.offc[:, o:o + 24])
+            r.append(done(q, V.tensor_copy(out, src) if q == "v" else A.activation(out, src, AF.Copy)))
+        dq, sem = ("s", "sty") if q == "v" else ("a", "sty2")
+        for k, d in zip(quarters, r):
+            need(dq, [d])
+            Q[dq][0].dma_start(T.y[:, NT * k:NT * k + NT], T.yy[:, NT * k:NT * k + NT]).then_inc(T.sem[sem], 16)
+
+    g.wait_ge(T.sem["loc"], local[0])
+    for s in count:
+        g.wait_ge(T.sem[s], count[s])
+    g.wait_ge(T.sem["sty"], 32)
+    g.wait_ge(T.sem["sty2"], 32)

@@ -5,35 +5,38 @@ OP = AluOpType
 AF = ActivationFunctionType
 NT, CK, N = 384, 96, 6
 BIG = 1e29
+STEP = 2.0 ** 90
 F8, U8, F32, BF, U16, I32 = "float8_e4m3fn_x4", "uint8", "float32", "bfloat16", "uint16", "int32"
 
 FAR0, NEAR0, OWN0, ALLC = 0, 3 * CK, 5 * CK, 5 * CK + 128
 HALF = NT // 2
+WIN = HALF + CK
 NP = CK * (N - 1)
-ROUNDS = ({"k": "1", "W": 32, "NS": 5, "bank": 0}, {"k": "2", "W": 64, "NS": 3, "bank": 2})
+ROUNDS = ({"k": "1", "W": 16, "NS": 5, "bank": 0, "G": 144, "views": (16, 0), "P": 128},
+          {"k": "2", "W": 32, "NS": 6, "bank": 2, "G": 192, "views": (64, 0), "P": 64})
 
 SHAPES = {
-    BF: {"xsb": 4 * NT, "wgs": 32, "wga1": 512, "wga2": 512, "w1s": 2048, "ones": 512, "et": 2048, "reset1": NT, "reset2": NT,
-         "reset4": NP, "xt": 4 * ALLC, "rt": 4 * ALLC},
-    F8: {"qx": NT, "qg1": 128, "qg2": 128, "qw": 512, "qe": 512, "ct": ALLC, "rxn": 192, "rxf": 288, "rc": ALLC, "bkn": 192, "bkf": 288},
-    U8: {"px": NT, "pg1": 128, "pg2": 128, "pw": 512, "pe": 512, "cs": ALLC, "rxns": 192, "rxfs": 288, "rs": ALLC, "bkns": 192, "bkfs": 288},
+    BF: {"xsb": 4 * NT, "wgs": 32, "w1s": 2048, "ones": 512, "et": 2048, "reset4": NP, "xt": 4 * ALLC, "rt": 4 * ALLC, "sums": 7 * CK},
+    F8: {"qx": NT, "qw": 512, "qe": 512, "ct": ALLC, "rxn": 192, "rxf": 288, "rc": ALLC, "bkn": 192, "bkf": 288},
+    U8: {"px": NT, "pw": 512, "pe": 512, "cs": ALLC, "rxns": 192, "rxfs": 288, "rs": ALLC, "bkns": 192, "bkfs": 288},
     I32: {"pi": 2, "pci": 8},
-    U16: {"offw": 64, "off4": 144, "off16": 36, "offc": 216},
-    F32: {"pc": 8, "offwf": 64, "k1": NT, "k2": NT, "im4": 32, "im16": 32, "k4s": CK, "k16s": CK, "k4": NP, "cut1": 12, "cut2": 6,
-          "slots": 576, "mask4": 32, "mask16": 32, "rr4": CK, "rr16": CK, "mcol": 4, "v2": 6, "offf": 36,
-          "cl": NP + NT, "cm": NP + NT, "cq": NP + NT, "aa": 8 + 4 * 576, "yy": 4 * NT},
+    U16: {"offw": 32, "off4": 144, "off16": 36, "offc": 216, "offz": 6},
+    F32: {"pc": 8, "pd": 12, "offwf": 32, "im4": 32, "slots": 576, "mask4": 32, "mask16": 32, "rr4": CK, "mcol": 4, "s6": 12, "offf": 36,
+          "first": 12, "zc": CK, "akm": 44, "cl": NP + NT, "cm": NP + NT, "cq": NP + NT, "aa": 8 + 4 * 576, "yy": 4 * NT},
 }
 for R in ROUNDS:
-    k, n, ns = R["k"], NT // R["W"], R["NS"]
+    k, n, ns = R["k"], HALF // R["W"], R["NS"]
     R["n"] = n
-    SHAPES[BF].update({"cmp" + k: n * NT, "sums" + k: (n - ns) * HALF, "eqw" + k: NT, "corr" + k: NT})
+    SHAPES[BF].update({"wga" + k: 4 * R["G"], "cmp" + k: n * HALF, "reset" + k: HALF, "eqw" + k: HALF, "corr" + k: HALF})
+    SHAPES[F8].update({"qg" + k: R["G"]})
+    SHAPES[U8].update({"pg" + k: R["G"]})
     SHAPES[U16].update({"offr" + k: n})
-    SHAPES[F32].update({"m3" + k: NT, "rr" + k: NT, "md" + k: NT, "sc" + k: NT, "acc" + k: ns, "accb" + k: ns, "accc" + k: ns, "rk" + k: ns, "rkb" + k: ns,
-                        "first" + k: n, "tok" + k: 16 * n, "tokf" + k: 16 * n, "win" + k: NT, "t1" + k: CK, "wa" + k: CK, "t2" + k: CK, "s4" + k: CK,
-                        "wb" + k: CK, "t3" + k: CK, "s16" + k: CK})
+    SHAPES[F32].update({"k" + k: HALF, "m3" + k: HALF, "rr" + k: HALF, "md" + k: HALF, "sc" + k: HALF, "zs" + k: HALF, "akk" + k: 4 * ns, "akq" + k: 4 * ns,
+                        "tok" + k: 16 * n, "tokf" + k: 16 * n, "win" + k: 2 * WIN, "t1" + k: 2 * CK, "pick" + k: 12,
+                        "wa" + k: CK, "t2" + k: CK, "s4" + k: CK, "wb" + k: CK, "t3" + k: CK, "s16" + k: CK})
 SCRATCH = {name: ("sbuf", [128, n], kind) for kind in SHAPES for name, n in SHAPES[kind].items()}
 SCRATCH["pp"] = ("psum", [128, 4096], F32)
-SEMAPHORES = ["sv", "sa", "sten", "sp", "ldx", "ldx2", "ldg", "ldw", "sty", "sty2", "loc", "dn", "df", "rn", "rf"]
+SEMAPHORES = ["sv", "sa", "sten", "ldx", "ldx2", "ldg", "ldw", "sty", "sty2", "loc", "dn", "df", "rn", "rf"] + ["sp%d" % i for i in range(12)]
 
 
 def rank_program(g, core, T, topo):
@@ -53,8 +56,8 @@ def rank_program(g, core, T, topo):
     idx = {e: i for i, e in enumerate(order)}
     pos = {e: CK * idx[e] for e in order}
 
-    Q = {"v": (g.vector, "sv"), "a": (g.scalar, "sa"), "t": (g.tensor, "sten"), "p": (g, "sp"), "s": (g.sync, None)}
-    count = {"sv": 0, "sa": 0, "sten": 0, "sp": 0}
+    Q = {"v": (g.vector, "sv"), "a": (g.scalar, "sa"), "t": (g.tensor, "sten"), "p": (g, None), "s": (g.sync, None)}
+    count = {"sv": 0, "sa": 0, "sten": 0}
     seen = {}
 
     def need(q, deps):
@@ -65,13 +68,15 @@ def rank_program(g, core, T, topo):
 
     def done(q, ins):
         s = Q[q][1]
+        if q == "p":
+            s = "sp%d" % sum(1 for c in count if c.startswith("sp"))
+            count[s] = 0
         ins.then_inc(T.sem[s], 1)
         count[s] += 1
-        if q == "p":
-            need("p", [(s, count[s])])
         return (s, count[s])
 
     V, A, TE = g.vector, g.scalar, g.tensor
+    R1, R2 = ROUNDS
 
     g.sync.dma_start(T.xsb[:, 0:4 * HALF], T.x[:, 0:4 * HALF]).then_inc(T.sem["ldx"], 16)
     g.scalar.dma_start(T.wgs[:], T.wg[:, 0:32]).then_inc(T.sem["ldg"], 16)
@@ -79,255 +84,293 @@ def rank_program(g, core, T, topo):
     g.sync.dma_start(T.w1s[:], T.w1[:]).then_inc(T.sem["ldw"], 16)
     LDX, LDX2, LDG, LDW = ("ldx", 16), ("ldx2", 16), ("ldg", 16), ("ldw", 16)
 
-    def iota(name, pattern, base=0, cm=0):
-        if name == "pi":
-            return done("p", g.iota(T.pi[:], pattern, base, cm))
-        return done("p", g.iota(T[name][:], pattern, base, cm, allow_small_or_imprecise_dtypes=True))
+    def iota(name, pattern, base=0):
+        return done("p", g.iota(T[name][:], pattern, base, 0, allow_small_or_imprecise_dtypes=True))
 
-    c_pi = iota("pi", [[0, 2]], 0, 1)
-    c_k = {"1": iota("k1", [[0, 12], [1, 32]])}
+    c_pi = done("p", g.iota(T.pi[:], [[0, 2]], 0, 1))
+    c_k = {"1": iota("k1", [[0, 12], [1, 16]])}
+    c_tokf = {"1": iota("tokf1", [[1, HALF]])}
+    c_k["2"] = iota("k2", [[0, 6], [1, 32]])
     c_im4 = iota("im4", [[0, 2], [1, 4], [0, 4]])
-    c_im16 = iota("im16", [[0, 2], [1, 16]])
-    c_k4s = iota("k4s", [[0, 24], [1, 4]])
-    c_k16s = iota("k16s", [[0, 6], [1, 16]])
-    c_cut = {"1": iota("cut1", [[32, 12]], 32)}
-    c_k["2"] = iota("k2", [[0, 6], [1, 64]])
-    c_tokf = {"1": iota("tokf1", [[32, 12], [1, 16]]), "2": iota("tokf2", [[64, 6], [1, 16]])}
-    c_cut["2"] = iota("cut2", [[64, 6]], 64)
-    c_slots = iota("slots", [[1, 576]], 1)
-    c_k4 = iota("k4", [[0, NP // 4], [1, 4]])
+    c_tokf["2"] = iota("tokf2", [[32, 6], [1, 16]])
 
+    c_zero = {"1": done("v", V.memset(T.wga1[:], 0.0))}
     for i in range(4):
-        done("v", V.memset(T.offwf[:, 8 * i:8 * i + 8], float(4 * order[i])))
-    for i in (4, 5):
-        c_offwf = done("v", V.memset(T.offwf[:, 16 * i - 32:16 * i - 16], float(4 * order[i])))
-    c_ones = done("v", V.memset(T.ones[:], 1.0))
-    P3, P15, W31, W63, H16, H48, PM = range(7)
+        done("v", V.memset(T.offwf[:, 4 * i:4 * i + 4], float(4 * order[i])))
+    P3, P15, P31, P16, PM, H1, H2 = range(7)
     need("v", [c_pi])
-    for k, m in enumerate((3, 15, 31, 63, 16, 48)):
+    for k, m in enumerate((3, 15, 31, 16)):
         done("v", V.tensor_scalar(T.pci[:, k:k + 1], T.pi[:, 0:1], m, None, OP.bitwise_and))
-    done("v", V.tensor_scalar(T.pci[:, PM:PM + 1], T.pi[:, 0:1], 15, 2, OP.bitwise_and, OP.logical_shift_right))
-    d = done("v", V.tensor_scalar(T.pci[:, 7:8], T.pi[:, 0:1], 0, None, OP.bitwise_and))
-    c_win = [done("v", V.memset(T[w][:, 0:CK], 0.0)) for w in ("win1", "win2")][-1]
+    for k, m, s in ((PM, 15, 2), (H1, 16, 4), (H2, 64, 6)):
+        d = done("v", V.tensor_scalar(T.pci[:, k:k + 1], T.pi[:, 0:1], m, s, OP.bitwise_and, OP.logical_shift_right))
+    for i in (4, 5):
+        c_offwf = done("v", V.memset(T.offwf[:, 8 * i - 16:8 * i - 8], float(4 * order[i])))
     need("v", [d])
-    c_pc = done("v", V.tensor_copy(T.pc[:], T.pci[:]))
-    c_v2 = done("v", V.memset(T.v2[:], 0.0))
+    c_pc = done("v", V.tensor_copy(T.pc[:, 0:7], T.pci[:, 0:7]))
+    for j, c in enumerate((0.0, 1.0)):
+        done("v", V.memset(T.akm[:, j:44:4], c))
 
     def pcol(k, lo=0, hi=128):
         return T.pc[lo:hi, k:k + 1]
 
     need("v", [c_offwf, c_pc])
     c_offw = done("v", V.tensor_scalar(T.offw[:], T.offwf[:], pcol(P3), None, OP.add))
-    c_m3 = {}
+    c_akm = done("v", V.memset(T.akm[:, 2:44:4], -1.0))
+    done("v", V.memset(T.wga2[:, 0:256], 0.0))
+    c_zero["2"] = done("v", V.memset(T.wga2[:, 512:768], 0.0))
 
-    def m3(k, col):
-        need("v", [c_k[k]])
-        c_m3[k] = done("v", V.tensor_scalar(T["m3" + k][:], T["k" + k][:], pcol(col), -BIG, OP.not_equal, OP.mult))
+    SGN, KC, TOK, MB, CV, TOK2 = 0, 2, 4, 6, 8, 9
+    need("a", [c_pc])
+    done("a", A.activation(T.pd[:, MB:MB + 2], T.pc[:, P15:P15 + 2], AF.Copy, scale=-STEP))
+    done("a", A.activation(T.pd[:, SGN:SGN + 2], T.pc[:, H1:H1 + 2], AF.Copy, bias=1.0, scale=-2.0))
+    done("a", A.activation(T.pd[:, KC:KC + 2], T.pc[:, H1:H1 + 2], AF.Copy, bias=CK + 1.0, scale=CK - 3.0))
+    done("a", A.activation(T.pd[:, TOK:TOK + 1], pcol(H1), AF.Copy, scale=float(HALF)))
+    done("a", A.activation(T.pd[:, TOK + 1:TOK + 2], pcol(H2), AF.Identity, bias=pcol(P16), scale=float(HALF)))
+    c_pd = done("a", A.activation(T.pd[:, CV:CV + 1], pcol(H1), AF.Copy, bias=float(HALF), scale=-(CK + 1.0)))
 
-    m3("1", W31)
-    c_xpad = done("v", V.memset(T.xt[:, 4 * (OWN0 + CK):4 * ALLC], 0.0))
-    c_aa = done("v", V.memset(T.aa[:, 0:4], 0.0))
+    def dcol(j, R):
+        j += ROUNDS.index(R)
+        return T.pd[:, j:j + 1]
 
-    c_reset, c_rr, c_tok, a_wga = {}, {}, {}, {}
+    def gate(q, R, col, lo, n):
+        k = R["k"]
+        out, win = T["wga" + k][:, 4 * col:4 * col + 16 * n], T.wgs[:, 0:32].indirect(T.offw[:, lo:lo + n])
+        need(q, [c_offw, LDG, c_zero[k]])
+        return done(q, A.activation(out, win, AF.Copy) if q == "a" else V.tensor_copy(out, win))
 
-    def reset(k):
-        need("a", [c_k[k]])
+    c_reset, c_rr, c_m3, c_tok, c_kc = {}, {}, {}, {}, {}
+
+    def windows(R):
+        k = R["k"]
+        need("a", [c_k[k], c_pd])
         c_reset[k] = done("a", A.activation(T["reset" + k][:], T["k" + k][:], AF.Sign))
-
-    def rr(k):
+        c_m3[k] = done("a", A.activation(T["m3" + k][:], T["k" + k][:], AF.Abs, bias=dcol(MB, R), scale=STEP))
         need("a", [c_reset[k]])
         c_rr[k] = done("a", A.activation(T["rr" + k][:], T["reset" + k][:], AF.Copy, bias=-BIG, scale=BIG))
 
-    def tokens(k, col):
-        need("a", [c_tokf[k], c_pc])
-        c_tok[k] = done("a", A.activation(T["tok" + k][:], T["tokf" + k][:], AF.Identity, bias=pcol(col)))
+    def tokens(R):
+        k, W, ns = R["k"], R["W"], R["NS"]
+        o = 0 if R is R1 else 4 * R1["NS"]
+        need("a", [c_tokf[k], c_tokf["1"], c_pd])
+        c_tok[k] = done("a", A.activation(T["tok" + k][:], T["tokf" + k][:], AF.Identity, bias=dcol(TOK, R)))
+        ends = T.tokf1[:, W - 1:W * ns:W]
+        done("a", A.activation(T["akk" + k][:, 3:4 * ns:4], ends, AF.Identity, bias=dcol(KC, R), scale=dcol(SGN, R)))
+        c_kc[k] = done("a", A.activation(T.akm[:, o + 3:o + 4 * ns:4], ends, AF.Identity, bias=dcol(SGN, R), scale=0.0))
 
-    def gates(k, lo):
-        need("a", [c_offw, LDG])
-        a_wga[k] = done("a", A.activation(T["wga" + k][:], T.wgs[:, 0:32].indirect(T.offw[:, lo:lo + 32]), AF.Copy))
+    a_g1 = [gate("a", R1, 16 + 32 * i, 4 * i, 4) for i in (2, 3)][-1]
+    windows(R1)
+    a_g2 = [gate("a", R2, 64 + 32 * i, 16 + 8 * i, 8) for i in (0, 1)][-1]
+    tokens(R1)
+    windows(R2)
 
-    reset("1")
-    gates("1", 0)
-    rr("1")
-    gates("2", 32)
-    tokens("1", H16)
-    reset("2")
-    tokens("2", H48)
-
-    need("p", [c_ones])
-
-    def one_tile(b):
-        return done("p", g.affine_select(T.et[:, 512 * b:512 * b + 512], T.ones[:], [[-1, 512]], OP.is_equal, 0.0, b, 4))
-
-    c_et = [one_tile(0), one_tile(1)]
-
-    need("v", [a_wga["1"]])
-    done("v", V.quantize_mx(T.qg1[:], T.pg1[:], T.wga1[:]))
+    v_g1 = [gate("v", R1, 16 + 32 * i, 4 * i, 4) for i in (0, 1)][-1]
+    c_ones = done("v", V.memset(T.ones[:], 1.0))
+    need("v", [v_g1, a_g1])
+    v_qg1 = done("v", V.quantize_mx(T.qg1[:], T.pg1[:], T.wga1[:]))
     need("v", [LDX])
-    done("v", V.quantize_mx(T.qx[:, 0:HALF], T.px[:, 0:HALF], T.xsb[:, 0:4 * HALF]))
-    need("v", [c_im4, c_im16, c_k4s, c_k16s])
-    done("v", V.tensor_scalar(T.mask4[:], T.im4[:], pcol(P3), -BIG, OP.not_equal, OP.mult))
-    done("v", V.tensor_scalar(T.mask16[:], T.im16[:], pcol(P15), -BIG, OP.not_equal, OP.mult))
-    done("v", V.tensor_scalar(T.mcol[:], T.k4s[:, 0:4], pcol(PM), 4.0, OP.is_equal, OP.mult))
-    done("v", V.tensor_scalar(T.rr4[:], T.k4s[:], 0.0, -BIG, OP.is_equal, OP.mult))
-    c_lists = done("v", V.tensor_scalar(T.rr16[:], T.k16s[:], 0.0, -BIG, OP.is_equal, OP.mult))
+    v_qx0 = done("v", V.quantize_mx(T.qx[:, 0:HALF], T.px[:, 0:HALF], T.xsb[:, 0:4 * HALF]))
+    c_reset4 = done("v", V.memset(T.reset4[:], 1.0))
     need("v", [LDX2])
-    v_qx = done("v", V.quantize_mx(T.qx[:, HALF:NT], T.px[:, HALF:NT], T.xsb[:, 4 * HALF:4 * NT]))
-    m3("2", W63)
-    need("v", [a_wga["2"]])
+    v_qx1 = done("v", V.quantize_mx(T.qx[:, HALF:NT], T.px[:, HALF:NT], T.xsb[:, 4 * HALF:4 * NT]))
+    need("v", [a_g2])
     v_qg2 = done("v", V.quantize_mx(T.qg2[:], T.pg2[:], T.wga2[:]))
+    need("v", [c_im4, c_k["1"], c_reset4])
+    c_reset4 = done("v", V.memset(T.reset4[:, 0:NP:4], 0.0))
+    done("v", V.tensor_scalar(T.mask4[:], T.im4[:], pcol(P3), -BIG, OP.not_equal, OP.mult))
     t_z = {}
-    for R, dep in zip(ROUNDS, (v_qx, v_qg2)):
-        k = R["k"]
-        need("t", [dep])
-        t_z[k] = [done("t", TE.matmul_mx(T.pp[:, 512 * b:512 * b + NT], T["qg" + k][:], T["pg" + k][:], T.qx[:], T.px[:], True, True)) for b in (R["bank"], R["bank"] + 1)]
 
-    def z(R, other, lo=0, hi=NT):
+    def z(R, other, lo=0, hi=HALF):
         o = 512 * (R["bank"] + other)
         return T.pp[:, o + lo:o + hi]
 
-    v_sc = {}
+    for R, deps in ((R1, (v_qx0, v_qx1)), (R2, (v_qg2, v_qg2))):
+        k = R["k"]
+        for h in (0, 1):
+            need("t", [deps[h]])
+            s, c = slice(R["views"][h], R["views"][h] + 128), slice(HALF * h, HALF * h + HALF)
+            t_z[k] = [done("t", TE.matmul_mx(z(R, b), T["qg" + k][:, s], T["pg" + k][:, s], T.qx[:, c], T.px[:, c], h == 0, h == 1)) for b in (0, 1)]
+
+    need("p", [c_ones])
+    c_et = [done("p", g.affine_select(T.et[:, 512 * b:512 * b + 512], T.ones[:], [[-1, 512]], OP.is_equal, 0.0, b, 4)) for b in range(4)]
+
+    v_md, v_sc = {}, {}
 
     def own_mask(R, lo, hi):
         k = R["k"]
         need("v", [t_z[k][0], c_m3[k]])
-        return done("v", V.tensor_tensor(T["md" + k][:, lo:hi], z(R, 0, lo, hi), T["m3" + k][:, lo:hi], OP.add))
+        v_md[k, lo] = done("v", V.tensor_tensor(T["md" + k][:, lo:hi], z(R, 0, lo, hi), T["m3" + k][:, lo:hi], OP.subtract))
 
-    def own_scan(R, lo, hi, dep):
+    def own_scan(R, lo, hi):
         k = R["k"]
-        need("v", [dep, c_rr[k]])
-        v_sc[k + str(lo)] = done("v", V.tensor_tensor_scan(T["sc" + k][:, lo:hi], T["rr" + k][:, lo:hi], T["md" + k][:, lo:hi], 0.0, OP.add, OP.max))
+        need("v", [v_md[k, lo], c_rr[k]])
+        v_sc[k, lo] = done("v", V.tensor_tensor_scan(T["sc" + k][:, lo:hi], T["rr" + k][:, lo:hi], T["md" + k][:, lo:hi], 0.0, OP.add, OP.max))
 
-    a_acc = {}
+    v_tie = {}
+
+    def equal(R, lo, hi):
+        k = R["k"]
+        need("v", [d for (j, _), d in v_sc.items() if j == k])
+        v_tie[k] = done("v", V.tensor_tensor(T["eqw" + k][:, lo:hi], z(R, 0, lo, hi), T["sc" + k][:, lo:hi], OP.is_equal))
+
+    def ties(R):
+        k = R["k"]
+        need("v", [v_tie[k], c_reset[k]])
+        v_tie[k] = done("v", V.tensor_tensor_scan(T["corr" + k][:], T["reset" + k][:], T["eqw" + k][:], 0.0, OP.mult, OP.add))
+
+    def ties_out(R):
+        k, W, ns = R["k"], R["W"], R["NS"]
+        need("v", [v_tie[k]])
+        v_tie[k] = done("v", V.tensor_copy(T["akk" + k][:, 0:4 * ns:4], T["corr" + k][:, W - 1:W * ns:W]))
+
+    a_acc, a_zs = {}, {}
+
+    def scores_out(R):
+        k = R["k"]
+        need("a", [t_z[k][1]])
+        a_zs[k] = done("a", A.activation(T["zs" + k][:], z(R, 1), AF.Copy))
 
     def scalar_ranks(R):
         k, W, ns = R["k"], R["W"], R["NS"]
-        need("a", [t_z[k][1], v_sc[k + "0"]])
-        cmp, signs = T["cmp" + k], []
+        need("a", [t_z[k][1], v_sc[k, 0]])
+        cmp, akk, signs = T["cmp" + k], T["akk" + k], []
         for q in range(ns + 1):
             if q < ns:
-                signs.append(done("a", A.activation(cmp[:, NT * q:NT * q + NT], z(R, 1), AF.Sign, bias=T["sc" + k][:, W * q + W - 1:W * q + W], scale=-1.0)))
+                signs.append(done("a", A.activation(cmp[:, HALF * q:HALF * q + HALF], z(R, 1), AF.Sign, bias=T["sc" + k][:, W * q + W - 1:W * q + W], scale=-1.0)))
             if q:
-                j, c = q - 1, NT * (q - 1)
-                lower, higher = cmp[:, c:c + W * q], cmp[:, c + W * q:c + NT]
+                j, c = q - 1, HALF * (q - 1)
+                lower = cmp[:, c:c + W * q]
                 need("a", [signs[j]])
-                done("a", A.activation(lower, lower, AF.Relu, accum_out=T["acc" + k][:, j:j + 1]))
-                a_acc[k] = done("a", A.activation(higher, higher, AF.Relu, scale=-1.0, accum_out=T["accb" + k][:, j:j + 1]))
+                a_acc[k] = done("a", A.activation(lower, lower, AF.Relu, accum_out=akk[:, 4 * j + 1:4 * j + 2]))
+                if W * q < HALF:
+                    higher = cmp[:, c + W * q:c + HALF]
+                    a_acc[k] = done("a", A.activation(higher, higher, AF.Relu, scale=-1.0, accum_out=akk[:, 4 * j + 2:4 * j + 3]))
 
-    v_eq = {}
+    def scalar_places(R, fill):
+        k, ns = R["k"], R["NS"]
+        o = 0 if R is R1 else 4 * R1["NS"]
+        need("v", [a_acc[k], v_tie[k], c_kc[k], c_akm])
+        d = done("v", V.tensor_tensor_scan(T["akq" + k][:], T.akm[:, o:o + 4 * ns], T["akk" + k][:], 0.0, OP.mult, OP.add))
+        fill()
+        need("v", [d])
+        return done("v", V.tensor_copy(T["offr" + k][:, 0:ns], T["akq" + k][:, 3:4 * ns:4]))
 
-    def vector_ranks(R, fill):
+    def vector_ranks(R, steps):
         k, W, ns, n = R["k"], R["W"], R["NS"], R["n"]
-        cmp, sc, corr, first, offr = T["cmp" + k], T["sc" + k], T["corr" + k], T["first" + k], T["offr" + k]
-        s0 = W * ns
-
-        def total(q, deps):
-            o, c = HALF * (q - ns), NT * q
-            need("v", deps)
-            return done("v", V.tensor_tensor_scan(T["sums" + k][:, o:o + HALF], cmp[:, c:c + HALF], cmp[:, c + HALF:c + NT], first[:, q:q + 1], OP.add, OP.add))
-
-        need("v", [v_sc[k + str(s0)]])
-        v_eq[k] = done("v", V.tensor_tensor(T["eqw" + k][:], z(R, 0), sc[:], OP.is_equal))
+        cmp, sc = T["cmp" + k], T["sc" + k]
         late = []
+
+        def total():
+            q, d = late.pop(0)
+            o, c = CK * (q - ns), HALF * q
+            need("v", [d])
+            return done("v", V.tensor_tensor_scan(T.sums[:, o:o + CK], cmp[:, c:c + CK], cmp[:, c + CK:c + HALF], T.first[:, q:q + 1], OP.add, OP.add))
+
+        equal(R, 0, HALF)
         for q in range(ns, n):
             s = sc[:, W * q + W - 1:W * q + W]
-            cut, c = W * q + W, NT * q
+            cut, c = W * q + W, HALF * q
             d = done("v", V.tensor_scalar(cmp[:, c:c + cut], z(R, 0, 0, cut), s, None, OP.is_ge))
-            if cut < NT:
-                d = done("v", V.tensor_scalar(cmp[:, c + cut:c + NT], z(R, 0, cut, NT), s, None, OP.is_gt))
+            if cut < HALF:
+                d = done("v", V.tensor_scalar(cmp[:, c + cut:c + HALF], z(R, 0, cut, HALF), s, None, OP.is_gt))
             late.append((q, d))
             if q == ns:
-                need("v", [v_eq[k], c_reset[k]])
-                v_corr = done("v", V.tensor_tensor_scan(corr[:], T["reset" + k][:], T["eqw" + k][:], 0.0, OP.mult, OP.add))
+                ties(R)
             elif q == ns + 1:
-                need("v", [v_corr, c_cut[k]])
-                v_first = done("v", V.tensor_scalar(first[:], corr[:, W - 1:NT:W], -1.0, -float(HALF), OP.mult, OP.add))
-                v_k = done("v", V.tensor_tensor(T["rkb" + k][:], T["cut" + k][:, 0:ns], corr[:, W - 1:s0:W], OP.subtract))
+                need("v", [v_tie[k]])
+                done("v", V.tensor_scalar(T.first[:], T["corr" + k][:, W - 1:HALF:W], -1.0, -float(CK), OP.mult, OP.add))
+                ties_out(R)
             else:
-                j, d = late.pop(0)
-                total(j, [d, v_first])
-        j, d = late.pop(0)
-        total(j, [d, v_first])
-        need("v", [a_acc[k], v_k])
-        d0 = done("v", V.tensor_tensor(T["accc" + k][:], T["accb" + k][:], T["acc" + k][:], OP.subtract))
-        j, d = late.pop(0)
-        v_sum = total(j, [d])
-        need("v", [d0])
-        d0 = done("v", V.tensor_tensor(T["rk" + k][:], T["accc" + k][:], T["rkb" + k][:], OP.add))
-        need("v", [v_sum])
-        done("v", V.tensor_scalar(offr[:, ns:n], T["sums" + k][:, HALF - 1:HALF * (n - ns):HALF], float(HALF), None, OP.add))
-        need("v", [d0])
-        v_offr = done("v", V.tensor_copy(offr[:, 0:ns], T["rk" + k][:]))
+                if q == ns + 2:
+                    steps[0]()
+                    need("v", [v_tie[k]])
+                elif q == ns + 3:
+                    steps[1]()
+                total()
+        total()
+        v_sum = total()
+
+        def places():
+            need("v", [v_sum, c_pd])
+            done("v", V.tensor_scalar(T["offr" + k][:, ns:n], T.sums[:, CK - 1:CK * (n - ns):CK], dcol(SGN, R), T.pd[:, CV:CV + 1], OP.mult, OP.add))
+        return scalar_places(R, places)
+
+    v_pick, v_t3, v_s16, off = {}, {}, {}, {}
+
+    def under(R, w, mask, u):
+        k, P = R["k"], R["P"]
+        first = T.t11[:, CK + 32 * u:CK + 32 * u + 1] if R is R1 else T.s6[0:P, 3 + u:4 + u]
+        return done("v", V.tensor_scalar(T[w + k][0:P, 32 * u:32 * u + 32], T[mask][0:P, :], first, T["pick" + k][0:P, 6 + u:7 + u], OP.add, OP.subtract))
+
+    def lists(R, v_offr, scores, deps, fill):
+        k, n, P = R["k"], R["n"], R["P"]
+        win, t1, pick, offr = T["win" + k], T["t1" + k], T["pick" + k], T["offr" + k]
         fill()
-        need("v", [v_offr, c_tok[k], c_win])
-        return done("v", V.tensor_copy(T["win" + k][:, 0:NT].indirect(offr[:, 0:n]), T["tok" + k][:]))
-
-    v_t3, v_s16, off = {}, {}, {}
-
-    def lists(R, v_win, fill):
-        k = R["k"]
-        t1 = T["t1" + k]
-        fill()
-        need("v", [v_win, c_lists])
-        d = done("v", V.transpose(t1[:], T["win" + k][:, 0:CK]))
-        fill()
+        need("v", [v_offr, c_tok[k]] + deps)
+        d = done("v", V.tensor_copy(win[:, 0:WIN].indirect(offr[:, 0:n]), scores))
+        e = done("v", V.tensor_copy(win[:, WIN:2 * WIN].indirect(offr[:, 0:n]), T["tok" + k][:]))
         need("v", [d])
-        if k == "1":
-            pair = [(t1[:, 32 * u:32 * u + 1], t1[:, 32 * u + 16:32 * u + 17]) for u in range(3)]
-        else:
-            for b in (0, 64):
-                d = done("v", V.tensor_tensor(T.v2[b:b + 32, :], t1[b:b + 32, 0:CK:16], t1[b + 32:b + 64, 0:CK:16], OP.add))
-            pair = [(T.v2[:, 2 * u:2 * u + 1], T.v2[:, 2 * u + 1:2 * u + 2]) for u in range(3)]
-            fill()
-            need("v", [d, c_v2])
-
-        def under(w, mask, u):
-            return done("v", V.tensor_scalar(T[w + k][:, 32 * u:32 * u + 32], T[mask][:], pair[u][0], pair[u][1], OP.add, OP.add))
-
-        d = [under("wa", "mask4", u) for u in range(3)][-1]
-        under("wb", "mask16", 0)
-        need("v", [d])
-        d = done("v", V.transpose(T["t2" + k][:], T["wa" + k][:]))
-        under("wb", "mask16", 1)
-        need("v", [d])
-        d = done("v", V.tensor_tensor_scan(T["s4" + k][:], T.rr4[:], T["t2" + k][:], 0.0, OP.add, OP.max))
-        e = under("wb", "mask16", 2)
-        need("v", [d])
-
-        def offsets(i, block, blocks):
-            for b in blocks:
-                off[i] = done("v", V.tensor_scalar(T.off4[32 * b:32 * b + 32, 24 * i:24 * i + 24], T["s4" + k][32 * block:32 * block + 32, 3:CK:4], 4.0, pcol(P3, 32 * b, 32 * b + 32), OP.mult, OP.add))
-
-        def upper(lo, hi):
-            need("v", [off[hi - 1]])
-            d = done("v", V.tensor_copy(T.off4[64:128, 24 * lo:24 * hi], T.off4[0:64, 24 * lo:24 * hi]))
-            for i in range(lo, hi):
-                off[i] = d
-
-        if k == "1":
-            offsets(0, 0, range(4))
-            offsets(1, 1, (0, 1))
-            offsets(2, 2, (0, 1))
-            offsets(3, 3, (0, 1))
-        else:
-            offsets(4, 0, (0, 1))
-            offsets(5, 2, (0, 1))
+        d = done("v", V.transpose(t1[:, 0:CK], win[:, CK:2 * CK]))
         need("v", [e])
-        v_t3[k] = done("v", V.transpose(T["t3" + k][:], T["wb" + k][:]))
-        if k == "1":
-            upper(1, 4)
+        e = done("v", V.transpose(t1[:, CK:2 * CK], win[:, WIN + CK:WIN + 2 * CK]))
+        if R is R1:
+            sides = [(t1[:, o:o + CK:32], t1[:, o + 16:o + CK:32]) for o in (0, CK)]
         else:
-            upper(4, 6)
+            fill()
+            need("v", [e])
+            for h in (0, 1):
+                d = e = done("v", V.tensor_tensor(T.s6[0:64, 6 * h:6 * h + 6], t1[64 * h:64 * h + 64, 0:2 * CK:32], t1[64 * h:64 * h + 64, 16:2 * CK:32], OP.add))
+            fill()
+            sides = [(T.s6[0:64, o:o + 3], T.s6[0:64, o + 6:o + 9]) for o in (0, 3)]
+        need("v", [d])
+        done("v", V.tensor_tensor(pick[0:P, 0:3], sides[0][0], sides[0][1], OP.is_lt))
+        need("v", [e])
+        d = done("v", V.tensor_tensor(pick[0:P, 3:6], sides[1][0], sides[1][1], OP.subtract))
+        fill()
+        need("v", [d])
+        v_pick[k] = done("v", V.tensor_tensor(pick[0:P, 6:9], pick[0:P, 0:3], pick[0:P, 3:6], OP.mult))
+        fill()
+        need("v", [v_pick[k]])
+        d = [under(R, "wa", "mask4", u) for u in range(3)][-1]
+        fill()
+        need("v", [d])
+        d = done("v", V.transpose(T["t2" + k][0:P, :], T["wa" + k][0:P, :]))
+        fill()
+        need("v", [d, c_rr4])
+        d = done("v", V.tensor_tensor_scan(T["s4" + k][0:P, :], T.rr4[0:P, :], T["t2" + k][0:P, :], 0.0, OP.add, OP.max))
+        fill()
+        need("v", [d])
 
-    def singles(k):
-        need("v", [v_t3[k]])
-        v_s16[k] = done("v", V.tensor_tensor_scan(T["s16" + k][:], T.rr16[:], T["t3" + k][:], 0.0, OP.add, OP.max))
+    def offsets(i, blocks):
+        k, block = ("1", i) if i < 4 else ("2", i - 4)
+        for b in blocks:
+            off[i] = done("v", V.tensor_scalar(T.off4[32 * b:32 * b + 32, 24 * i:24 * i + 24], T["s4" + k][32 * block:32 * block + 32, 3:CK:4], 4.0, pcol(P3, 32 * b, 32 * b + 32), OP.mult, OP.add))
 
-    def gather(q, e):
-        i = idx[e]
-        out = T.xt[:, 4 * pos[e]:4 * pos[e] + 4 * CK]
-        win = T.xsb[:, 0:4 * NT].indirect(T.off4[:, 24 * i:24 * i + 24])
-        need(q, [off[i], LDX, LDX2])
+    def upper(lo, hi):
+        need("v", [off[hi - 1]])
+        d = done("v", V.tensor_copy(T.off4[64:128, 24 * lo:24 * hi], T.off4[0:64, 24 * lo:24 * hi]))
+        for i in range(lo, hi):
+            off[i] = d
+
+    def single_steps(R):
+        k, P, last = R["k"], R["P"], []
+
+        def spread_out(u):
+            need("v", [v_pick[k], c_lists])
+            last.append(under(R, "wb", "mask16", u))
+
+        def turn():
+            need("v", [last[-1]])
+            last.append(done("v", V.transpose(T["t3" + k][0:P, :], T["wb" + k][0:P, :])))
+
+        def scan():
+            need("v", [last[-1]])
+            v_s16[k] = done("v", V.tensor_tensor_scan(T["s16" + k][0:P, :], T.rr1[0:P, 0:CK], T["t3" + k][0:P, :], 0.0, OP.add, OP.max))
+        return [lambda u=u: spread_out(u) for u in range(3)] + [turn, scan]
+
+    def gather(q, lo, hi):
+        out = T.xt[:, 16 * lo:16 * hi]
+        win = T.xsb[:, 0:4 * NT].indirect(T.off4[:, lo:hi])
+        need(q, [off[i] for i in range(lo // 24, (hi + 23) // 24)] + [LDX, LDX2])
         return done(q, A.activation(out, win, AF.Copy) if q == "a" else V.tensor_copy(out, win))
 
     def pack(lo, hi, deps, src, qc, qs):
@@ -338,16 +381,15 @@ def rank_program(g, core, T, topo):
 
     def lanes(isfar, bits, i):
         if not isfar:
-            return (8 + 4 * i, 12 + 4 * i)
-        return (2 * i, 2 * i + 2) if bits else ((6, 7), (7, 8), (0, 4))[i]
+            return slice(8 + i, 16, 2)
+        return ((slice(0, 4, 2), slice(4, 8, 2), slice(1, 8, 2)) if bits else (slice(1, 4, 2), slice(5, 8, 2), slice(0, 8, 2)))[i]
 
     def arrivals(isfar):
         n = 0
         for r in (far if isfar else near):
             i = (far_of(r) if isfar else near_of(r)).index(me)
             for bits in (True, False):
-                lo, hi = lanes(isfar, bits, i)
-                n += hi - lo
+                n += len(topo.engines(cores[r], core)[lanes(isfar, bits, i)])
         return n
 
     def send(isfar, dep, codes, planes, dcodes, dplanes, rsem):
@@ -355,8 +397,7 @@ def rank_program(g, core, T, topo):
         for bits, sname, dname in ((True, codes, dcodes), (False, planes, dplanes)):
             tr = []
             for i, r in enumerate(far if isfar else near):
-                lo, hi = lanes(isfar, bits, i)
-                es = topo.engines(core, cores[r])[lo:hi]
+                es = topo.engines(core, cores[r])[lanes(isfar, bits, i)]
                 there = (far_of(r) if isfar else near_of(r)).index(me) * CK
                 src = T[sname][:, pos[r]:pos[r] + CK]
                 dst = T[dname][:, there:there + CK]
@@ -385,53 +426,77 @@ def rank_program(g, core, T, topo):
                 steps.pop(0)()
         return fill
 
-    R1, R2 = ROUNDS
-    s1, s2 = R1["W"] * R1["NS"], R2["W"] * R2["NS"]
-    d1, d2 = own_mask(R1, 0, s1), own_mask(R1, s1, NT)
-    own_scan(R1, 0, s1, d1)
-    own_scan(R1, s1, NT, d2)
+    s1 = R1["W"] * R1["NS"]
+    own_mask(R1, 0, s1)
+    own_mask(R1, s1, HALF)
+    own_scan(R1, 0, s1)
+    own_scan(R1, s1, HALF)
+    scores_out(R1)
     scalar_ranks(R1)
-    rr("2")
-    need("a", [c_k4])
-    c_r4 = done("a", A.activation(T.reset4[:], T.k4[:], AF.Sign))
-    c_cl = done("a", A.activation(T.cl[:, NP:NP + NT], T.k1[:], AF.Copy, scale=0.0))
-    md2 = []
-    fill = filler([lambda lo=lo: md2.append(own_mask(R2, lo, lo + 96)) for lo in range(0, NT, 96)])
-    v_win = vector_ranks(R1, fill)
-    lists(R1, v_win, fill)
-    for e in far[:2]:
-        a_gf = gather("a", e)
-    fill(4)
-    v_gf = gather("v", far[2])
+    v_offr = vector_ranks(R1, [lambda: own_mask(R2, 0, HALF), lambda: own_scan(R2, 0, HALF)])
+    scores_out(R2)
+    tokens(R2)
+    need("a", [c_reset4])
+    c_rr4 = done("a", A.activation(T.rr4[:], T.reset4[:, 0:CK], AF.Copy, bias=-BIG, scale=BIG))
+    scalar_ranks(R2)
+    later = {}
+
+    def zeros(name, ap):
+        later[name] = done("v", V.memset(ap, 0.0))
+
+    def window_offsets():
+        need("v", [c_tokf["1"]])
+        later["offz"] = done("v", V.tensor_scalar(T.offz[:], T.tokf1[:, 0:HALF:32], pcol(P31), None, OP.add))
+
+    fill = filler([window_offsets, lambda: equal(R2, 0, CK), lambda: equal(R2, CK, HALF), lambda: ties(R2), lambda: ties_out(R2),
+                   lambda: zeros("last", T.akk2[:, 22:23]), lambda: zeros("win", T.win2[:, CK:2 * CK]), lambda: zeros("win", T.win2[:, WIN + CK:WIN + 2 * CK])])
+    lists(R1, v_offr, T.zs1[:], [a_zs["1"]], fill)
+    need("a", [later["offz"], a_zs["2"]])
+    a_zc = done("a", A.activation(T.zc[:], T.zs2[:].indirect(T.offz[:]), AF.Copy))
+    offsets(0, range(4))
+    gather("a", 0, 24)
+    for i in (1, 2, 3):
+        offsets(i, (0, 1))
+    fill()
+    upper(1, 4)
+    fill()
+    a_gf = gather("a", 24, 36)
+    v_gf = gather("v", 36, 72)
+    fill(8)
     v_qfar = pack(FAR0, NEAR0, [a_gf, v_gf], "xt", "ct", "cs")
     send(True, v_qfar, "ct", "cs", "rxf", "rxfs", "df")
-    c_et += [one_tile(2), one_tile(3)]
+    c_slots = iota("slots", [[1, 576]], 1)
 
-    own_scan(R2, 0, s2, md2[-1])
-    own_scan(R2, s2, NT, md2[-1])
-    singles("1")
-    scalar_ranks(R2)
-    a_gn = gather("a", near[0])
+    a_gn = gather("a", 72, 96)
+    c_cl = done("a", A.activation(T.cl[:, NP:NP + HALF], T.k1[:], AF.Copy, scale=0.0))
+    c_cl = done("a", A.activation(T.cl[:, NP + HALF:NP + NT], T.k1[:], AF.Copy, scale=0.0))
+    v_qw = []
+    done("v", V.tensor_scalar(T.mcol[:], T.k1[:, 0:4], pcol(PM), 4.0, OP.is_equal, OP.mult))
+    c_lists = done("v", V.tensor_scalar(T.mask16[:], T.k1[:, 0:32], pcol(P15), -BIG, OP.not_equal, OP.mult))
+    one = single_steps(R1)
+    fill = filler([lambda: v_qw.append(qweight(0))] + one[0:3] + [lambda: v_qw.append(qweight(1)), one[3], lambda: v_qw.append(qweight(2)), one[4],
+                                                                  lambda: v_qw.append(qweight(3)), lambda: zeros("pad", T.xt[:, 4 * (OWN0 + CK):4 * ALLC])])
+    need("v", [later["last"]])
+    v_offr = scalar_places(R2, fill)
+    lists(R2, v_offr, T.zc[:], [a_zc, later["win"]], fill)
+    offsets(4, (0, 1))
+    offsets(5, (0, 1))
+    fill()
+    upper(4, 6)
+    fill()
+    a_gn = gather("a", 96, 108)
+    v_gn = gather("v", 108, 120)
+    a_go = gather("a", 120, 144)
+    fill(10)
+    v_qnear = pack(NEAR0, OWN0, [a_gn, v_gn], "xt", "ct", "cs")
+    send(False, v_qnear, "ct", "cs", "rxn", "rxns", "dn")
 
     def spread(i):
-        k, block = ("1", i) if i < 4 else ("2", 2 * (i - 4))
+        k, block = ("1", i) if i < 4 else ("2", i - 4)
         need("a", [v_s16[k]])
         for b in (0, 1):
             d = done("a", A.activation(T.offf[32 * b:32 * b + 32, 6 * i:6 * i + 6], T["s16" + k][32 * block:32 * block + 32, 15:CK:16], AF.Copy))
         return d
-
-    for i in range(4):
-        spread(i)
-    v_qw = []
-    fill = filler([lambda i=i: v_qw.append(qweight(i)) for i in range(4)])
-    fill()
-    v_win = vector_ranks(R2, fill)
-    lists(R2, v_win, fill)
-    v_gn = gather("v", near[1])
-    fill(4)
-    singles("2")
-    v_qnear = pack(NEAR0, OWN0, [a_gn, v_gn], "xt", "ct", "cs")
-    send(False, v_qnear, "ct", "cs", "rxn", "rxns", "dn")
 
     def products(stat, plane, codes, planes, lo, hi, bank, deps):
         need("t", deps)
@@ -442,11 +507,12 @@ def rank_program(g, core, T, topo):
             r.append(done("t", TE.matmul_mx(T.pp[:, o:o + hi - lo], T[stat][:, c], T[plane][:, c], T[codes][:, lo:hi], T[planes][:, lo:hi], True, True)))
         return r
 
-    def relus(lo, hi, bank, deps):
-        for i in range(4):
-            need("a", [deps[i]])
+    def relus(q, which, lo, hi, bank, deps):
+        for i in which:
+            need(q, [deps[i]])
             o = 512 * (bank + i)
-            d = done("a", A.activation(T.rt[:, 4 * lo + i:4 * hi:4], T.pp[:, o:o + hi - lo], AF.Relu, scale=0.05))
+            out, src = T.rt[:, 4 * lo + i:4 * hi:4], T.pp[:, o:o + hi - lo]
+            d = done(q, A.activation(out, src, AF.Relu, scale=0.05) if q == "a" else V.tensor_scalar(out, src, 0.0, 0.05, OP.max, OP.mult))
         return d
 
     def slot(e):
@@ -479,69 +545,85 @@ def rank_program(g, core, T, topo):
             tk[lo] = done("a", A.activation(T.cm[:, lo + m:hi:4], T.cl[:, lo + m:hi:4], AF.Copy, scale=T.mcol[:, m:m + 1]))
 
     def wrap(lo, hi):
-        need("v", [tk[lo], c_r4])
+        need("v", [tk[lo], c_reset4])
         d = done("v", V.tensor_tensor_scan(T.cq[:, lo:hi], T.reset4[:, 0:hi - lo], T.cm[:, lo:hi], 0.0, OP.mult, OP.add))
         need("v", [d])
         return done("v", V.tensor_scalar(T.offc[:, lo // 4:hi // 4], T.cq[:, lo + 3:hi:4], pcol(P3), None, OP.add))
 
-    p_far = products("qw", "pw", "rxf", "rxfs", 0, 288, 4, [DF, v_qw[-1]])
-    a_far = relus(FAR0, NEAR0, 4, p_far)
-    spread(4)
-    d = spread(5)
+    two = single_steps(R2)
+    for step in two[0:4]:
+        step()
+    v_qown = pack(OWN0, ALLC, [a_go, later["pad"]], "xt", "ct", "cs")
+    two[4]()
+    for i in range(6):
+        d = spread(i)
     need("a", [d])
     a_offf = done("a", A.activation(T.offf[64:128, :], T.offf[0:64, :], AF.Copy))
-    a_go = gather("a", me)
-    v_rfar = pack(FAR0, NEAR0, [a_far], "rt", "rc", "rs")
-    send(True, v_rfar, "rc", "rs", "bkf", "bkfs", "rf")
-
+    p_own = products("qw", "pw", "ct", "cs", OWN0, ALLC, 0, [v_qown, v_qw[-1], a_acc["2"], v_tie["2"]])
+    a_own = relus("a", range(4), OWN0, ALLC, 0, p_own)
+    qunpack(0)
+    qunpack(1)
     need("v", [a_offf])
     v_o16 = done("v", V.tensor_copy(T.off16[:], T.offf[:]))
-    qunpack(0)
+    qunpack(2)
     need("v", [v_o16, c_cl, c_slots])
     tab(0)
-    v_qown = pack(OWN0, ALLC, [a_go, c_xpad], "xt", "ct", "cs")
     tab(1)
-    p_own = products("qw", "pw", "ct", "cs", OWN0, ALLC, 0, [v_qown, v_eq["2"], a_acc["2"], v_win])
-    a_own = relus(OWN0, ALLC, 0, p_own)
-    tab(2)
-    tab(3)
-    qunpack(1)
     v_rown = pack(OWN0, ALLC, [a_own], "rt", "rc", "rs")
-    tab(4)
-    p_near = products("qw", "pw", "rxn", "rxns", 0, 192, 4, [DN, a_far])
-    a_near = relus(NEAR0, OWN0, 4, p_near)
-    qunpack(2)
+    tab(2)
+    p_far = products("qw", "pw", "rxf", "rxfs", 0, 288, 4, [DF])
+    a_far = relus("a", (1, 3), FAR0, NEAR0, 4, p_far)
+    v_far = relus("v", (0, 2), FAR0, NEAR0, 4, p_far)
     v_qe = qunpack(3)
-    v_rnear = pack(NEAR0, OWN0, [a_near], "rt", "rc", "rs")
+    v_rfar = pack(FAR0, NEAR0, [a_far, v_far], "rt", "rc", "rs")
+    send(True, v_rfar, "rc", "rs", "bkf", "bkfs", "rf")
+    tab(3)
+    tab(4)
+    p_near = products("qw", "pw", "rxn", "rxns", 0, 192, 0, [DN, a_own])
+    a_near = relus("a", (1, 3), NEAR0, OWN0, 0, p_near)
+    v_near = relus("v", (0, 2), NEAR0, OWN0, 0, p_near)
+    zeros("aa", T.aa[:, 0:4])
+    v_rnear = pack(NEAR0, OWN0, [a_near, v_near], "rt", "rc", "rs")
     send(False, v_rnear, "rc", "rs", "bkn", "bkns", "rn")
     for k in range(5, 2 * N - 1):
         tab(k)
     mask(NP, NP + NT)
 
-    u_own = products("qe", "pe", "rc", "rs", OWN0, ALLC, 0, [v_rown, v_qe, a_own])
-    d_own = [unpack("a", me, CK, 0, 0, b, u_own[b]) for b in range(4)]
+    u_own = products("qe", "pe", "rc", "rs", OWN0, ALLC, 4, [v_rown, v_qe, a_far, v_far])
+    d_own = [unpack("a", me, CK, 4, 0, b, u_own[b]) for b in range(4)]
     v_prev = wrap(0, NP)
     v_last = wrap(NP, NP + NT)
 
-    u_near = products("qe", "pe", "bkn", "bkns", 0, 192, 4, [RN, a_near])
-    d_near = [unpack("a", near[i], CK, 4, CK * i, b, u_near[b]) for b in range(4) for i in range(2)]
-    u_far = products("qe", "pe", "bkf", "bkfs", 0, 288, 0, [RF, d_own[-1]])
-
     def chain(e, deps):
-        need("v", deps + [v_prev, c_aa])
+        need("v", deps + [v_prev, later["aa"]])
         o = 24 * (e - 1)
         s = slice(slot(e), slot(e) + 4 * CK)
         return done("v", V.tensor_tensor(T.aa[:, s], T.aa[:, 0:slot(e)].indirect(T.offc[:, o:o + 24]), T.aa[:, s], OP.add))
 
-    dlast = [d_own[-1], d_near[-1]]
+    def near_back():
+        u = products("qe", "pe", "bkn", "bkns", 0, 192, 0, [RN, a_near, v_near])
+        for i in range(2):
+            got[near[i]] = [unpack("a", near[i], CK, 0, CK * i, b, u[b]) for b in range(4)][-1:]
+
+    def far_back(first):
+        u = products("qe", "pe", "bkf", "bkfs", 0, 288, 4, [RF, d_own[-1]])
+        d1 = [unpack("v", far[0], first * CK, 4, 0, b, u[b]) for b in (0, 1)][-1]
+        d2 = [unpack("a", far[0], first * CK, 4, 0, b, u[b]) for b in (2, 3)][-1]
+        need("a", [d1])
+        for i in range(3):
+            got[far[i]] = [d1, d2] if i < first else [unpack("a", far[i], CK, 4, CK * i, b, u[b]) for b in (2, 3, 0, 1)][-1:]
+
+    got = {me: d_own[-1:]}
     step = None
-    if far[0] != 0:
-        for e in (1, 2):
-            step = chain(e, dlast + [step])
-    d1 = [unpack("v", far[0], 3 * CK, 0, 0, b, u_far[b]) for b in (0, 1)][-1]
-    d2 = [unpack("a", far[0], 3 * CK, 0, 0, b, u_far[b]) for b in (2, 3)][-1]
-    for e in range(1 if far[0] == 0 else 3, N):
-        step = chain(e, dlast + [d1, d2, step])
+    if far[0] == 0:
+        far_back(2)
+        near_back()
+    else:
+        near_back()
+    for e in range(1, N):
+        if e == far[0]:
+            far_back(1)
+        step = chain(e, got[e] + got[0] + [step])
 
     win = T.aa[:, 0:slot(N)]
     for q, quarters in (("v", (0, 1)), ("a", (2, 3))):

@@ -8,7 +8,8 @@ BIG = 1e29
 STEP = 2.0 ** 90
 F8, U8, F32, BF, U16, I32 = "float8_e4m3fn_x4", "uint8", "float32", "bfloat16", "uint16", "int32"
 
-FAR0, NEAR0, OWN0, ALLC = 0, 3 * CK, 5 * CK, 5 * CK + 128
+PAD = 128 - CK
+FAR0, NEAR0, OWN0, LAND0 = 0, 3 * CK, 5 * CK, 5 * CK + 128
 HALF = NT // 2
 WIN = HALF + CK
 NP = CK * (N - 1)
@@ -16,12 +17,12 @@ ROUNDS = ({"k": "1", "W": 16, "NS": 5, "bank": 0, "G": 144, "views": (16, 0), "P
           {"k": "2", "W": 32, "NS": 6, "bank": 2, "G": 192, "views": (64, 0), "P": 64})
 
 SHAPES = {
-    BF: {"xsb": 4 * NT, "wgs": 32, "w1s": 2048, "ones": 512, "et": 2048, "reset4": NP, "xt": 4 * ALLC, "rt": 4 * ALLC, "sums": 7 * CK},
-    F8: {"qx": NT, "qw": 512, "qe": 512, "ct": ALLC, "rxn": 192, "rxf": 288, "rc": ALLC, "bkn": 192, "bkf": 288},
-    U8: {"px": NT, "pw": 512, "pe": 512, "cs": ALLC, "rxns": 192, "rxfs": 288, "rs": ALLC, "bkns": 192, "bkfs": 288},
+    BF: {"xsb": 4 * NT, "wgs": 32, "w1s": 2048, "ones": 512, "et": 2048, "reset4": NP, "xt": 4 * (PAD + N * CK), "rt": 4 * LAND0, "sums": 7 * CK},
+    F8: {"qx": NT, "qw": 512, "qe": 512, "ct": 128 * N, "rxn": 192, "rxf": 288, "rc": LAND0 + NP},
+    U8: {"px": NT, "pw": 512, "pe": 512, "cs": 128 * N, "rxns": 192, "rxfs": 288, "rs": LAND0 + NP},
     I32: {"pi": 2, "pci": 8},
     U16: {"offw": 32, "off4": 144, "off16": 36, "offc": 216, "offz": 6},
-    F32: {"pc": 8, "pd": 12, "offwf": 32, "im4": 32, "slots": 576, "mask4": 32, "mask16": 32, "rr4": CK, "mcol": 4, "s6": 12, "offf": 36,
+    F32: {"pc": 8, "pd": 12, "offwf": 32, "im4": CK, "slots": 576, "mask4": 32, "mk": CK, "rr4": CK, "mcol": 8, "s6": 12,
           "first": 12, "zc": CK, "akm": 44, "cl": NP + NT, "cm": NP + NT, "cq": NP + NT, "aa": 8 + 4 * 576, "yy": 4 * NT},
 }
 for R in ROUNDS:
@@ -33,10 +34,13 @@ for R in ROUNDS:
     SHAPES[U16].update({"offr" + k: n})
     SHAPES[F32].update({"k" + k: HALF, "m3" + k: HALF, "rr" + k: HALF, "md" + k: HALF, "sc" + k: HALF, "zs" + k: HALF, "akk" + k: 4 * ns, "akq" + k: 4 * ns,
                         "tok" + k: 16 * n, "tokf" + k: 16 * n, "win" + k: 2 * WIN, "t1" + k: 2 * CK, "pick" + k: 12,
-                        "wa" + k: CK, "t2" + k: CK, "s4" + k: CK, "wb" + k: CK, "t3" + k: CK, "s16" + k: CK})
+                        "wa" + k: CK, "t2" + k: CK, "s4" + k: CK})
+PLAN = ["satudf.Fng.N.c.o.z.b.O....", "satud.f.Fng.N.c.o.z.b.O...", "satudmg.Nc.fzFo.b.O.......",
+        "satudf.Fg.n.c.o.N.z.b.O...", "gsatud.c.f.Fno.N.z.b.O....", "gsatud.c.z..f.Fno.N.b.O..."]
+BOTH = [(5,), (5,), (5,), (1, 2), (1, 2), (1, 2)]
 SCRATCH = {name: ("sbuf", [128, n], kind) for kind in SHAPES for name, n in SHAPES[kind].items()}
 SCRATCH["pp"] = ("psum", [128, 4096], F32)
-SEMAPHORES = ["sv", "sa", "sten", "ldx", "ldx2", "ldg", "ldw", "sty", "sty2", "loc", "dn", "df", "rn", "rf"] + ["sp%d" % i for i in range(12)]
+SEMAPHORES = ["sv", "sa", "sten", "ldx", "ldx2", "ldg", "ldw", "sty", "sty2", "loc", "dn", "df"] + ["r%d" % e for e in range(N)] + ["sp%d" % i for i in range(12)]
 
 
 def rank_program(g, core, T, topo):
@@ -52,9 +56,8 @@ def rank_program(g, core, T, topo):
         return [k for k in range(N) if k != r and topo.chip(cores[k]) == topo.chip(cores[r])]
 
     far, near = far_of(me), near_of(me)
-    order = far + near + [me]
+    order = far + near + [me] if far[0] == 0 else far[:1] + near + far[1:] + [me]
     idx = {e: i for i, e in enumerate(order)}
-    pos = {e: CK * idx[e] for e in order}
 
     Q = {"v": (g.vector, "sv"), "a": (g.scalar, "sa"), "t": (g.tensor, "sten"), "p": (g, None), "s": (g.sync, None)}
     count = {"sv": 0, "sa": 0, "sten": 0}
@@ -91,7 +94,7 @@ def rank_program(g, core, T, topo):
     c_k = {"1": iota("k1", [[0, 12], [1, 16]])}
     c_tokf = {"1": iota("tokf1", [[1, HALF]])}
     c_k["2"] = iota("k2", [[0, 6], [1, 32]])
-    c_im4 = iota("im4", [[0, 2], [1, 4], [0, 4]])
+    c_im4 = iota("im4", [[0, 6], [1, 4], [0, 4]])
     c_tokf["2"] = iota("tokf2", [[32, 6], [1, 16]])
 
     c_zero = {"1": done("v", V.memset(T.wga1[:], 0.0))}
@@ -170,13 +173,14 @@ def rank_program(g, core, T, topo):
     need("v", [LDX])
     v_qx0 = done("v", V.quantize_mx(T.qx[:, 0:HALF], T.px[:, 0:HALF], T.xsb[:, 0:4 * HALF]))
     c_reset4 = done("v", V.memset(T.reset4[:], 1.0))
+    c_win = [done("v", V.memset(T.win2[:, o + CK:o + 2 * CK], 0.0)) for o in (0, WIN)][-1]
     need("v", [LDX2])
     v_qx1 = done("v", V.quantize_mx(T.qx[:, HALF:NT], T.px[:, HALF:NT], T.xsb[:, 4 * HALF:4 * NT]))
     need("v", [a_g2])
     v_qg2 = done("v", V.quantize_mx(T.qg2[:], T.pg2[:], T.wga2[:]))
     need("v", [c_im4, c_k["1"], c_reset4])
     c_reset4 = done("v", V.memset(T.reset4[:, 0:NP:4], 0.0))
-    done("v", V.tensor_scalar(T.mask4[:], T.im4[:], pcol(P3), -BIG, OP.not_equal, OP.mult))
+    done("v", V.tensor_scalar(T.mask4[:], T.im4[:, 0:32], pcol(P3), -BIG, OP.not_equal, OP.mult))
     t_z = {}
 
     def z(R, other, lo=0, hi=HALF):
@@ -192,6 +196,7 @@ def rank_program(g, core, T, topo):
 
     need("p", [c_ones])
     c_et = [done("p", g.affine_select(T.et[:, 512 * b:512 * b + 512], T.ones[:], [[-1, 512]], OP.is_equal, 0.0, b, 4)) for b in range(4)]
+    c_slots = iota("slots", [[16, 36], [1, 4], [4, 4]], 1)
 
     v_md, v_sc = {}, {}
 
@@ -306,31 +311,36 @@ def rank_program(g, core, T, topo):
         win, t1, pick, offr = T["win" + k], T["t1" + k], T["pick" + k], T["offr" + k]
         fill()
         need("v", [v_offr, c_tok[k]] + deps)
-        d = done("v", V.tensor_copy(win[:, 0:WIN].indirect(offr[:, 0:n]), scores))
         e = done("v", V.tensor_copy(win[:, WIN:2 * WIN].indirect(offr[:, 0:n]), T["tok" + k][:]))
-        need("v", [d])
-        d = done("v", V.transpose(t1[:, 0:CK], win[:, CK:2 * CK]))
+        if R is R2:
+            fill()
+        d = done("v", V.tensor_copy(win[:, 0:WIN].indirect(offr[:, 0:n]), scores))
         need("v", [e])
         e = done("v", V.transpose(t1[:, CK:2 * CK], win[:, WIN + CK:WIN + 2 * CK]))
+        need("v", [d])
+        d = done("v", V.transpose(t1[:, 0:CK], win[:, CK:2 * CK]))
         if R is R1:
-            sides = [(t1[:, o:o + CK:32], t1[:, o + 16:o + CK:32]) for o in (0, CK)]
+            src, step, other = t1, 32, 16
         else:
             fill()
-            need("v", [e])
+            need("v", [d])
             for h in (0, 1):
                 d = e = done("v", V.tensor_tensor(T.s6[0:64, 6 * h:6 * h + 6], t1[64 * h:64 * h + 64, 0:2 * CK:32], t1[64 * h:64 * h + 64, 16:2 * CK:32], OP.add))
             fill()
-            sides = [(T.s6[0:64, o:o + 3], T.s6[0:64, o + 6:o + 9]) for o in (0, 3)]
-        need("v", [d])
-        done("v", V.tensor_tensor(pick[0:P, 0:3], sides[0][0], sides[0][1], OP.is_lt))
+            src, step, other = T.s6, 1, 6
         need("v", [e])
-        d = done("v", V.tensor_tensor(pick[0:P, 3:6], sides[1][0], sides[1][1], OP.subtract))
+        o = 3 * step
+        d = done("v", V.tensor_tensor(pick[0:P, 3:6], src[0:P, o:2 * o:step], src[0:P, o + other:2 * o + other - step + 1:step], OP.subtract))
         fill()
         need("v", [d])
-        v_pick[k] = done("v", V.tensor_tensor(pick[0:P, 6:9], pick[0:P, 0:3], pick[0:P, 3:6], OP.mult))
-        fill()
-        need("v", [v_pick[k]])
-        d = [under(R, "wa", "mask4", u) for u in range(3)][-1]
+        picks = []
+        for u in range(3):
+            c = u * step
+            picks.append(done("v", V.tensor_scalar(pick[0:P, 6 + u:7 + u], src[0:P, c:c + 1], src[0:P, c + other:c + other + 1], pick[0:P, 3 + u:4 + u], OP.is_lt, OP.mult)))
+        v_pick[k] = picks[-1]
+        for u in range(3):
+            need("v", [picks[u]])
+            d = under(R, "wa", "mask4", u)
         fill()
         need("v", [d])
         d = done("v", V.transpose(T["t2" + k][0:P, :], T["wa" + k][0:P, :]))
@@ -351,24 +361,8 @@ def rank_program(g, core, T, topo):
         for i in range(lo, hi):
             off[i] = d
 
-    def single_steps(R):
-        k, P, last = R["k"], R["P"], []
-
-        def spread_out(u):
-            need("v", [v_pick[k], c_lists])
-            last.append(under(R, "wb", "mask16", u))
-
-        def turn():
-            need("v", [last[-1]])
-            last.append(done("v", V.transpose(T["t3" + k][0:P, :], T["wb" + k][0:P, :])))
-
-        def scan():
-            need("v", [last[-1]])
-            v_s16[k] = done("v", V.tensor_tensor_scan(T["s16" + k][0:P, :], T.rr1[0:P, 0:CK], T["t3" + k][0:P, :], 0.0, OP.add, OP.max))
-        return [lambda u=u: spread_out(u) for u in range(3)] + [turn, scan]
-
     def gather(q, lo, hi):
-        out = T.xt[:, 16 * lo:16 * hi]
+        out = T.xt[:, 4 * PAD + 16 * lo:4 * PAD + 16 * hi]
         win = T.xsb[:, 0:4 * NT].indirect(T.off4[:, lo:hi])
         need(q, [off[i] for i in range(lo // 24, (hi + 23) // 24)] + [LDX, LDX2])
         return done(q, A.activation(out, win, AF.Copy) if q == "a" else V.tensor_copy(out, win))
@@ -384,31 +378,40 @@ def rank_program(g, core, T, topo):
             return slice(8 + i, 16, 2)
         return ((slice(0, 4, 2), slice(4, 8, 2), slice(1, 8, 2)) if bits else (slice(1, 4, 2), slice(5, 8, 2), slice(0, 8, 2)))[i]
 
-    def arrivals(isfar):
-        n = 0
-        for r in (far if isfar else near):
-            i = (far_of(r) if isfar else near_of(r)).index(me)
-            for bits in (True, False):
-                n += len(topo.engines(cores[r], core)[lanes(isfar, bits, i)])
-        return n
+    def landing(r, e):
+        return e - (e > r)
 
-    def send(isfar, dep, codes, planes, dcodes, dplanes, rsem):
+    def answers(e):
+        isfar = e in far
+        i = (far_of(e) if isfar else near_of(e)).index(me)
+        return sum(len(topo.engines(cores[e], core)[lanes(isfar, bits, i)]) for bits in (True, False))
+
+    def transfer(r, es, bits, src, lo, dst, there, rsem):
+        src, dst = T[src][:, lo:lo + CK], T[dst][:, there:there + CK]
+        if bits:
+            src, dst = src.bitcast(dt.uint8), dst.bitcast(dt.uint8)
+        ad = topo.addr(cores[r])
+        local[0] += len(es)
+        return RemoteDMATransfer(dst_ids=[DstId(rid=ad[0], pnc=ad[1])], dma_engine_mask=sum(1 << k for k in es), remote_sem=T.sem[rsem], src=src, dst=dst)
+
+    def tile_codes(i, deps):
+        need("v", deps)
+        return done("v", V.quantize_mx(T.ct[:, 128 * i:128 * i + 128], T.cs[:, 128 * i:128 * i + 128], T.xt[:, 4 * CK * i:4 * CK * i + 512]))
+
+    def dispatch(i, deps):
+        r = order[i]
+        isfar = r in far
+        es = topo.engines(core, cores[r])[-8:]
+        there = (far_of(r) if isfar else near_of(r)).index(me) * CK
+        need("p", [tile_codes(i, deps)])
+        for bits, src, dst in ((True, "ct", "rxf" if isfar else "rxn"), (False, "cs", "rxfs" if isfar else "rxns")):
+            g.remote_dma_fused([transfer(r, es, bits, src, 128 * i + PAD, dst, there, "df" if isfar else "dn")], local_sem=T.sem["loc"])
+
+    def answer(isfar, dep):
         need("p", [dep])
-        for bits, sname, dname in ((True, codes, dcodes), (False, planes, dplanes)):
-            tr = []
-            for i, r in enumerate(far if isfar else near):
-                es = topo.engines(core, cores[r])[lanes(isfar, bits, i)]
-                there = (far_of(r) if isfar else near_of(r)).index(me) * CK
-                src = T[sname][:, pos[r]:pos[r] + CK]
-                dst = T[dname][:, there:there + CK]
-                if bits:
-                    src, dst = src.bitcast(dt.uint8), dst.bitcast(dt.uint8)
-                ad = topo.addr(cores[r])
-                tr.append(RemoteDMATransfer(dst_ids=[DstId(rid=ad[0], pnc=ad[1])], dma_engine_mask=sum(1 << k for k in es), remote_sem=T.sem[rsem], src=src, dst=dst))
-                local[0] += len(es)
-            g.remote_dma_fused(tr, local_sem=T.sem["loc"])
-
-    DF, DN, RF, RN = ("df", arrivals(True)), ("dn", arrivals(False)), ("rf", arrivals(True)), ("rn", arrivals(False))
+        for bits, name in ((True, "rc"), (False, "rs")):
+            g.remote_dma_fused([transfer(r, topo.engines(core, cores[r])[lanes(isfar, bits, i)], bits, name, (FAR0 if isfar else NEAR0) + CK * i,
+                                         name, LAND0 + CK * landing(r, me), "r%d" % me) for i, r in enumerate(far if isfar else near)], local_sem=T.sem["loc"])
 
     def qweight(i):
         need("v", [LDW])
@@ -449,54 +452,42 @@ def rank_program(g, core, T, topo):
         later["offz"] = done("v", V.tensor_scalar(T.offz[:], T.tokf1[:, 0:HALF:32], pcol(P31), None, OP.add))
 
     fill = filler([window_offsets, lambda: equal(R2, 0, CK), lambda: equal(R2, CK, HALF), lambda: ties(R2), lambda: ties_out(R2),
-                   lambda: zeros("last", T.akk2[:, 22:23]), lambda: zeros("win", T.win2[:, CK:2 * CK]), lambda: zeros("win", T.win2[:, WIN + CK:WIN + 2 * CK])])
+                   lambda: zeros("last", T.akk2[:, 22:23]), lambda: zeros("pad", T.xt[:, 0:4 * PAD])])
     lists(R1, v_offr, T.zs1[:], [a_zs["1"]], fill)
     need("a", [later["offz"], a_zs["2"]])
     a_zc = done("a", A.activation(T.zc[:], T.zs2[:].indirect(T.offz[:]), AF.Copy))
     offsets(0, range(4))
-    gather("a", 0, 24)
+    a_x = [gather("a", 0, 24)]
     for i in (1, 2, 3):
         offsets(i, (0, 1))
     fill()
     upper(1, 4)
-    fill()
-    a_gf = gather("a", 24, 36)
-    v_gf = gather("v", 36, 72)
+    a_x += [gather("a", 24 * i, 24 * i + 24) for i in (1, 2, 3)]
     fill(8)
-    v_qfar = pack(FAR0, NEAR0, [a_gf, v_gf], "xt", "ct", "cs")
-    send(True, v_qfar, "ct", "cs", "rxf", "rxfs", "df")
-    c_slots = iota("slots", [[1, 576]], 1)
+    qunpack(0)
+    qunpack(1)
+    dispatch(0, [a_x[0], later["pad"]])
 
-    a_gn = gather("a", 72, 96)
     c_cl = done("a", A.activation(T.cl[:, NP:NP + HALF], T.k1[:], AF.Copy, scale=0.0))
     c_cl = done("a", A.activation(T.cl[:, NP + HALF:NP + NT], T.k1[:], AF.Copy, scale=0.0))
     v_qw = []
-    done("v", V.tensor_scalar(T.mcol[:], T.k1[:, 0:4], pcol(PM), 4.0, OP.is_equal, OP.mult))
-    c_lists = done("v", V.tensor_scalar(T.mask16[:], T.k1[:, 0:32], pcol(P15), -BIG, OP.not_equal, OP.mult))
-    one = single_steps(R1)
-    fill = filler([lambda: v_qw.append(qweight(0))] + one[0:3] + [lambda: v_qw.append(qweight(1)), one[3], lambda: v_qw.append(qweight(2)), one[4],
-                                                                  lambda: v_qw.append(qweight(3)), lambda: zeros("pad", T.xt[:, 4 * (OWN0 + CK):4 * ALLC])])
+
+    def masks():
+        done("v", V.tensor_scalar(T.mcol[:, 0:4], T.k1[:, 0:4], pcol(PM), 4.0, OP.is_equal, OP.mult))
+        done("v", V.tensor_scalar(T.mcol[:, 4:8], T.k1[:, 0:4], pcol(P3), 0.25, OP.is_equal, OP.mult))
+        later["masks"] = done("v", V.tensor_scalar(T.mk[:], T.im4[:], pcol(PM), 4.0, OP.is_equal, OP.mult))
+
+    weights = [lambda i=i: v_qw.append(qweight(i)) for i in range(4)]
+    sends = [lambda i=i: dispatch(i, [a_x[i]]) for i in range(4)]
+    fill = filler([masks, weights[0], sends[1], weights[1], sends[2], weights[2], sends[3], weights[3]])
     need("v", [later["last"]])
     v_offr = scalar_places(R2, fill)
-    lists(R2, v_offr, T.zc[:], [a_zc, later["win"]], fill)
+    lists(R2, v_offr, T.zc[:], [a_zc, c_win], fill)
     offsets(4, (0, 1))
     offsets(5, (0, 1))
     fill()
     upper(4, 6)
-    fill()
-    a_gn = gather("a", 96, 108)
-    v_gn = gather("v", 108, 120)
-    a_go = gather("a", 120, 144)
-    fill(10)
-    v_qnear = pack(NEAR0, OWN0, [a_gn, v_gn], "xt", "ct", "cs")
-    send(False, v_qnear, "ct", "cs", "rxn", "rxns", "dn")
-
-    def spread(i):
-        k, block = ("1", i) if i < 4 else ("2", i - 4)
-        need("a", [v_s16[k]])
-        for b in (0, 1):
-            d = done("a", A.activation(T.offf[32 * b:32 * b + 32, 6 * i:6 * i + 6], T["s16" + k][32 * block:32 * block + 32, 15:CK:16], AF.Copy))
-        return d
+    a_x.append(gather("a", 96, 120))
 
     def products(stat, plane, codes, planes, lo, hi, bank, deps):
         need("t", deps)
@@ -525,74 +516,92 @@ def rank_program(g, core, T, topo):
         return done(q, V.tensor_copy(out, src) if q == "v" else A.activation(out, src, AF.Copy))
 
     table = T.cl[:, NP:NP + NT]
-    tk = {"last": None}
+    tk = {"last": None, "step": 0}
 
-    def tab(k):
+    def singles():
+        need("v", [off[N - 1], later["masks"]])
+        for m in range(4):
+            tk["last"] = done("v", V.tensor_scalar(T.cq[:, m:24 * N:4], T.off4[:, m:24 * N:4], pcol(P3), T.mcol[:, 4 + m:5 + m], OP.subtract, OP.mult))
+
+    def singles_sum():
+        need("v", [tk["last"], c_reset4])
+        tk["last"] = done("v", V.tensor_tensor_scan(T.cq[:, NP:NP + 24 * N], T.reset4[:, 0:24 * N], T.cq[:, 0:24 * N], 0.0, OP.mult, OP.add))
+
+    def singles_out():
+        need("v", [tk["last"]])
+        tk["last"] = done("v", V.tensor_copy(T.off16[:], T.cq[:, NP + 3:NP + 24 * N:4]))
+
+    def tab():
+        k = tk["step"]
+        tk["step"] += 1
         e = (k + 1) // 2
         o16 = T.off16[:, 6 * idx[e]:6 * idx[e] + 6]
+        need("v", [tk["last"], c_cl, c_slots])
         if k % 2:
-            need("a", [tk["last"], v_o16])
-            tk["last"] = done("a", A.activation(T.cl[:, CK * (e - 1):CK * e], table.indirect(o16), AF.Copy))
-            if e == N - 1:
-                mask(0, NP)
+            tk["last"] = tk["prev"] = done("v", V.tensor_tensor(T.cm[:, CK * (e - 1):CK * e], table.indirect(o16), T.mk[:], OP.mult))
         else:
-            need("v", [tk["last"]])
             tk["last"] = done("v", V.tensor_copy(table.indirect(o16), T.slots[:, CK * e:CK * e + CK]))
 
-    def mask(lo, hi):
-        need("a", [tk["last"], c_lists])
-        for m in range(4):
-            tk[lo] = done("a", A.activation(T.cm[:, lo + m:hi:4], T.cl[:, lo + m:hi:4], AF.Copy, scale=T.mcol[:, m:m + 1]))
+    def expert(name, codes, planes, c0, lo, hi, bank, deps, both):
+        p = products("qw", "pw", codes, planes, c0, c0 + hi - lo, bank, deps)
+        tk[name] = [relus("a", (1, 3) if both else range(4), lo, hi, bank, p)]
+        if both:
+            tk[name].append(relus("v", (0, 2), lo, hi, bank, p))
 
-    def wrap(lo, hi):
-        need("v", [tk[lo], c_reset4])
-        d = done("v", V.tensor_tensor_scan(T.cq[:, lo:hi], T.reset4[:, 0:hi - lo], T.cm[:, lo:hi], 0.0, OP.mult, OP.add))
-        need("v", [d])
-        return done("v", V.tensor_scalar(T.offc[:, lo // 4:hi // 4], T.cq[:, lo + 3:hi:4], pcol(P3), None, OP.add))
+    def far_results():
+        expert("far", "rxf", "rxfs", 0, FAR0, NEAR0, 4, [("df", 48), v_qw[-1]], True)
 
-    two = single_steps(R2)
-    for step in two[0:4]:
-        step()
-    v_qown = pack(OWN0, ALLC, [a_go, later["pad"]], "xt", "ct", "cs")
-    two[4]()
-    for i in range(6):
-        d = spread(i)
-    need("a", [d])
-    a_offf = done("a", A.activation(T.offf[64:128, :], T.offf[0:64, :], AF.Copy))
-    p_own = products("qw", "pw", "ct", "cs", OWN0, ALLC, 0, [v_qown, v_qw[-1], a_acc["2"], v_tie["2"]])
-    a_own = relus("a", range(4), OWN0, ALLC, 0, p_own)
-    qunpack(0)
-    qunpack(1)
-    need("v", [a_offf])
-    v_o16 = done("v", V.tensor_copy(T.off16[:], T.offf[:]))
-    qunpack(2)
-    need("v", [v_o16, c_cl, c_slots])
-    tab(0)
-    tab(1)
-    v_rown = pack(OWN0, ALLC, [a_own], "rt", "rc", "rs")
-    tab(2)
-    p_far = products("qw", "pw", "rxf", "rxfs", 0, 288, 4, [DF])
-    a_far = relus("a", (1, 3), FAR0, NEAR0, 4, p_far)
-    v_far = relus("v", (0, 2), FAR0, NEAR0, 4, p_far)
-    v_qe = qunpack(3)
-    v_rfar = pack(FAR0, NEAR0, [a_far, v_far], "rt", "rc", "rs")
-    send(True, v_rfar, "rc", "rs", "bkf", "bkfs", "rf")
-    tab(3)
-    tab(4)
-    p_near = products("qw", "pw", "rxn", "rxns", 0, 192, 0, [DN, a_own])
-    a_near = relus("a", (1, 3), NEAR0, OWN0, 0, p_near)
-    v_near = relus("v", (0, 2), NEAR0, OWN0, 0, p_near)
-    zeros("aa", T.aa[:, 0:4])
-    v_rnear = pack(NEAR0, OWN0, [a_near, v_near], "rt", "rc", "rs")
-    send(False, v_rnear, "rc", "rs", "bkn", "bkns", "rn")
-    for k in range(5, 2 * N - 1):
-        tab(k)
-    mask(NP, NP + NT)
+    def far_answer():
+        answer(True, pack(FAR0, NEAR0, tk["far"], "rt", "rc", "rs"))
 
-    u_own = products("qe", "pe", "rc", "rs", OWN0, ALLC, 4, [v_rown, v_qe, a_far, v_far])
-    d_own = [unpack("a", me, CK, 4, 0, b, u_own[b]) for b in range(4)]
-    v_prev = wrap(0, NP)
-    v_last = wrap(NP, NP + NT)
+    def last_unpack():
+        tk["qe"] = qunpack(3)
+
+    def near_products(both):
+        expert("near", "rxn", "rxns", 0, NEAR0, OWN0, 0, [("dn", 32), v_qw[-1], a_acc["2"], v_tie["2"]], both)
+
+    def near_results():
+        answer(False, pack(NEAR0, OWN0, tk["near"], "rt", "rc", "rs"))
+
+    def own_codes():
+        tk["codes"] = tile_codes(N - 1, [a_x[N - 1]])
+
+    def own_products():
+        expert("own", "ct", "cs", 128 * (N - 1), OWN0, LAND0, 4, [tk["codes"]] + tk["far"], False)
+
+    def own_results():
+        d = pack(OWN0, LAND0, tk["own"], "rt", "rc", "rs")
+        u = products("qe", "pe", "rc", "rs", OWN0, LAND0, 0, [d, tk["qe"]] + tk["near"])
+        tk["back"] = [unpack("a", me, CK, 0, PAD, b, u[b]) for b in range(4)][-1]
+
+    work = {"s": singles, "t": singles_sum, "u": singles_out, "d": lambda: dispatch(4, [a_x[4]]), "c": own_codes,
+            "g": lambda: a_x.append(gather("a", 120, 144)),
+            "z": lambda: zeros("aa", T.aa[:, 0:4]), "f": far_results, "F": far_answer, "n": lambda: near_products(False), "m": lambda: near_products(True),
+            "N": near_results, "o": own_products, "O": own_results}
+    work.update({".": tab, "a": lambda: qunpack(2), "b": last_unpack})
+    for step in PLAN[me]:
+        work[step]()
+    d_own, a_own = tk["back"], tk["own"][0]
+
+    need("a", [tk["last"]])
+    for m in range(4):
+        a_last = done("a", A.activation(T.cm[:, NP + m:NP + NT:4], T.cl[:, NP + m:NP + NT:4], AF.Copy, scale=T.mcol[:, m:m + 1]))
+    need("v", [tk["prev"]])
+    sums = [done("v", V.tensor_tensor_scan(T.cq[:, b:NP:4], T.reset4[:, 0:NP // 4], T.cm[:, b:NP:4], 0.0, OP.mult, OP.add)) for b in range(4)]
+    for b in range(4):
+        need("v", [sums[b]])
+        v_prev = done("v", V.tensor_scalar(T.offc[:, b:NP // 4:4], T.cq[:, 12 + b:NP:16], pcol(P3), None, OP.add))
+
+    def last_sum(k):
+        lo = NP + 128 * k
+        need("v", [a_last])
+        tk["sum"] = done("v", V.tensor_tensor_scan(T.cq[:, lo:lo + 128], T.reset4[:, 0:128], T.cm[:, lo:lo + 128], 0.0, OP.mult, OP.add))
+
+    def last_out():
+        need("v", [tk["sum"]])
+        tk["out"] = done("v", V.tensor_scalar(T.offc[:, NP // 4:(NP + NT) // 4], T.cq[:, NP + 3:NP + NT:4], pcol(P3), None, OP.add))
+
+    fill = filler([lambda k=k: last_sum(k) for k in range(3)] + [last_out])
 
     def chain(e, deps):
         need("v", deps + [v_prev, later["aa"]])
@@ -600,30 +609,25 @@ def rank_program(g, core, T, topo):
         s = slice(slot(e), slot(e) + 4 * CK)
         return done("v", V.tensor_tensor(T.aa[:, s], T.aa[:, 0:slot(e)].indirect(T.offc[:, o:o + 24]), T.aa[:, s], OP.add))
 
-    def near_back():
-        u = products("qe", "pe", "bkn", "bkns", 0, 192, 0, [RN, a_near, v_near])
-        for i in range(2):
-            got[near[i]] = [unpack("a", near[i], CK, 0, CK * i, b, u[b]) for b in range(4)][-1:]
+    got = {me: [d_own]}
+    free = {4: [a_own], 0: [d_own]}
 
-    def far_back(first):
-        u = products("qe", "pe", "bkf", "bkfs", 0, 288, 4, [RF, d_own[-1]])
-        d1 = [unpack("v", far[0], first * CK, 4, 0, b, u[b]) for b in (0, 1)][-1]
-        d2 = [unpack("a", far[0], first * CK, 4, 0, b, u[b]) for b in (2, 3)][-1]
-        need("a", [d1])
-        for i in range(3):
-            got[far[i]] = [d1, d2] if i < first else [unpack("a", far[i], CK, 4, CK * i, b, u[b]) for b in (2, 3, 0, 1)][-1:]
+    def back(e, both):
+        j = landing(me, e)
+        bank, hi = (4, 0)[j % 2], LAND0 + CK * j + CK
+        u = products("qe", "pe", "rc", "rs", hi - 128, hi, bank, [("r%d" % e, answers(e))] + free[bank])
+        got[e] = [[unpack(q, e, CK, bank, PAD, b, u[b]) for b in which][-1] for q, which in ((("v", (0, 2)), ("a", (1, 3))) if both else (("a", range(4)),))]
+        free[bank] = got[e]
 
-    got = {me: d_own[-1:]}
     step = None
-    if far[0] == 0:
-        far_back(2)
-        near_back()
-    else:
-        near_back()
-    for e in range(1, N):
-        if e == far[0]:
-            far_back(1)
-        step = chain(e, got[e] + got[0] + [step])
+    for e in range(N):
+        if e != me:
+            back(e, e in BOTH[me])
+        if e > 1:
+            fill()
+        if e:
+            step = chain(e, got[e] + got[0] + [step])
+    v_last = tk["out"]
 
     win = T.aa[:, 0:slot(N)]
     for q, quarters in (("v", (0, 1)), ("a", (2, 3))):

@@ -9,7 +9,8 @@ STEP = 2.0 ** 90
 F8, U8, F32, BF, U16, I32 = "float8_e4m3fn_x4", "uint8", "float32", "bfloat16", "uint16", "int32"
 
 PAD = 128 - CK
-FAR0, NEAR0, OWN0, LAND0 = 0, 3 * CK, 5 * CK, 5 * CK + 128
+FAR0, NEAR0, OWN0, ALLR = PAD, PAD + 3 * CK, PAD + 5 * CK, PAD + 5 * CK + 128
+NEARC, OWNC, LAND0 = 3 * 128, 3 * 128 + 2 * CK, 4 * 128 + 2 * CK
 HALF = NT // 2
 WIN = HALF + CK
 NP = CK * (N - 1)
@@ -17,12 +18,12 @@ ROUNDS = ({"k": "1", "W": 16, "NS": 5, "bank": 0, "G": 144, "views": (16, 0), "P
           {"k": "2", "W": 32, "NS": 6, "bank": 2, "G": 192, "views": (64, 0), "P": 64})
 
 SHAPES = {
-    BF: {"xsb": 4 * NT, "wgs": 32, "w1s": 2048, "ones": 512, "et": 2048, "reset4": NP, "xt": 4 * (PAD + N * CK), "rt": 4 * LAND0, "sums": 7 * CK},
+    BF: {"xsb": 4 * NT, "wgs": 32, "w1s": 2048, "et": 2048, "reset4": 516, "xt": 4 * (PAD + N * CK), "rt": 4 * ALLR, "sums": 7 * CK},
     F8: {"qx": NT, "qw": 512, "qe": 512, "ct": 128 * N, "rxn": 192, "rxf": 288, "rc": LAND0 + NP},
     U8: {"px": NT, "pw": 512, "pe": 512, "cs": 128 * N, "rxns": 192, "rxfs": 288, "rs": LAND0 + NP},
     I32: {"pi": 2, "pci": 8},
     U16: {"offw": 32, "off4": 144, "off16": 36, "offc": 216, "offz": 6},
-    F32: {"pc": 8, "pd": 12, "offwf": 32, "im4": CK, "slots": 576, "mask4": 32, "mk": CK, "rr4": CK, "mcol": 8, "s6": 12,
+    F32: {"pc": 8, "pd": 12, "offwf": 32, "im4": CK, "slots": 576, "mask4": 32, "mk": CK, "rr4": CK, "mcol": 8, "s6": 12, "gg": 4 * CK, "one": 288, "tokr": 144,
           "first": 12, "zc": CK, "akm": 44, "cl": NP + NT, "cm": NP + NT, "cq": NP + NT, "aa": 8 + 4 * 576, "yy": 4 * NT},
 }
 for R in ROUNDS:
@@ -35,12 +36,18 @@ for R in ROUNDS:
     SHAPES[F32].update({"k" + k: HALF, "m3" + k: HALF, "rr" + k: HALF, "md" + k: HALF, "sc" + k: HALF, "zs" + k: HALF, "akk" + k: 4 * ns, "akq" + k: 4 * ns,
                         "tok" + k: 16 * n, "tokf" + k: 16 * n, "win" + k: 2 * WIN, "t1" + k: 2 * CK, "pick" + k: 12,
                         "wa" + k: CK, "t2" + k: CK, "s4" + k: CK})
-PLAN = ["satudf.Fng.N.c.o.z.b.O....", "satud.f.Fng.N.c.o.z.b.O...", "satudmg.Nc.fzFo.b.O.......",
-        "satudf.Fg.n.c.o.N.z.b.O...", "gsatud.c.f.Fno.N.z.b.O....", "gsatud.c.z..f.Fno.N.b.O..."]
-BOTH = [(5,), (5,), (5,), (1, 2), (1, 2), (1, 2)]
 SCRATCH = {name: ("sbuf", [128, n], kind) for kind in SHAPES for name, n in SHAPES[kind].items()}
 SCRATCH["pp"] = ("psum", [128, 4096], F32)
-SEMAPHORES = ["sv", "sa", "sten", "ldx", "ldx2", "ldg", "ldw", "sty", "sty2", "loc", "dn", "df"] + ["r%d" % e for e in range(N)] + ["sp%d" % i for i in range(12)]
+SEMAPHORES = ["sv", "sa", "sten", "ldx", "ldx2", "ldg", "ldw", "sty", "loc", "dn", "df"] + ["r%d" % e for e in range(N)] + ["sp%d" % i for i in range(17)]
+
+PLAN = ["seGtfudAFh.H.jn.NgJ.a.c.b..oO...", "esAGtug.df..FhcHj.nJoa.N.b..O...", "seGt.ug.nd.f..A..NFhcHjabJ.oO...",
+        "e.st.G.ugfd..FhAc.Hnj.oN.a.JbO..", "es.GAg.t.dac.o.bfuF.hHj..nO.NJ..", ".seG.g.Adt.acoub.Of....F.hHjn.JN"]
+SUM = ["WU1yUk2Ul3LUU4m5", "UWy1UUk2l3UUL4m5", "UUW1yUk2l3UUL4m5", "WUUU1yk2l3LU4Um5", "UWU1yUUkUl23L4m5", "WUUyU1k2lU3L4m5"]
+COMING = [[1, 2, 3, 4, 5], [0, 2, 3, 4, 5], [0, 1, 3, 4, 5], [1, 2, 0, 4, 5], [0, 1, 3, 2, 5], [0, 1, 3, 2, 4]]
+SECOND = list("uagsb1t2c3d")
+ORDER = [[3, 1, 2, 4, 5, 0], [3, 0, 2, 4, 5, 1], [3, 0, 1, 4, 5, 2], [0, 1, 2, 4, 5, 3], [0, 1, 2, 3, 5, 4], [0, 1, 2, 3, 4, 5]]
+BACKWARD = [True] + [False] * 5
+HELP = [0, 0, 0, 0, 0, 0]
 
 
 def rank_program(g, core, T, topo):
@@ -55,8 +62,11 @@ def rank_program(g, core, T, topo):
     def near_of(r):
         return [k for k in range(N) if k != r and topo.chip(cores[k]) == topo.chip(cores[r])]
 
+    def coming(r):
+        return COMING[r]
+
     far, near = far_of(me), near_of(me)
-    order = far + near + [me] if far[0] == 0 else far[:1] + near + far[1:] + [me]
+    order = ORDER[me] or [e for part in (range(4), range(4, N)) for e in far + near + [me] if e in part]
     idx = {e: i for i, e in enumerate(order)}
 
     Q = {"v": (g.vector, "sv"), "a": (g.scalar, "sa"), "t": (g.tensor, "sten"), "p": (g, None), "s": (g.sync, None)}
@@ -110,19 +120,18 @@ def rank_program(g, core, T, topo):
         c_offwf = done("v", V.memset(T.offwf[:, 8 * i - 16:8 * i - 8], float(4 * order[i])))
     need("v", [d])
     c_pc = done("v", V.tensor_copy(T.pc[:, 0:7], T.pci[:, 0:7]))
-    for j, c in enumerate((0.0, 1.0)):
-        done("v", V.memset(T.akm[:, j:44:4], c))
+    c_ones = done("v", V.memset(T.reset4[:], 1.0))
 
     def pcol(k, lo=0, hi=128):
         return T.pc[lo:hi, k:k + 1]
 
     need("v", [c_offwf, c_pc])
     c_offw = done("v", V.tensor_scalar(T.offw[:], T.offwf[:], pcol(P3), None, OP.add))
-    c_akm = done("v", V.memset(T.akm[:, 2:44:4], -1.0))
-    done("v", V.memset(T.wga2[:, 0:256], 0.0))
-    c_zero["2"] = done("v", V.memset(T.wga2[:, 512:768], 0.0))
+    need("v", [c_ones])
+    c_ones = c_reset4 = done("v", V.memset(T.reset4[:, 0:516:4], 0.0))
+    c_zero["2"] = None
 
-    SGN, KC, TOK, MB, CV, TOK2 = 0, 2, 4, 6, 8, 9
+    SGN, KC, TOK, MB, CV = 0, 2, 4, 6, 8
     need("a", [c_pc])
     done("a", A.activation(T.pd[:, MB:MB + 2], T.pc[:, P15:P15 + 2], AF.Copy, scale=-STEP))
     done("a", A.activation(T.pd[:, SGN:SGN + 2], T.pc[:, H1:H1 + 2], AF.Copy, bias=1.0, scale=-2.0))
@@ -135,17 +144,24 @@ def rank_program(g, core, T, topo):
         j += ROUNDS.index(R)
         return T.pd[:, j:j + 1]
 
+    def copy(q, out, in_):
+        return done(q, A.activation(out, in_, AF.Copy) if q == "a" else V.tensor_copy(out, in_))
+
     def gate(q, R, col, lo, n):
         k = R["k"]
-        out, win = T["wga" + k][:, 4 * col:4 * col + 16 * n], T.wgs[:, 0:32].indirect(T.offw[:, lo:lo + n])
         need(q, [c_offw, LDG, c_zero[k]])
-        return done(q, A.activation(out, win, AF.Copy) if q == "a" else V.tensor_copy(out, win))
+        return copy(q, T["wga" + k][:, 4 * col:4 * col + 16 * n], T.wgs[:, 0:32].indirect(T.offw[:, lo:lo + n]))
 
     c_reset, c_rr, c_m3, c_tok, c_kc = {}, {}, {}, {}, {}
 
     def windows(R):
         k = R["k"]
         need("a", [c_k[k], c_pd])
+        if R is R2:
+            d = done("a", A.activation(T.m32[:], T.k2[:], AF.Abs, bias=dcol(MB, R), scale=STEP))
+            need("a", [d])
+            c_reset[k] = done("a", A.activation(T.reset2[:], T.m32[:], AF.Sign))
+            return
         c_reset[k] = done("a", A.activation(T["reset" + k][:], T["k" + k][:], AF.Sign))
         c_m3[k] = done("a", A.activation(T["m3" + k][:], T["k" + k][:], AF.Abs, bias=dcol(MB, R), scale=STEP))
         need("a", [c_reset[k]])
@@ -167,20 +183,18 @@ def rank_program(g, core, T, topo):
     windows(R2)
 
     v_g1 = [gate("v", R1, 16 + 32 * i, 4 * i, 4) for i in (0, 1)][-1]
-    c_ones = done("v", V.memset(T.ones[:], 1.0))
+    d = [done("v", V.memset(T.wga2[:, o:o + 256], 0.0)) for o in (0, 512)][-1]
     need("v", [v_g1, a_g1])
-    v_qg1 = done("v", V.quantize_mx(T.qg1[:], T.pg1[:], T.wga1[:]))
+    done("v", V.quantize_mx(T.qg1[:], T.pg1[:], T.wga1[:]))
     need("v", [LDX])
     v_qx0 = done("v", V.quantize_mx(T.qx[:, 0:HALF], T.px[:, 0:HALF], T.xsb[:, 0:4 * HALF]))
-    c_reset4 = done("v", V.memset(T.reset4[:], 1.0))
-    c_win = [done("v", V.memset(T.win2[:, o + CK:o + 2 * CK], 0.0)) for o in (0, WIN)][-1]
+    c_akm = [done("v", V.memset(T.akm[:, j:44:4], c)) for j, c in enumerate((0.0, 1.0, -1.0))][-1]
     need("v", [LDX2])
     v_qx1 = done("v", V.quantize_mx(T.qx[:, HALF:NT], T.px[:, HALF:NT], T.xsb[:, 4 * HALF:4 * NT]))
-    need("v", [a_g2])
+    need("v", [a_g2, d])
     v_qg2 = done("v", V.quantize_mx(T.qg2[:], T.pg2[:], T.wga2[:]))
-    need("v", [c_im4, c_k["1"], c_reset4])
-    c_reset4 = done("v", V.memset(T.reset4[:, 0:NP:4], 0.0))
-    done("v", V.tensor_scalar(T.mask4[:], T.im4[:, 0:32], pcol(P3), -BIG, OP.not_equal, OP.mult))
+    need("v", [c_im4, c_k["1"]])
+    c_masks = done("v", V.tensor_scalar(T.mk[:], T.im4[:], pcol(PM), 4.0, OP.is_equal, OP.mult))
     t_z = {}
 
     def z(R, other, lo=0, hi=HALF):
@@ -195,8 +209,15 @@ def rank_program(g, core, T, topo):
             t_z[k] = [done("t", TE.matmul_mx(z(R, b), T["qg" + k][:, s], T["pg" + k][:, s], T.qx[:, c], T.px[:, c], h == 0, h == 1)) for b in (0, 1)]
 
     need("p", [c_ones])
-    c_et = [done("p", g.affine_select(T.et[:, 512 * b:512 * b + 512], T.ones[:], [[-1, 512]], OP.is_equal, 0.0, b, 4)) for b in range(4)]
+    c_et = [done("p", g.affine_select(T.et[:, 512 * b:512 * b + 512], T.reset4[:, o:o + 512], [[-1, 512]], OP.is_equal, 0.0, b, 4)) for b, o in enumerate((2, 0, 0, 0))]
+
+    def zeros(ap, n):
+        return done("p", g.iota(ap, [[0, n]], 0, 0, allow_small_or_imprecise_dtypes=True))
+
+    c_pad, c_last = zeros(T.xt[:, 0:4 * PAD], 4 * PAD), zeros(T.akk2[:, 22:23], 1)
+    c_win = [zeros(T.win2[:, o + CK:o + 2 * CK], CK) for o in (0, WIN)]
     c_slots = iota("slots", [[16, 36], [1, 4], [4, 4]], 1)
+    c_rt, c_aa = zeros(T.rt[:, 0:4 * PAD], 4 * PAD), zeros(T.aa[:, 0:4], 4)
 
     v_md, v_sc = {}, {}
 
@@ -225,14 +246,14 @@ def rank_program(g, core, T, topo):
     def ties_out(R):
         k, W, ns = R["k"], R["W"], R["NS"]
         need("v", [v_tie[k]])
-        v_tie[k] = done("v", V.tensor_copy(T["akk" + k][:, 0:4 * ns:4], T["corr" + k][:, W - 1:W * ns:W]))
+        v_tie[k] = copy("v", T["akk" + k][:, 0:4 * ns:4], T["corr" + k][:, W - 1:W * ns:W])
 
     a_acc, a_zs = {}, {}
 
     def scores_out(R):
         k = R["k"]
         need("a", [t_z[k][1]])
-        a_zs[k] = done("a", A.activation(T["zs" + k][:], z(R, 1), AF.Copy))
+        a_zs[k] = copy("a", T["zs" + k][:], z(R, 1))
 
     def scalar_ranks(R):
         k, W, ns = R["k"], R["W"], R["NS"]
@@ -257,7 +278,7 @@ def rank_program(g, core, T, topo):
         d = done("v", V.tensor_tensor_scan(T["akq" + k][:], T.akm[:, o:o + 4 * ns], T["akk" + k][:], 0.0, OP.mult, OP.add))
         fill()
         need("v", [d])
-        return done("v", V.tensor_copy(T["offr" + k][:, 0:ns], T["akq" + k][:, 3:4 * ns:4]))
+        return copy("v", T["offr" + k][:, 0:ns], T["akq" + k][:, 3:4 * ns:4])
 
     def vector_ranks(R, steps):
         k, W, ns, n = R["k"], R["W"], R["NS"], R["n"]
@@ -285,36 +306,28 @@ def rank_program(g, core, T, topo):
                 done("v", V.tensor_scalar(T.first[:], T["corr" + k][:, W - 1:HALF:W], -1.0, -float(CK), OP.mult, OP.add))
                 ties_out(R)
             else:
-                if q == ns + 2:
-                    steps[0]()
-                    need("v", [v_tie[k]])
-                elif q == ns + 3:
-                    steps[1]()
+                need("v", [v_tie[k]])
                 total()
         total()
         v_sum = total()
 
         def places():
+            steps[0]()
             need("v", [v_sum, c_pd])
             done("v", V.tensor_scalar(T["offr" + k][:, ns:n], T.sums[:, CK - 1:CK * (n - ns):CK], dcol(SGN, R), T.pd[:, CV:CV + 1], OP.mult, OP.add))
         return scalar_places(R, places)
 
-    v_pick, v_t3, v_s16, off = {}, {}, {}, {}
-
-    def under(R, w, mask, u):
-        k, P = R["k"], R["P"]
-        first = T.t11[:, CK + 32 * u:CK + 32 * u + 1] if R is R1 else T.s6[0:P, 3 + u:4 + u]
-        return done("v", V.tensor_scalar(T[w + k][0:P, 32 * u:32 * u + 32], T[mask][0:P, :], first, T["pick" + k][0:P, 6 + u:7 + u], OP.add, OP.subtract))
+    off = {}
 
     def lists(R, v_offr, scores, deps, fill):
         k, n, P = R["k"], R["n"], R["P"]
         win, t1, pick, offr = T["win" + k], T["t1" + k], T["pick" + k], T["offr" + k]
         fill()
         need("v", [v_offr, c_tok[k]] + deps)
-        e = done("v", V.tensor_copy(win[:, WIN:2 * WIN].indirect(offr[:, 0:n]), T["tok" + k][:]))
+        e = copy("v", win[:, WIN:2 * WIN].indirect(offr[:, 0:n]), T["tok" + k][:])
         if R is R2:
             fill()
-        d = done("v", V.tensor_copy(win[:, 0:WIN].indirect(offr[:, 0:n]), scores))
+        d = copy("v", win[:, 0:WIN].indirect(offr[:, 0:n]), scores)
         need("v", [e])
         e = done("v", V.transpose(t1[:, CK:2 * CK], win[:, WIN + CK:WIN + 2 * CK]))
         need("v", [d])
@@ -337,54 +350,46 @@ def rank_program(g, core, T, topo):
         for u in range(3):
             c = u * step
             picks.append(done("v", V.tensor_scalar(pick[0:P, 6 + u:7 + u], src[0:P, c:c + 1], src[0:P, c + other:c + other + 1], pick[0:P, 3 + u:4 + u], OP.is_lt, OP.mult)))
-        v_pick[k] = picks[-1]
         for u in range(3):
+            c = o + u * step
             need("v", [picks[u]])
-            d = under(R, "wa", "mask4", u)
+            d = done("v", V.tensor_scalar(T["wa" + k][0:P, 32 * u:32 * u + 32], T.mask4[0:P, :], src[0:P, c:c + 1], pick[0:P, 6 + u:7 + u], OP.add, OP.subtract))
         fill()
         need("v", [d])
         d = done("v", V.transpose(T["t2" + k][0:P, :], T["wa" + k][0:P, :]))
         fill()
         need("v", [d, c_rr4])
         d = done("v", V.tensor_tensor_scan(T["s4" + k][0:P, :], T.rr4[0:P, :], T["t2" + k][0:P, :], 0.0, OP.add, OP.max))
-        fill()
-        need("v", [d])
+        off["list"] = d
+        if R is R1:
+            fill()
+            need("v", [d])
 
-    def offsets(i, blocks):
-        k, block = ("1", i) if i < 4 else ("2", i - 4)
-        for b in blocks:
-            off[i] = done("v", V.tensor_scalar(T.off4[32 * b:32 * b + 32, 24 * i:24 * i + 24], T["s4" + k][32 * block:32 * block + 32, 3:CK:4], 4.0, pcol(P3, 32 * b, 32 * b + 32), OP.mult, OP.add))
+    def spread(lo, hi):
+        need("a", [off["list"]])
+        for i in range(lo, hi):
+            k, block = ("1", i) if i < 4 else ("2", i - 4)
+            for b in (0, 1):
+                d = copy("a", T.tokr[32 * b:32 * b + 32, 24 * i:24 * i + 24], T["s4" + k][32 * block:32 * block + 32, 3:CK:4])
+        need("a", [d])
+        off["spread"] = copy("a", T.tokr[64:128, 24 * lo:24 * hi], T.tokr[0:64, 24 * lo:24 * hi])
 
-    def upper(lo, hi):
-        need("v", [off[hi - 1]])
-        d = done("v", V.tensor_copy(T.off4[64:128, 24 * lo:24 * hi], T.off4[0:64, 24 * lo:24 * hi]))
+    def offsets(lo, hi):
+        need("v", [off["spread"]])
+        d = done("v", V.tensor_scalar(T.off4[:, 24 * lo:24 * hi], T.tokr[:, 24 * lo:24 * hi], 4.0, pcol(P3), OP.mult, OP.add))
         for i in range(lo, hi):
             off[i] = d
 
     def gather(q, lo, hi):
-        out = T.xt[:, 4 * PAD + 16 * lo:4 * PAD + 16 * hi]
-        win = T.xsb[:, 0:4 * NT].indirect(T.off4[:, lo:hi])
-        need(q, [off[i] for i in range(lo // 24, (hi + 23) // 24)] + [LDX, LDX2])
-        return done(q, A.activation(out, win, AF.Copy) if q == "a" else V.tensor_copy(out, win))
+        need(q, [off[lo // 24], LDX, LDX2])
+        return copy(q, T.xt[:, 4 * PAD + 16 * lo:4 * PAD + 16 * hi], T.xsb[:, 0:4 * NT].indirect(T.off4[:, lo:hi]))
 
-    def pack(lo, hi, deps, src, qc, qs):
+    def pack(src, lo, n, qc, qs, there, deps):
         need("v", deps)
-        return done("v", V.quantize_mx(T[qc][:, lo:hi], T[qs][:, lo:hi], T[src][:, 4 * lo:4 * hi]))
+        return done("v", V.quantize_mx(T[qc][:, there:there + n], T[qs][:, there:there + n], T[src][:, 4 * lo:4 * (lo + n)]))
 
     local = [0]
-
-    def lanes(isfar, bits, i):
-        if not isfar:
-            return slice(8 + i, 16, 2)
-        return ((slice(0, 4, 2), slice(4, 8, 2), slice(1, 8, 2)) if bits else (slice(1, 4, 2), slice(5, 8, 2), slice(0, 8, 2)))[i]
-
-    def landing(r, e):
-        return e - (e > r)
-
-    def answers(e):
-        isfar = e in far
-        i = (far_of(e) if isfar else near_of(e)).index(me)
-        return sum(len(topo.engines(cores[e], core)[lanes(isfar, bits, i)]) for bits in (True, False))
+    tk = {"last": None, "step": 0}
 
     def transfer(r, es, bits, src, lo, dst, there, rsem):
         src, dst = T[src][:, lo:lo + CK], T[dst][:, there:there + CK]
@@ -394,32 +399,30 @@ def rank_program(g, core, T, topo):
         local[0] += len(es)
         return RemoteDMATransfer(dst_ids=[DstId(rid=ad[0], pnc=ad[1])], dma_engine_mask=sum(1 << k for k in es), remote_sem=T.sem[rsem], src=src, dst=dst)
 
-    def tile_codes(i, deps):
-        need("v", deps)
-        return done("v", V.quantize_mx(T.ct[:, 128 * i:128 * i + 128], T.cs[:, 128 * i:128 * i + 128], T.xt[:, 4 * CK * i:4 * CK * i + 512]))
-
     def dispatch(i, deps):
         r = order[i]
+        d = pack("xt", CK * i, 128, "ct", "cs", 128 * i, deps)
+        if r == me:
+            tk["codes"] = d
+            return
         isfar = r in far
-        es = topo.engines(core, cores[r])[-8:]
-        there = (far_of(r) if isfar else near_of(r)).index(me) * CK
-        need("p", [tile_codes(i, deps)])
+        there = (far_of(r)[::-1 if BACKWARD[r] else 1] if isfar else near_of(r)).index(me) * CK
+        need("p", [d])
         for bits, src, dst in ((True, "ct", "rxf" if isfar else "rxn"), (False, "cs", "rxfs" if isfar else "rxns")):
-            g.remote_dma_fused([transfer(r, es, bits, src, 128 * i + PAD, dst, there, "df" if isfar else "dn")], local_sem=T.sem["loc"])
+            g.remote_dma_fused([transfer(r, topo.engines(core, cores[r])[-8:], bits, src, 128 * i + PAD, dst, there, "df" if isfar else "dn")], local_sem=T.sem["loc"])
 
-    def answer(isfar, dep):
+    def answer(ranks, lo, dep):
         need("p", [dep])
+        n = len(ranks)
         for bits, name in ((True, "rc"), (False, "rs")):
-            g.remote_dma_fused([transfer(r, topo.engines(core, cores[r])[lanes(isfar, bits, i)], bits, name, (FAR0 if isfar else NEAR0) + CK * i,
-                                         name, LAND0 + CK * landing(r, me), "r%d" % me) for i, r in enumerate(far if isfar else near)], local_sem=T.sem["loc"])
+            g.remote_dma_fused([transfer(r, topo.engines(core, cores[r])[-8:][i::n], bits, name, lo + CK * i, name, LAND0 + CK * coming(r).index(me), "r%d" % me)
+                                for i, r in enumerate(ranks)], local_sem=T.sem["loc"])
 
     def qweight(i):
-        need("v", [LDW])
-        return done("v", V.quantize_mx(T.qw[:, 128 * i:128 * i + 128], T.pw[:, 128 * i:128 * i + 128], T.w1s[:, 512 * i:512 * i + 512]))
+        return pack("w1s", 128 * i, 128, "qw", "pw", 128 * i, [LDW])
 
     def qunpack(i):
-        need("v", [c_et[i]])
-        return done("v", V.quantize_mx(T.qe[:, 128 * i:128 * i + 128], T.pe[:, 128 * i:128 * i + 128], T.et[:, 512 * i:512 * i + 512]))
+        return pack("et", 128 * i, 128, "qe", "pe", 128 * i, [c_et[i]])
 
     def filler(steps):
         steps = list(steps)
@@ -436,214 +439,217 @@ def rank_program(g, core, T, topo):
     own_scan(R1, s1, HALF)
     scores_out(R1)
     scalar_ranks(R1)
-    v_offr = vector_ranks(R1, [lambda: own_mask(R2, 0, HALF), lambda: own_scan(R2, 0, HALF)])
+
+    def own_turned():
+        need("v", [t_z["2"][0]])
+        v_sc["2", 0] = done("v", V.transpose(T.sc2[:], z(R2, 0)))
+
+    v_offr = vector_ranks(R1, [own_turned])
     scores_out(R2)
     tokens(R2)
     need("a", [c_reset4])
     c_rr4 = done("a", A.activation(T.rr4[:], T.reset4[:, 0:CK], AF.Copy, bias=-BIG, scale=BIG))
-    scalar_ranks(R2)
+    c_cl = [done("a", A.activation(T.cl[:, NP + o:NP + o + HALF], T.k1[:], AF.Copy, scale=0.0)) for o in (0, HALF)][-1]
     later = {}
 
-    def zeros(name, ap):
-        later[name] = done("v", V.memset(ap, 0.0))
+    scalar_ranks(R2)
 
     def window_offsets():
+        done("v", V.tensor_scalar(T.mask4[:], T.im4[:, 0:32], pcol(P3), -BIG, OP.not_equal, OP.mult))
         need("v", [c_tokf["1"]])
         later["offz"] = done("v", V.tensor_scalar(T.offz[:], T.tokf1[:, 0:HALF:32], pcol(P31), None, OP.add))
 
-    fill = filler([window_offsets, lambda: equal(R2, 0, CK), lambda: equal(R2, CK, HALF), lambda: ties(R2), lambda: ties_out(R2),
-                   lambda: zeros("last", T.akk2[:, 22:23]), lambda: zeros("pad", T.xt[:, 0:4 * PAD])])
-    lists(R1, v_offr, T.zs1[:], [a_zs["1"]], fill)
-    need("a", [later["offz"], a_zs["2"]])
-    a_zc = done("a", A.activation(T.zc[:], T.zs2[:].indirect(T.offz[:]), AF.Copy))
-    offsets(0, range(4))
-    a_x = [gather("a", 0, 24)]
-    for i in (1, 2, 3):
-        offsets(i, (0, 1))
-    fill()
-    upper(1, 4)
-    a_x += [gather("a", 24 * i, 24 * i + 24) for i in (1, 2, 3)]
-    fill(8)
-    qunpack(0)
-    qunpack(1)
-    dispatch(0, [a_x[0], later["pad"]])
-
-    c_cl = done("a", A.activation(T.cl[:, NP:NP + HALF], T.k1[:], AF.Copy, scale=0.0))
-    c_cl = done("a", A.activation(T.cl[:, NP + HALF:NP + NT], T.k1[:], AF.Copy, scale=0.0))
-    v_qw = []
-
-    def masks():
+    def scales():
         done("v", V.tensor_scalar(T.mcol[:, 0:4], T.k1[:, 0:4], pcol(PM), 4.0, OP.is_equal, OP.mult))
-        done("v", V.tensor_scalar(T.mcol[:, 4:8], T.k1[:, 0:4], pcol(P3), 0.25, OP.is_equal, OP.mult))
-        later["masks"] = done("v", V.tensor_scalar(T.mk[:], T.im4[:], pcol(PM), 4.0, OP.is_equal, OP.mult))
+        later["scales"] = done("v", V.tensor_scalar(T.mcol[:, 4:8], T.k1[:, 0:4], pcol(P3), None, OP.is_equal))
 
-    weights = [lambda i=i: v_qw.append(qweight(i)) for i in range(4)]
-    sends = [lambda i=i: dispatch(i, [a_x[i]]) for i in range(4)]
-    fill = filler([masks, weights[0], sends[1], weights[1], sends[2], weights[2], sends[3], weights[3]])
-    need("v", [later["last"]])
-    v_offr = scalar_places(R2, fill)
-    lists(R2, v_offr, T.zc[:], [a_zc, c_win], fill)
-    offsets(4, (0, 1))
-    offsets(5, (0, 1))
+    fill = filler([window_offsets, lambda: equal(R2, 0, CK), lambda: equal(R2, CK, HALF), lambda: ties(R2), scales, lambda: ties_out(R2)])
+    lists(R1, v_offr, T.zs1[:], [a_zs["1"]], fill)
+    for b in range(4):
+        off[0] = done("v", V.tensor_scalar(T.off4[32 * b:32 * b + 32, 0:24], T.s41[0:32, 3:CK:4], 4.0, pcol(P3, 32 * b, 32 * b + 32), OP.mult, OP.add))
+    need("a", [later["offz"], a_zs["2"]])
+    a_zc = copy("a", T.zc[:], T.zs2[:].indirect(T.offz[:]))
+    a_x = [gather("a", 0, 12)]
     fill()
-    upper(4, 6)
-    a_x.append(gather("a", 96, 120))
+    v_x = gather("v", 12, 24)
+    spread(0, 4)
+    fill(8)
+    dispatch(0, [a_x[0], v_x, c_pad])
 
-    def products(stat, plane, codes, planes, lo, hi, bank, deps):
-        need("t", deps)
+    def other_gathers():
+        offsets(1, 4)
+        a_x.extend(gather("a", 24 * i, 24 * i + 24) for i in (1, 2, 3))
+
+    def singles(lo, hi):
+        need("a", [off["spread"], later["scales"]])
+        for m in range(4):
+            tk["one"] = done("a", A.activation(T.one[:, 24 * lo + m:24 * hi:4], T.tokr[:, 24 * lo + m:24 * hi:4], AF.Copy, scale=T.mcol[:, 4 + m:5 + m]))
+
+    def singles_sum(lo, hi):
+        need("v", [tk["one"], c_reset4])
+        tk["one"] = done("v", V.tensor_tensor_scan(T.one[:, 24 * (N + lo):24 * (N + hi)], T.reset4[:, 0:24 * (hi - lo)], T.one[:, 24 * lo:24 * hi], 0.0, OP.mult, OP.add))
+
+    def singles_out(lo, hi):
+        need("v", [tk["one"]])
+        d = copy("v", T.off16[:, 6 * lo:6 * hi], T.one[:, 24 * (N + lo) + 3:24 * (N + hi):4])
+        for i in range(lo, hi):
+            tk["single", i] = d
+
+    singles(0, 4)
+
+    v_qw = []
+    weights = [lambda i=i: v_qw.append(qweight(i)) for i in range(4)]
+    sends = [lambda i=i: dispatch(i, [a_x[i]]) for i in range(N)]
+    steps = {"g": other_gathers, "u": lambda: qunpack(0), "v": lambda: qunpack(1), "w": lambda: qunpack(2), "1": sends[1], "2": sends[2], "3": sends[3],
+             "a": weights[0], "b": weights[1], "c": weights[2], "d": weights[3], "s": lambda: singles_sum(0, 4), "t": lambda: singles_out(0, 4)}
+    fill = filler([steps[s] for s in SECOND])
+    need("v", [c_last])
+    v_offr = scalar_places(R2, fill)
+    lists(R2, v_offr, T.zc[:], [a_zc] + c_win, fill)
+    spread(4, 6)
+    fill(8)
+
+    free = {0: [a_acc["2"], v_tie["2"]], 4: []}
+
+    def products(stat, plane, codes, planes, lo, n, bank, deps):
+        need("t", deps + free[bank])
         r = []
         for i in range(4):
             c = slice(128 * i, 128 * i + 128)
             o = 512 * (bank + i)
-            r.append(done("t", TE.matmul_mx(T.pp[:, o:o + hi - lo], T[stat][:, c], T[plane][:, c], T[codes][:, lo:hi], T[planes][:, lo:hi], True, True)))
+            r.append(done("t", TE.matmul_mx(T.pp[:, o:o + n], T[stat][:, c], T[plane][:, c], T[codes][:, lo:lo + n], T[planes][:, lo:lo + n], True, True)))
         return r
 
-    def relus(q, which, lo, hi, bank, deps):
-        for i in which:
+    def relus(lo, n, bank, col, deps, both):
+        last = {}
+        for i in range(4):
+            q = "v" if both and i % 2 == 0 else "a"
             need(q, [deps[i]])
-            o = 512 * (bank + i)
-            out, src = T.rt[:, 4 * lo + i:4 * hi:4], T.pp[:, o:o + hi - lo]
-            d = done(q, A.activation(out, src, AF.Relu, scale=0.05) if q == "a" else V.tensor_scalar(out, src, 0.0, 0.05, OP.max, OP.mult))
-        return d
+            o = 512 * (bank + i) + col
+            out, src = T.rt[:, 4 * lo + i:4 * (lo + n):4], T.pp[:, o:o + n]
+            last[q] = done(q, A.activation(out, src, AF.Relu, scale=0.05) if q == "a" else V.tensor_scalar(out, src, 0.0, 0.05, OP.max, OP.mult))
+        free[bank] = list(last.values())
+        return free[bank]
 
     def slot(e):
         return 4 * (1 + CK * e)
 
-    def unpack(q, e0, n, bank, col, b, dep):
-        need(q, [dep])
-        o = 512 * (bank + b) + col
-        out, src = T.aa[:, slot(e0) + b:slot(e0) + 4 * n:4], T.pp[:, o:o + n]
-        return done(q, V.tensor_copy(out, src) if q == "v" else A.activation(out, src, AF.Copy))
+    def unpack(e, bank, deps):
+        for b in range(4):
+            need("a", [deps[b]])
+            o = 512 * (bank + b) + PAD
+            d = copy("a", T.aa[:, slot(e) + b:slot(e) + 4 * CK:4], T.pp[:, o:o + CK])
+        free[bank] = got[e] = [d]
 
     table = T.cl[:, NP:NP + NT]
-    tk = {"last": None, "step": 0}
-
-    def singles():
-        need("v", [off[N - 1], later["masks"]])
-        for m in range(4):
-            tk["last"] = done("v", V.tensor_scalar(T.cq[:, m:24 * N:4], T.off4[:, m:24 * N:4], pcol(P3), T.mcol[:, 4 + m:5 + m], OP.subtract, OP.mult))
-
-    def singles_sum():
-        need("v", [tk["last"], c_reset4])
-        tk["last"] = done("v", V.tensor_tensor_scan(T.cq[:, NP:NP + 24 * N], T.reset4[:, 0:24 * N], T.cq[:, 0:24 * N], 0.0, OP.mult, OP.add))
-
-    def singles_out():
-        need("v", [tk["last"]])
-        tk["last"] = done("v", V.tensor_copy(T.off16[:], T.cq[:, NP + 3:NP + 24 * N:4]))
+    got = {}
 
     def tab():
         k = tk["step"]
         tk["step"] += 1
         e = (k + 1) // 2
         o16 = T.off16[:, 6 * idx[e]:6 * idx[e] + 6]
-        need("v", [tk["last"], c_cl, c_slots])
+        need("v", [tk["last"], tk["single", idx[e]], c_cl, c_slots])
         if k % 2:
             tk["last"] = tk["prev"] = done("v", V.tensor_tensor(T.cm[:, CK * (e - 1):CK * e], table.indirect(o16), T.mk[:], OP.mult))
         else:
-            tk["last"] = done("v", V.tensor_copy(table.indirect(o16), T.slots[:, CK * e:CK * e + CK]))
+            tk["last"] = copy("v", table.indirect(o16), T.slots[:, CK * e:CK * e + CK])
 
-    def expert(name, codes, planes, c0, lo, hi, bank, deps, both):
-        p = products("qw", "pw", codes, planes, c0, c0 + hi - lo, bank, deps)
-        tk[name] = [relus("a", (1, 3) if both else range(4), lo, hi, bank, p)]
-        if both:
-            tk[name].append(relus("v", (0, 2), lo, hi, bank, p))
+    def previous(lo, hi):
+        need("v", [tk["prev"]])
+        sums = [done("v", V.tensor_tensor_scan(T.cq[:, CK * lo + b:CK * hi:4], T.reset4[:, 0:24 * (hi - lo)], T.cm[:, CK * lo + b:CK * hi:4], 0.0, OP.mult, OP.add)) for b in range(4)]
+        for b in range(4):
+            need("v", [sums[b]])
+            d = done("v", V.tensor_scalar(T.offc[:, 24 * lo + b:24 * hi:4], T.cq[:, CK * lo + 12 + b:CK * hi:16], pcol(P3), None, OP.add))
+        for e in range(lo + 1, hi + 1):
+            tk["list", e] = d
 
-    def far_results():
-        expert("far", "rxf", "rxfs", 0, FAR0, NEAR0, 4, [("df", 48), v_qw[-1]], True)
+    def masked_last():
+        need("a", [tk["last"]])
+        for m in range(4):
+            tk["masked"] = done("a", A.activation(T.cm[:, NP + m:NP + NT:4], T.cl[:, NP + m:NP + NT:4], AF.Copy, scale=T.mcol[:, m:m + 1]))
 
-    def far_answer():
-        answer(True, pack(FAR0, NEAR0, tk["far"], "rt", "rc", "rs"))
+    def summed(lo, hi):
+        need("v", [tk["masked"]])
+        tk["sum"] = done("v", V.tensor_tensor_scan(T.cq[:, lo:hi], T.reset4[:, 0:hi - lo], T.cm[:, lo:hi], 0.0, OP.mult, OP.add))
+
+    def last_list():
+        need("v", [tk["sum"]])
+        tk["out"] = done("v", V.tensor_scalar(T.offc[:, NP // 4:(NP + NT) // 4], T.cq[:, NP + 3:NP + NT:4], pcol(P3), None, OP.add))
+
+    def far_products():
+        tk["far"] = [products("qw", "pw", "rxf", "rxfs", 0, 128, 4, [("df", 48), v_qw[-1]]), products("qw", "pw", "rxf", "rxfs", CK, 2 * CK, 0, [])]
+        far_relus(0)
+
+    def far_relus(i):
+        tk["relu"] = relus(FAR0 + CK * i, CK, 0 if i else 4, CK * (i - 1) if i else 0, tk["far"][min(i, 1)], i < HELP[me])
+
+    def far_answer(i):
+        answer([far[2 - i if BACKWARD[me] else i]], 128 * i + PAD, pack("rt", CK * i, 128, "rc", "rs", 128 * i, tk["relu"] + [c_rt]))
+
+    def near_products(both):
+        tk["near"] = relus(NEAR0, 2 * CK, 4, 0, products("qw", "pw", "rxn", "rxns", 0, 2 * CK, 4, [("dn", 32), v_qw[-1]]), both)
+
+    def own_products():
+        tk["own"] = relus(OWN0, 128, 0, 0, products("qw", "pw", "ct", "cs", 128 * idx[me], 128, 0, [tk["codes"], v_qw[-1]]), False)
+
+    def own_results():
+        d = pack("rt", OWN0, 128, "rc", "rs", OWNC, tk["own"])
+        unpack(me, 4, products("qe", "pe", "rc", "rs", OWNC, 128, 4, [d, tk["qe"]]))
 
     def last_unpack():
         tk["qe"] = qunpack(3)
 
-    def near_products(both):
-        expert("near", "rxn", "rxns", 0, NEAR0, OWN0, 0, [("dn", 32), v_qw[-1], a_acc["2"], v_tie["2"]], both)
+    todo = list(coming(me))
 
-    def near_results():
-        answer(False, pack(NEAR0, OWN0, tk["near"], "rt", "rc", "rs"))
+    def back():
+        e = todo.pop(0)
+        j = coming(me).index(e)
+        bank = 4 * (j % 2)
+        return e, bank, products("qe", "pe", "rc", "rs", LAND0 + CK * j - PAD, 128, bank, [("r%d" % e, 16 if e in far else 8)] + got[me])
 
-    def own_codes():
-        tk["codes"] = tile_codes(N - 1, [a_x[N - 1]])
+    def sums_so_far(e, lo, hi):
+        return T.aa[:, 0:slot(e)].indirect(T.offc[:, 24 * (e - 1) + lo:24 * (e - 1) + hi])
 
-    def own_products():
-        expert("own", "ct", "cs", 128 * (N - 1), OWN0, LAND0, 4, [tk["codes"]] + tk["far"], False)
+    def chain(e):
+        ready = [tk["list", e], c_aa, tk.get("chain")] + got[0]
+        if e in got:
+            need("v", ready + got[e])
+            s = slice(slot(e), slot(e) + 4 * CK)
+            tk["chain"] = done("v", V.tensor_tensor(T.aa[:, s], sums_so_far(e, 0, 24), T.aa[:, s], OP.add))
+            return
+        need("a", ready)
+        d = copy("a", T.gg[:, 192:384], sums_so_far(e, 12, 24))
+        need("v", ready)
+        need("v", [d, copy("v", T.gg[:, 0:192], sums_so_far(e, 0, 12))])
+        _, bank, u = back()
+        for b in range(4):
+            need("v", [u[b]])
+            o = 512 * (bank + b) + PAD
+            tk["chain"] = done("v", V.tensor_tensor(T.aa[:, slot(e) + b:slot(e) + 4 * CK:4], T.gg[:, b:4 * CK:4], T.pp[:, o:o + CK], OP.add))
+        free[bank] = [tk["chain"]]
 
-    def own_results():
-        d = pack(OWN0, LAND0, tk["own"], "rt", "rc", "rs")
-        u = products("qe", "pe", "rc", "rs", OWN0, LAND0, 0, [d, tk["qe"]] + tk["near"])
-        tk["back"] = [unpack("a", me, CK, 0, PAD, b, u[b]) for b in range(4)][-1]
-
-    work = {"s": singles, "t": singles_sum, "u": singles_out, "d": lambda: dispatch(4, [a_x[4]]), "c": own_codes,
-            "g": lambda: a_x.append(gather("a", 120, 144)),
-            "z": lambda: zeros("aa", T.aa[:, 0:4]), "f": far_results, "F": far_answer, "n": lambda: near_products(False), "m": lambda: near_products(True),
-            "N": near_results, "o": own_products, "O": own_results}
-    work.update({".": tab, "a": lambda: qunpack(2), "b": last_unpack})
-    for step in PLAN[me]:
+    work = {"s": lambda: singles(4, N), "t": lambda: singles_sum(4, N), "u": lambda: singles_out(4, N), ".": tab,
+            "W": lambda: previous(0, N - 1), "w": lambda: previous(0, 3), "x": lambda: previous(3, N - 1), "e": lambda: offsets(4, N),
+            "y": masked_last, "k": lambda: summed(NP, NP + 128), "l": lambda: summed(NP + 128, NP + 256), "L": lambda: summed(NP + 256, NP + NT), "m": last_list,
+            "d": sends[4], "G": lambda: a_x.append(gather("a", 96, 120)), "g": lambda: a_x.append(gather("a", 120, 144)), "c": sends[5], "o": own_products, "O": own_results,
+            "f": far_products, "h": lambda: far_relus(1), "j": lambda: far_relus(2),
+            "F": lambda: far_answer(0), "H": lambda: far_answer(1), "J": lambda: far_answer(2),
+            "n": lambda: near_products(False), "p": lambda: near_products(True),
+            "N": lambda: answer(near, NEARC, pack("rt", NEAR0, 2 * CK, "rc", "rs", NEARC, tk["near"])),
+            "a": lambda: qunpack(2), "A": lambda: qunpack(1), "b": last_unpack, "U": lambda: unpack(*back())}
+    work.update({str(e): lambda e=e: chain(e) for e in range(1, N)})
+    for step in PLAN[me] + SUM[me]:
         work[step]()
-    d_own, a_own = tk["back"], tk["own"][0]
-
-    need("a", [tk["last"]])
-    for m in range(4):
-        a_last = done("a", A.activation(T.cm[:, NP + m:NP + NT:4], T.cl[:, NP + m:NP + NT:4], AF.Copy, scale=T.mcol[:, m:m + 1]))
-    need("v", [tk["prev"]])
-    sums = [done("v", V.tensor_tensor_scan(T.cq[:, b:NP:4], T.reset4[:, 0:NP // 4], T.cm[:, b:NP:4], 0.0, OP.mult, OP.add)) for b in range(4)]
-    for b in range(4):
-        need("v", [sums[b]])
-        v_prev = done("v", V.tensor_scalar(T.offc[:, b:NP // 4:4], T.cq[:, 12 + b:NP:16], pcol(P3), None, OP.add))
-
-    def last_sum(k):
-        lo = NP + 128 * k
-        need("v", [a_last])
-        tk["sum"] = done("v", V.tensor_tensor_scan(T.cq[:, lo:lo + 128], T.reset4[:, 0:128], T.cm[:, lo:lo + 128], 0.0, OP.mult, OP.add))
-
-    def last_out():
-        need("v", [tk["sum"]])
-        tk["out"] = done("v", V.tensor_scalar(T.offc[:, NP // 4:(NP + NT) // 4], T.cq[:, NP + 3:NP + NT:4], pcol(P3), None, OP.add))
-
-    fill = filler([lambda k=k: last_sum(k) for k in range(3)] + [last_out])
-
-    def chain(e, deps):
-        need("v", deps + [v_prev, later["aa"]])
-        o = 24 * (e - 1)
-        s = slice(slot(e), slot(e) + 4 * CK)
-        return done("v", V.tensor_tensor(T.aa[:, s], T.aa[:, 0:slot(e)].indirect(T.offc[:, o:o + 24]), T.aa[:, s], OP.add))
-
-    got = {me: [d_own]}
-    free = {4: [a_own], 0: [d_own]}
-
-    def back(e, both):
-        j = landing(me, e)
-        bank, hi = (4, 0)[j % 2], LAND0 + CK * j + CK
-        u = products("qe", "pe", "rc", "rs", hi - 128, hi, bank, [("r%d" % e, answers(e))] + free[bank])
-        got[e] = [[unpack(q, e, CK, bank, PAD, b, u[b]) for b in which][-1] for q, which in ((("v", (0, 2)), ("a", (1, 3))) if both else (("a", range(4)),))]
-        free[bank] = got[e]
-
-    step = None
-    for e in range(N):
-        if e != me:
-            back(e, e in BOTH[me])
-        if e > 1:
-            fill()
-        if e:
-            step = chain(e, got[e] + got[0] + [step])
-    v_last = tk["out"]
 
     win = T.aa[:, 0:slot(N)]
-    for q, quarters in (("v", (0, 1)), ("a", (2, 3))):
-        need(q, [step, v_last])
-        r = []
-        for k in quarters:
-            o = NP // 4 + 24 * k
-            out, src = T.yy[:, NT * k:NT * k + NT], win.indirect(T.offc[:, o:o + 24])
-            r.append(done(q, V.tensor_copy(out, src) if q == "v" else A.activation(out, src, AF.Copy)))
-        dq, sem = ("s", "sty") if q == "v" else ("a", "sty2")
-        for k, d in zip(quarters, r):
-            need(dq, [d])
-            Q[dq][0].dma_start(T.y[:, NT * k:NT * k + NT], T.yy[:, NT * k:NT * k + NT]).then_inc(T.sem[sem], 16)
+    for k in range(4):
+        q = "va"[k % 2]
+        need(q, [tk["chain"], tk["out"]])
+        need("s", [copy(q, T.yy[:, NT * k:NT * k + NT], win.indirect(T.offc[:, NP // 4 + 24 * k:NP // 4 + 24 * k + 24]))])
+        g.sync.dma_start(T.y[:, NT * k:NT * k + NT], T.yy[:, NT * k:NT * k + NT]).then_inc(T.sem["sty"], 16)
 
     g.wait_ge(T.sem["loc"], local[0])
     for s in count:
         g.wait_ge(T.sem[s], count[s])
-    g.wait_ge(T.sem["sty"], 32)
-    g.wait_ge(T.sem["sty2"], 32)
+    g.wait_ge(T.sem["sty"], 64)

@@ -6,48 +6,704 @@ AF = ActivationFunctionType
 NT, CK, N = 384, 96, 6
 BIG = 1e29
 STEP = 2.0 ** 90
+UNIT = 2.0 ** 75
 F8, U8, F32, BF, U16, I32 = "float8_e4m3fn_x4", "uint8", "float32", "bfloat16", "uint16", "int32"
 
 PAD = 128 - CK
-FAR0, NEAR0, OWN0, ALLR = PAD, PAD + 3 * CK, PAD + 5 * CK, PAD + 5 * CK + 128
-NEARC, OWNC, LAND0 = 3 * 128, 3 * 128 + 2 * CK, 4 * 128 + 2 * CK
 HALF = NT // 2
 WIN = HALF + CK
 NP = CK * (N - 1)
+LAST = N - 1
 ROUNDS = ({"k": "1", "W": 16, "NS": 5, "bank": 0, "G": 144, "views": (16, 0), "P": 128},
           {"k": "2", "W": 32, "NS": 6, "bank": 2, "G": 192, "views": (64, 0), "P": 64})
+XW, RW = NT + 128 * N + NP, 128 * N + NP
 
 SHAPES = {
-    BF: {"xsb": 4 * NT, "wgs": 32, "w1s": 2048, "et": 2048, "reset4": 516, "xt": 4 * (PAD + N * CK), "rt": 4 * ALLR, "sums": 7 * CK},
-    F8: {"qx": NT, "qw": 512, "qe": 512, "ct": 128 * N, "rxn": 192, "rxf": 288, "rc": LAND0 + NP},
-    U8: {"px": NT, "pw": 512, "pe": 512, "cs": 128 * N, "rxns": 192, "rxfs": 288, "rs": LAND0 + NP},
-    I32: {"pi": 2, "pci": 8},
-    U16: {"offw": 32, "off4": 144, "off16": 36, "offc": 216, "offz": 6},
-    F32: {"pc": 8, "pd": 12, "offwf": 32, "im4": CK, "slots": 576, "mask4": 32, "mk": CK, "rr4": CK, "mcol": 8, "s6": 12, "gg": 4 * CK, "one": 288, "tokr": 144,
-          "first": 12, "zc": CK, "akm": 44, "cl": NP + NT, "cm": NP + NT, "cq": NP + NT, "aa": 8 + 4 * 576, "yy": 4 * NT},
+    BF: {"xsb": 4 * NT, "x2": 4 * NT, "wgs": 32, "w1s": 2048, "et": 516, "reset4": 516, "xt": 4 * (PAD + N * CK), "rt": 4 * 128 * N},
+    F8: {"xc": XW, "qw": 512, "qe": 512, "rc": RW},
+    U8: {"xs": XW, "pw": 512, "pe": 512, "rs": RW},
+    I32: {"pi": 2, "pci": 12},
+    U16: {"offw": 8 * N, "offx": 6 * N, "offy": 6 * N, "off1": 6 * N, "offm": 2, "offc": (NP + 2 * NT) // 4, "offz": 6},
+    F32: {"pc": 12, "pd": 24, "offwf": 8 * N, "offmf": 2, "im4": CK, "slots": NP, "mk": CK, "mcol": 4, "both": 32, "tokr": 6 * N, "zs": HALF, "m31": HALF, "m32": HALF,
+          "rr1": HALF, "md1": HALF, "cl": 2 * NT, "cm": NP + 2 * NT, "cq": NP + 2 * NT, "aa": 4 + 4 * NP, "gg": 4 + 4 * CK, "yy": 4 * NT},
 }
 for R in ROUNDS:
-    k, n, ns = R["k"], HALF // R["W"], R["NS"]
+    k, n = R["k"], HALF // R["W"]
     R["n"] = n
-    SHAPES[BF].update({"wga" + k: 4 * R["G"], "cmp" + k: n * HALF, "reset" + k: HALF, "eqw" + k: HALF, "corr" + k: HALF})
+    SHAPES[BF].update({"wga" + k: 4 * R["G"], "cmp" + k: n * HALF, "reset" + k: HALF, "eqw" + k: HALF, "corr" + k: HALF, "sums" + k: n * CK})
     SHAPES[F8].update({"qg" + k: R["G"]})
     SHAPES[U8].update({"pg" + k: R["G"]})
     SHAPES[U16].update({"offr" + k: n})
-    SHAPES[F32].update({"k" + k: HALF, "m3" + k: HALF, "rr" + k: HALF, "md" + k: HALF, "sc" + k: HALF, "zs" + k: HALF, "akk" + k: 4 * ns, "akq" + k: 4 * ns,
-                        "tok" + k: 16 * n, "tokf" + k: 16 * n, "win" + k: 2 * WIN, "t1" + k: 2 * CK, "pick" + k: 12,
-                        "wa" + k: CK, "t2" + k: CK, "s4" + k: CK})
+    SHAPES[F32].update({"k" + k: HALF, "sc" + k: HALF, "akk" + k: 4 * n, "akq" + k: 4 * n, "akm" + k: 4 * n, "first" + k: n, "tok" + k: 16 * n, "tokf" + k: 16 * n,
+                        "sin" + k: 16 * n, "win" + k: WIN, "t1" + k: CK + 128, "pair" + k: 32, "pick" + k: 16, "s4" + k: 16})
 SCRATCH = {name: ("sbuf", [128, n], kind) for kind in SHAPES for name, n in SHAPES[kind].items()}
 SCRATCH["pp"] = ("psum", [128, 4096], F32)
-SEMAPHORES = ["sv", "sa", "sten", "ldx", "ldx2", "ldg", "ldw", "sty", "loc", "dn", "df"] + ["r%d" % e for e in range(N)] + ["sp%d" % i for i in range(17)]
+SEMAPHORES = (["sv", "sa", "st", "ldx", "ldx2", "ldg", "ldw", "ld2", "sty", "loc"] + ["x%d" % e for e in range(N)] + ["r%d" % e for e in range(N)]
+              + ["sp%d" % i for i in range(28)])
 
-PLAN = ["seGtfudAFh.H.jn.NgJ.a.c.b..oO...", "esAGtug.df..FhcHj.nJoa.N.b..O...", "seGt.ug.nd.f..A..NFhcHjabJ.oO...",
-        "e.st.G.ugfd..FhAc.Hnj.oN.a.JbO..", "es.GAg.t.dac.o.bfuF.hHj..nO.NJ..", ".seG.g.Adt.acoub.Of....F.hHjn.JN"]
-SUM = ["WU1yUk2Ul3LUU4m5", "UWy1UUk2l3UUL4m5", "UUW1yUk2l3UUL4m5", "WUUU1yk2l3LU4Um5", "UWU1yUUkUl23L4m5", "WUUyU1k2lU3L4m5"]
-COMING = [[1, 2, 3, 4, 5], [0, 2, 3, 4, 5], [0, 1, 3, 4, 5], [1, 2, 0, 4, 5], [0, 1, 3, 2, 5], [0, 1, 3, 2, 4]]
-SECOND = list("uagsb1t2c3d")
-ORDER = [[3, 1, 2, 4, 5, 0], [3, 0, 2, 4, 5, 1], [3, 0, 1, 4, 5, 2], [0, 1, 2, 4, 5, 3], [0, 1, 2, 3, 5, 4], [0, 1, 2, 3, 4, 5]]
-BACKWARD = [True] + [False] * 5
-HELP = [0, 0, 0, 0, 0, 0]
+SERVED = [[3, 1, 4, 2, 5, 0], [2, 4, 5, 0, 3, 1], [0, 5, 1, 3, 4, 2], [0, 2, 1, 4, 3, 5], [1, 2, 0, 3, 5, 4], [0, 1, 2, 3, 4, 5]]
+RUNS = ((0,), (1,), (2, 3), (4,), (5,))
+TOGETHER = [[[3], [4], [1], [5, 2], [0]], [[4], [5], [3], [1, 2], [0]], [[5, 3], [4, 1], [0], [2]], [[0], [1], [2], [3, 4], [5]], [[1], [5], [0], [3, 2], [4]],
+            [[5], [0], [1], [3, 4], [2]]]
+UNPACKED = [[[e] for e in range(N)] for s in range(N)]
+PIECES = (12, 24, 24, 24, 12)
+PREVIOUS = ((0, 2), (2, 4))
+DIRECT = (1, 0)
+
+CYC, LEAST, FIRST, STORE = 0.83e-3, 64, 1.0, 0.62 / 24
+LOADS = {"ldg": 1.45, "ldx": 2.0, "ldx2": 2.6, "ldw": 5.6, "ld2": 6.7}
+PACES = [{"all": 1.0, "tensor": 1.3, "gather": 1.5, "scatter": 3.0, "wake": 0.17, "issue": 0.15, "start": 1.3, "far": (0.42, 0.2), "near": (0.42, 0.2), "scale": 1.0},
+         {"all": 1.2, "tensor": 1.5, "gather": 1.6, "scatter": 3.8, "wake": 0.15, "issue": 0.3, "start": 1.5, "far": (0.95, 0.55), "near": (0.7, 0.35), "scale": 1.2},
+         {"all": 1.4, "tensor": 1.8, "gather": 1.8, "scatter": 4.8, "wake": 0.16, "issue": 0.15, "start": 1.3, "far": (0.55, 0.3), "near": (0.42, 0.2), "scale": 1.35}]
+DUE, FEED = (16.5, 16.2, 15.4, 15.0, 14.2, 13.8), 23.4
+GRAB, TURNS, MENDS, EVEN, HEAT, SEED = 0.3, 4, 4000, 0.5, 0.02, 1
+
+
+def cyc(n):
+    return max(LEAST, n) * CYC
+
+
+def layout(r):
+    at, col = {}, 0
+    mine = [grp for grp in TOGETHER[r] if r in grp][0]
+    singles = [grp[0] for grp in TOGETHER[r] if len(grp) == 1 and grp != mine]
+    for tile in (("q0",), ("q1",)) + RUNS:
+        col += HALF if tile[0] in ("q0", "q1") else max(128, CK * len(tile))
+        for i, t in enumerate(tile):
+            at["x", t] = col - (HALF if t in ("q0", "q1") else CK * (len(tile) - i))
+        if tile[-1] == SERVED[r].index(r) and len(mine) > 1:
+            for s in mine[1:]:
+                at["xl", s] = col
+                col += CK
+        elif singles:
+            at["xl", singles[0]], at["xpad", singles[0]] = col, tile[-1]
+            singles.pop(0)
+            col += CK
+    for s in [s for grp in TOGETHER[r] if len(grp) > 1 and grp != mine for s in grp]:
+        at["xl", s] = col
+        col += CK
+    col = o = 0
+    singles = [grp[0] for grp in UNPACKED[r] if len(grp) == 1 and grp != [r]]
+    for j, grp in enumerate(TOGETHER[r]):
+        sides = [singles.pop(0) for _ in range(2) if singles]
+        for e in sides[:1]:
+            at["rl", e], at["rpad", e], at["first", e] = col, j, True
+            col += CK
+        at["r", j], at["rt", j] = col, o
+        col, o = col + max(128, CK * len(grp)), o + max(128, CK * len(grp))
+        for i, s in enumerate(grp):
+            at["rc", s] = col - CK * (len(grp) - i)
+        for e in sides[1:]:
+            at["rl", e], at["rpad", e] = col, j
+            col += CK
+    for e in [e for grp in UNPACKED[r] if len(grp) > 1 for e in grp]:
+        at["rl", e] = col
+        col += CK
+    at["rl", r] = at["rc", r]
+    return at
+
+
+def graph(me, cores, topo, T, g):
+    core = cores[me]
+    at = layout(me)
+    order = SERVED[me]
+    idx = {e: i for i, e in enumerate(order)}
+    tasks, part = [], [0]
+    V, A, TE = g.vector, g.scalar, g.tensor
+    R1, R2 = ROUNDS
+
+    def flat(deps):
+        out = []
+        for d in deps:
+            if isinstance(d, list):
+                out.extend(flat(d))
+            elif d is not None:
+                out.append(d)
+        return out
+
+    def add(q, cost, call, *deps, **more):
+        tasks.append(dict(q=q, part=part[0], cost=cost if isinstance(cost, tuple) else (cost, 0, 0), call=call, deps=flat(list(deps)), **more))
+        return len(tasks) - 1
+
+    def vec(n, call, *deps):
+        return add("v", cyc(n), lambda q, b: call(), *deps)
+
+    def act(n, call, *deps):
+        return add("a", cyc(n), lambda q, b: call(), *deps)
+
+    def pool(fixed, n, call, *deps):
+        return add("p", fixed + 2 * n * CYC, lambda q, b: call(), *deps)
+
+    def copy(q, out, in_):
+        return A.activation(out, in_, AF.Copy) if q == "a" else V.tensor_copy(out, in_)
+
+    def picked(n):
+        return (0.055, n, 0)
+
+    def strewn(n):
+        return (0.05, 0, n)
+
+    def pack(src, lo, n, qc, qs, there, *deps):
+        return add("v", 0.012 + 0.88e-3 * n, lambda q, b: V.quantize_mx(T[qc][:, there:there + n], T[qs][:, there:there + n], T[src][:, lo:lo + 4 * n]), *deps)
+
+    def load(q, sem, out, in_, behind=None, *deps):
+        return add(q, 0.05, lambda q, b: (g.sync if q == "s" else A).dma_start(out(), in_()), *deps, sem=(sem, 16), lands=LOADS[sem], behind=behind)
+
+    LDX = load("s", "ldx", lambda: T.xsb[:, 0:4 * HALF], lambda: T.x[:, 0:4 * HALF])
+    LDG = load("a", "ldg", lambda: T.wgs[:], lambda: T.wg[:, 0:32])
+    LDX2 = load("s", "ldx2", lambda: T.xsb[:, 4 * HALF:4 * NT], lambda: T.x[:, 4 * HALF:4 * NT], LDX)
+    LDW = load("s", "ldw", lambda: T.w1s[:], lambda: T.w1[:], LDX2, LDX2)
+    LD2 = load("s", "ld2", lambda: T.x2[:, 0:4 * NT - 2], lambda: T.x[:, 2:4 * NT], LDW)
+
+    def iota(name, pattern, n, base=0, lo=0):
+        return pool(0.13, n, lambda: g.iota(T[name][:, lo:lo + n], pattern, base, 0, allow_small_or_imprecise_dtypes=True))
+
+    def zeros(name, lo, n):
+        return iota(name, [[0, n]], n, 0, lo)
+
+    def fill(name, cols, value, n=1, *deps):
+        return vec(n, lambda: V.memset(T[name][:, cols], value), *deps)
+
+    c_pi = pool(0.13, 2, lambda: g.iota(T.pi[:], [[0, 2]], 0, 1))
+    c_k = {"1": iota("k1", [[0, 12], [1, 16]], HALF), "2": iota("k2", [[0, 6], [1, 32]], HALF)}
+    c_tokf = {"1": iota("tokf1", [[1, HALF]], HALF), "2": iota("tokf2", [[32, 6], [1, 16]], CK)}
+    c_im4, c_offmf, c_offwf = iota("im4", [[0, 24], [1, 4]], CK), iota("offmf", [[8, 2]], 2), iota("offwf", [[4, N], [0, 8]], 8 * N)
+    c_slots = iota("slots", [[1, NP]], NP, 1)
+    c_pad, c_aa, c_gg = zeros("xt", 0, 4 * PAD), zeros("aa", 0, 4), zeros("gg", 0, 4)
+    c_win = {"1": [zeros("win1", CK - 16, 16), zeros("win1", HALF, 16)], "2": zeros("win2", CK - 16, 128)}
+    c_pick = {R["k"]: zeros("pick" + R["k"], 0, 16) for R in ROUNDS}
+    c_cl = [zeros("cl", o, NT) for o in (0, NT)]
+
+    c_zero = {"1": [fill("wga1", slice(None), 0.0, 288)], "2": [fill("wga2", slice(o, o + 256), 0.0, 128) for o in (0, 512)]}
+    P3, P15, P31, P16, PM, H1, H2, FT, P14, P2, P1 = range(11)
+
+    def bits(k, m, s):
+        return vec(1, lambda: V.tensor_scalar(T.pci[:, k:k + 1], T.pi[:, 0:1], m, s, OP.bitwise_and, OP.logical_shift_right), c_pi)
+
+    c_pc = vec(8, lambda: V.tensor_copy(T.pc[:, 0:8], T.pci[:, 0:8]),
+               [bits(*x) for x in ((P3, 3, 0), (P15, 15, 0), (P31, 31, 0), (P16, 16, 0), (H1, 16, 4), (H2, 64, 6), (FT, 8, 3), (PM, 15, 2))])
+    c_pc2 = vec(3, lambda: V.tensor_copy(T.pc[:, 8:11], T.pci[:, 8:11]), [bits(*x) for x in ((P14, 14, 1), (P2, 2, 1), (P1, 1, 0))])
+    c_reset4 = fill("reset4", slice(0, 516, 4), 0.0, 65, fill("reset4", slice(None), 1.0, 258))
+
+    def pcol(k):
+        return T.pc[:, k:k + 1]
+
+    c_offw = vec(8 * N, lambda: V.tensor_scalar(T.offw[:], T.offwf[:], pcol(P3), None, OP.add), c_offwf, c_pc)
+
+    SGN, KC, TOK, MB, CV, BIAS, TU, TB, LOW, MA, MC = range(0, 22, 2)
+
+    def two(j):
+        return T.pd[:, j:j + 2]
+
+    def one(j):
+        return T.pd[:, j:j + 1]
+
+    def dcol(j, R):
+        return one(j + ROUNDS.index(R))
+
+    c_mb = act(2, lambda: A.activation(two(MB), T.pc[:, P15:P15 + 2], AF.Copy, scale=-STEP), c_pc)
+    c_sgn = act(2, lambda: A.activation(two(SGN), T.pc[:, H1:H1 + 2], AF.Copy, bias=1.0, scale=-2.0), c_pc)
+    c_kc0 = act(2, lambda: A.activation(two(KC), T.pc[:, H1:H1 + 2], AF.Copy, bias=CK + 1.0, scale=CK - 3.0), c_pc)
+    c_cv = act(2, lambda: A.activation(two(CV), T.pc[:, H1:H1 + 2], AF.Copy, bias=float(HALF), scale=-(CK + 1.0)), c_pc)
+    d = [act(1, lambda: A.activation(one(TOK), pcol(H1), AF.Copy, scale=float(HALF)), c_pc),
+         act(1, lambda: A.activation(one(TOK + 1), pcol(H2), AF.Identity, bias=pcol(P16), scale=float(HALF)), c_pc),
+         act(1, lambda: A.activation(one(TU), pcol(FT), AF.Copy, scale=4.0 * UNIT), c_pc),
+         act(1, lambda: A.activation(one(LOW), pcol(FT), AF.Copy, bias=-BIG, scale=BIG), c_pc)]
+    d = [act(1, lambda: A.activation(one(TB), pcol(FT), AF.Identity, bias=one(LOW), scale=UNIT), d), d]
+    c_bias = act(2, lambda: A.activation(two(BIAS), two(TOK), AF.Identity, bias=one(TB), scale=one(TU)), d)
+    d = [vec(1, lambda: V.tensor_scalar(one(MA), pcol(H1), -224.0, 112.0, OP.mult, OP.add), c_pc),
+         vec(1, lambda: V.tensor_scalar(one(MA + 1), pcol(P14), pcol(P1), 16.0, OP.subtract, OP.mult), c_pc2)]
+    d = [vec(1, lambda: V.tensor_scalar(one(MC), one(MA), pcol(P2), one(MA + 1), OP.mult, OP.add), d),
+         vec(1, lambda: V.tensor_scalar(one(MC + 1), pcol(H1), 96.0, 16.0, OP.mult, OP.add), c_pc)]
+    d = vec(2, lambda: V.tensor_scalar(T.offmf[:], T.offmf[:], one(MC), one(MC + 1), OP.add, OP.add), d, c_offmf)
+    c_offm = vec(2, lambda: V.tensor_scalar(T.offm[:], T.offmf[:], CK + 127.0, None, OP.min), d)
+
+    def gate(R, col, e, n):
+        k = R["k"]
+        return add("va", picked(16 * n), lambda q, b: copy(q, T["wga" + k][:, 4 * col:4 * col + 16 * n], T.wgs[:, 0:32].indirect(T.offw[:, 8 * e:8 * e + n])),
+                   c_offw, LDG, c_zero[k] if R is R1 else None)
+
+    c_reset, c_tok, c_kc = {}, {}, {}
+    c_reset["1"] = act(HALF, lambda: A.activation(T.reset1[:], T.k1[:], AF.Sign), c_k["1"])
+    c_m3 = act(HALF, lambda: A.activation(T.m31[:], T.k1[:], AF.Abs, bias=dcol(MB, R1), scale=STEP), c_k["1"], c_mb)
+    c_rr = act(HALF, lambda: A.activation(T.rr1[:], T.reset1[:], AF.Copy, bias=-BIG, scale=BIG), c_reset["1"])
+    d = act(HALF, lambda: A.activation(T.m32[:], T.k2[:], AF.Abs, bias=dcol(MB, R2), scale=STEP), c_k["2"], c_mb)
+    c_reset["2"] = act(HALF, lambda: A.activation(T.reset2[:], T.m32[:], AF.Sign), d)
+
+    def tokens(R):
+        k, W, ns = R["k"], R["W"], R["NS"]
+        c_tok[k] = act(16 * R["n"], lambda: A.activation(T["tok" + k][:], T["tokf" + k][:], AF.Identity, bias=dcol(BIAS, R), scale=one(TU)), c_tokf[k], c_bias)
+        ends = lambda: T.tokf1[:, W - 1:W * ns:W]
+        c_kc[k] = [act(ns, lambda: A.activation(T["akk" + k][:, 3:4 * ns:4], ends(), AF.Identity, bias=dcol(KC, R), scale=dcol(SGN, R)), c_tokf["1"], c_sgn, c_kc0),
+                   act(ns, lambda: A.activation(T["akm" + k][:, 3:4 * ns:4], ends(), AF.Identity, bias=dcol(SGN, R), scale=0.0), c_tokf["1"], c_sgn,
+                       iota("akm" + k, [[0, ns], [-1, 2], [1, 2]], 4 * ns)),
+                   zeros("akk" + k, 4 * ns - 2, 1) if W * ns == HALF else None]
+
+    tokens(R1)
+    tokens(R2)
+    c_masks = vec(CK, lambda: V.tensor_scalar(T.mk[:], T.im4[:], pcol(PM), 4.0, OP.is_equal, OP.mult), c_im4, c_pc)
+    c_offz = vec(6, lambda: V.tensor_scalar(T.offz[:], T.tokf1[:, 0:HALF:32], pcol(P31), None, OP.add), c_tokf["1"], c_pc)
+    c_scales = vec(4, lambda: V.tensor_scalar(T.mcol[:], T.k1[:, 0:4], pcol(PM), 4.0, OP.is_equal, OP.mult), c_k["1"], c_pc)
+    c_et = pool(0.17, 516, lambda: g.affine_select(T.et[:, 0:515], T.reset4[:, 0:515], [[-1, 515]], OP.is_equal, 0.0, 3, 4), c_reset4)
+    v_qe = [pack("et", 3 - b, 128, "qe", "pe", 128 * b, c_et) for b in range(4)]
+    v_qw = [pack("w1s", 512 * i, 128, "qw", "pw", 128 * i, LDW) for i in range(4)]
+
+    part[0] += 1
+    v_qg = {"1": pack("wga1", 0, R1["G"], "qg1", "pg1", 0, [gate(R1, 16 + 32 * i, order[i], 4) for i in range(4)]),
+            "2": pack("wga2", 0, R2["G"], "qg2", "pg2", 0, [gate(R2, 64 + 32 * i, order[4 + i], 8) for i in (0, 1)], c_zero["2"])}
+    made = {"q0": pack("xsb", 0, HALF, "xc", "xs", at["x", "q0"], LDX), "q1": pack("xsb", 4 * HALF, HALF, "xc", "xs", at["x", "q1"], LDX2)}
+
+    def z(R, other, lo=0, hi=HALF):
+        o = 512 * (R["bank"] + other)
+        return T.pp[:, o + lo:o + hi]
+
+    def score(R, other, h, before):
+        k, s, c = R["k"], R["views"][h], at["x", "q%d" % h]
+        return add("t", (HALF + 16) * CYC, lambda q, b: TE.matmul_mx(z(R, other), T["qg" + k][:, s:s + 128], T["pg" + k][:, s:s + 128],
+                                                                      T.xc[:, c:c + HALF], T.xs[:, c:c + HALF], h == 0, h == 1), v_qg[k], made["q%d" % h], behind=before)
+
+    t_z = {R["k"]: [score(R, b, 1, score(R, b, 0, None)) for b in (0, 1)] for R in ROUNDS}
+    readers = {b: [] for b in range(8)}
+
+    def reads(R, other, t):
+        readers[R["bank"] + other].append(t)
+        return t
+
+    part[0] += 1
+    s1 = R1["W"] * R1["NS"]
+    v_sc = {"1": [], "2": [reads(R2, 0, vec(HALF, lambda: V.transpose(T.sc2[:], z(R2, 0)), t_z["2"][0]))]}
+    tasks[v_sc["2"][0]]["due"] = FEED
+    for lo, hi in ((0, s1), (s1, HALF)):
+        d = reads(R1, 0, vec(hi - lo, lambda lo=lo, hi=hi: V.tensor_tensor(T.md1[:, lo:hi], z(R1, 0, lo, hi), T.m31[:, lo:hi], OP.subtract), t_z["1"][0], c_m3))
+        v_sc["1"].append(vec(hi - lo, lambda lo=lo, hi=hi: V.tensor_tensor_scan(T.sc1[:, lo:hi], T.rr1[:, lo:hi], T.md1[:, lo:hi], 0.0, OP.add, OP.max), d, c_rr))
+
+    def ranks(R):
+        k, W, ns, n = R["k"], R["W"], R["NS"], R["n"]
+        cmp, sc, akk, offr = (lambda lo, hi: T["cmp" + k][:, lo:hi]), (lambda q: T["sc" + k][:, W * q + W - 1:W * q + W]), "akk" + k, "offr" + k
+        d = [reads(R, 0, vec(CK, lambda lo=lo: V.tensor_tensor(T["eqw" + k][:, lo:lo + CK], z(R, 0, lo, lo + CK), T["sc" + k][:, lo:lo + CK], OP.is_equal), v_sc[k], t_z[k][0]))
+             for lo in (0, CK)]
+        tie = vec(CK, lambda: V.tensor_tensor_scan(T["corr" + k][:], T["reset" + k][:], T["eqw" + k][:], 0.0, OP.mult, OP.add), d, c_reset[k])
+        acc = [add("va", cyc(ns), lambda q, b: copy(q, T[akk][:, 0:4 * ns:4], T["corr" + k][:, W - 1:W * ns:W]), tie)]
+        for j in range(ns):
+            c, cut = HALF * j, W * j + W
+            d = reads(R, 1, act(HALF, lambda j=j, c=c: A.activation(cmp(c, c + HALF), z(R, 1), AF.Sign, bias=sc(j), scale=-1.0), t_z[k][1], v_sc[k][0]))
+            acc.append(act(max(cut, LEAST) + 24, lambda j=j, c=c, cut=cut: A.activation(cmp(c, c + cut), cmp(c, c + cut), AF.Relu, accum_out=T[akk][:, 4 * j + 1:4 * j + 2]), d))
+            if cut < HALF:
+                acc.append(act(max(HALF - cut, LEAST) + 24, lambda j=j, c=c, cut=cut: A.activation(cmp(c + cut, c + HALF), cmp(c + cut, c + HALF), AF.Relu, scale=-1.0,
+                                                                                                   accum_out=T[akk][:, 4 * j + 2:4 * j + 3]), d))
+        d = vec(4 * ns, lambda: V.tensor_tensor_scan(T["akq" + k][:, 0:4 * ns], T["akm" + k][:, 0:4 * ns], T[akk][:, 0:4 * ns], 0.0, OP.mult, OP.add), acc, c_kc[k])
+        places = [vec(ns, lambda: V.tensor_copy(T[offr][:, 0:ns], T["akq" + k][:, 3:4 * ns:4]), d)]
+        if ns == n:
+            return places
+        first = vec(n, lambda: V.tensor_scalar(T["first" + k][:], T["corr" + k][:, W - 1:HALF:W], -1.0, -float(CK), OP.mult, OP.add), tie)
+        sums = []
+        for j in range(ns, n):
+            c, cut, o = HALF * j, W * j + W, CK * (j - ns)
+            d = [reads(R, 0, vec(cut, lambda j=j, c=c, cut=cut: V.tensor_scalar(cmp(c, c + cut), z(R, 0, 0, cut), sc(j), None, OP.is_ge), t_z[k][0], v_sc[k][-1]))]
+            if cut < HALF:
+                d.append(reads(R, 0, vec(HALF - cut, lambda j=j, c=c, cut=cut: V.tensor_scalar(cmp(c + cut, c + HALF), z(R, 0, cut, HALF), sc(j), None, OP.is_gt), t_z[k][0], v_sc[k][-1])))
+            sums.append(vec(CK // 2, lambda j=j, c=c, o=o: V.tensor_tensor_scan(T["sums" + k][:, o:o + CK], cmp(c, c + CK), cmp(c + CK, c + HALF), T["first" + k][:, j:j + 1], OP.add, OP.add),
+                            d, first))
+        return places + [vec(n, lambda: V.tensor_scalar(T[offr][:, ns:n], T["sums" + k][:, CK - 1:CK * (n - ns):CK], dcol(SGN, R), dcol(CV, R), OP.mult, OP.add), sums, c_sgn, c_cv)]
+
+    part[0] += 1
+    a_zs = reads(R2, 1, act(HALF, lambda: copy("a", T.zs[:], z(R2, 1)), t_z["2"][1]))
+    v_sin = {"1": reads(R1, 0, vec(HALF, lambda: V.tensor_tensor(T.sin1[:], z(R1, 0), T.tok1[:], OP.max), t_z["1"][0], c_tok["1"])),
+             "2": add("v", picked(CK), lambda q, b: V.tensor_tensor(T.sin2[:], T.zs[:].indirect(T.offz[:]), T.tok2[:], OP.max), a_zs, c_offz, c_tok["2"])}
+
+    def lists(R):
+        k, n, P = R["k"], R["n"], R["P"]
+        win, t1, pair, pick = "win" + k, "t1" + k, "pair" + k, "pick" + k
+        part[0] += 1
+        d = add("v", strewn(16 * n), lambda q, b: V.tensor_copy(T[win][:].indirect(T["offr" + k][:]), T["sin" + k][:]), ranks(R), v_sin[k], c_win[k])
+        part[0] += 1
+        d = [vec(CK, lambda: V.transpose(T[t1][:, 0:CK], T[win][:, CK:2 * CK]), d), vec(128, lambda: V.transpose(T[t1][:, CK:CK + 128], T[win][:, CK - 16:CK + 112]), d)]
+        if R is R1:
+            d = add("v", picked(32), lambda q, b: V.tensor_copy(T[pair][:], T[t1][:].indirect(T.offm[:])), d, c_offm)
+        else:
+            d = add("va", picked(32), lambda q, b: copy(q, T.both[:], T[t1][:].indirect(T.offm[:])), d, c_offm)
+            d = [vec(32, lambda h=h: V.tensor_tensor(T[pair][0:64, 1 - h:32:2], T.both[64 * h:64 * h + 64, 0:32:2], T.both[64 * h:64 * h + 64, 1:32:2], OP.add), d) for h in (0, 1)]
+        d = vec(16, lambda: V.tensor_tensor(T[pick][0:P, 1:16:2], T[pair][0:P, 1:16:2], T[pair][0:P, 0:16:2], OP.is_lt), d, c_pick[k])
+        return vec(16, lambda: V.tensor_tensor_scan(T["s4" + k][0:P, :], T[pick][0:P, :], T[pair][0:P, 16:32], 0.0, OP.mult, OP.max), d)
+
+    off, odd, single = {}, {}, {}
+
+    def spread(R, lo, hi):
+        k, done = R["k"], lists(R)
+        mid = lo + DIRECT[ROUNDS.index(R)]
+
+        def found(i):
+            return T["s4" + k][32 * (i - lo):32 * (i - lo) + 32, 1:12:2]
+
+        for i in range(lo, mid):
+            off[i] = [vec(6, lambda i=i, b=b: V.tensor_scalar(T.offx[32 * b:32 * b + 32, 6 * i:6 * i + 6], found(i), 1.0 / UNIT, -1.0, OP.mult, OP.add), done) for b in range(4)]
+        part[0] += 1
+        if mid < hi:
+            d = [act(6, lambda i=i, b=b: A.activation(T.tokr[32 * b:32 * b + 32, 6 * i:6 * i + 6], found(i), AF.Copy, bias=-1.0, scale=1.0 / UNIT), done)
+                 for i in range(mid, hi) for b in (0, 1)]
+            d = [vec(6, lambda h=h: V.tensor_copy(T.offx[64 * h:64 * h + 64, 6 * mid:6 * hi], T.tokr[0:64, 6 * mid:6 * hi]), d) for h in (0, 1)]
+            for i in range(mid, hi):
+                off[i] = d
+        for a, b in ((lo, mid), (mid, hi)):
+            if a < b:
+                d = vec(6, lambda a=a, b=b: V.tensor_scalar(T.offy[:, 6 * a:6 * b], T.offx[:, 6 * a:6 * b], 1.0, None, OP.add), [off[i] for i in range(a, b)])
+                for i in range(a, b):
+                    odd[i] = d
+        d = vec(6, lambda: V.tensor_scalar(T.off1[:, 6 * lo:6 * hi], T.offx[:, 6 * lo:6 * hi], 0.25, None, OP.mult), [off[i] for i in range(lo, hi)])
+        for i in range(lo, hi):
+            single[order[i]] = d
+
+    spread(R1, 0, 4)
+    spread(R2, 4, N)
+
+    def send(r, names, lo, there, sem, dep, due=None):
+        es = topo.engines(core, cores[r])[-8:]
+        ad = topo.addr(cores[r])
+
+        def call(name, bits):
+            src, dst = T[name][:, lo:lo + CK], T[name][:, there:there + CK]
+            if bits:
+                src, dst = src.bitcast(dt.uint8), dst.bitcast(dt.uint8)
+            return g.remote_dma_fused([RemoteDMATransfer(dst_ids=[DstId(rid=ad[0], pnc=ad[1])], dma_engine_mask=sum(1 << e for e in es), remote_sem=T.sem[sem], src=src, dst=dst)],
+                                      local_sem=T.sem["loc"])
+
+        for name, bits in zip(names, (True, False)):
+            add("p", 0.0, lambda q, b, name=name, bits=bits: call(name, bits), dep, to=(r, sem), engines=es[0],
+                moves=("near" if topo.chip(core) == topo.chip(cores[r]) else "far", 1 - bits), due=due)
+
+    before = c_pad
+    for run in RUNS:
+        part[0] += 1
+        lo, hi = run[0], run[-1] + 1
+        d = [add("va", picked(CK * len(run)), lambda q, b, lo=lo, hi=hi, t=t: copy(q, T.xt[:, 4 * (PAD + CK * lo) + t:4 * (PAD + CK * hi):4],
+                                                                                   T[("xsb", "x2")[t // 2]][:, 0:4 * NT - 2].indirect(T[("offx", "offy")[t % 2]][:, 6 * lo:6 * hi])),
+                 [(off, odd)[t % 2][i] for i in run], LD2 if t > 1 else [LDX, LDX2]) for t in range(4)]
+        skip = PAD if len(run) == 1 else 0
+        t = pack("xt", 4 * (PAD + CK * lo - skip), CK * len(run) + skip, "xc", "xs", at["x", lo] - skip, d, before if skip else None)
+        before = d
+        for i in run:
+            made[i] = t
+            if order[i] != me:
+                send(order[i], ("xc", "xs"), at["x", i], layout(order[i])["xl", me], "x%d" % me, t, DUE[i])
+
+    def products(stat, plane, codes, planes, lo, n, packed, deps):
+        return [add("t", (n + 16) * CYC, lambda q, b, i=i: TE.matmul_mx(T.pp[:, 512 * b:512 * b + n], T[stat][:, 128 * i:128 * i + 128], T[plane][:, 128 * i:128 * i + 128],
+                                                                         T[codes][:, lo:lo + n], T[planes][:, lo:lo + n], True, True), packed[i], deps, bank=True)
+                for i in range(4)]
+
+    def reader(n, call, product):
+        tasks[product]["reader"] = add("va", cyc(n), call, product, of=product)
+        return tasks[product]["reader"]
+
+    results = {}
+    for j, grp in enumerate(TOGETHER[me]):
+        part[0] += 1
+        n = CK * len(grp)
+        skip = max(0, 128 - n)
+        deps = [made[idx[me]] if s == me else ("x%d" % s, 16) for s in grp] + [made[at["xpad", s]] for s in grp if ("xpad", s) in at]
+        lo, o = (at["x", idx[me]] if grp[0] == me else at["xl", grp[0]]) - skip, 4 * at["rt", j]
+
+        def relu(q, b, i, o=o, n=n, skip=skip):
+            out, src = T.rt[:, o + 4 * skip + i:o + 4 * (skip + n):4], T.pp[:, 512 * b + skip:512 * b + skip + n]
+            return A.activation(out, src, AF.Relu, scale=0.05) if q == "a" else V.tensor_scalar(out, src, 0.0, 0.05, OP.max, OP.mult)
+
+        d = [reader(n, lambda q, b, i=i, relu=relu: relu(q, b, i), p) for i, p in enumerate(products("qw", "pw", "xc", "xs", lo, n + skip, v_qw, deps))]
+        results[j] = pack("rt", o, n + skip, "rc", "rs", at["r", j], d, zeros("rt", o, 4 * skip) if skip else None)
+        for s in grp:
+            if s != me:
+                send(s, ("rc", "rs"), at["rc", s], layout(s)["rl", me], "r%d" % me, results[j])
+    own = [j for j, grp in enumerate(TOGETHER[me]) if me in grp][0]
+
+    part[0] = 20
+
+    def table(e, h):
+        return T.cl[:, NT * h:NT * h + NT].indirect(T.off1[:, 6 * idx[e]:6 * idx[e] + 6])
+
+    d, prev = [c_cl[0], c_slots], {}
+    for e in range(LAST):
+        if e:
+            d = prev[e] = add("v", picked(CK), lambda q, b, e=e: V.tensor_tensor(T.cm[:, CK * (e - 1):CK * e], table(e, 0), T.mk[:], OP.mult), d, single[e], c_masks)
+        d = add("v", strewn(CK), lambda q, b, e=e: V.tensor_copy(table(e, 0), T.slots[:, CK * e:CK * e + CK]), d, single[e])
+    part[0] += 1
+    listed = {}
+    for lo, hi in PREVIOUS:
+        s = vec(CK * (hi - lo), lambda lo=lo, hi=hi: V.tensor_tensor_scan(T.cq[:, CK * lo:CK * hi], T.reset4[:, 0:CK * (hi - lo)], T.cm[:, CK * lo:CK * hi], 0.0, OP.mult, OP.add),
+                [prev[e] for e in range(lo + 1, hi + 1)], c_reset4)
+        s = vec(24 * (hi - lo), lambda lo=lo, hi=hi: V.tensor_scalar(T.offc[:, 24 * lo:24 * hi], T.cq[:, CK * lo + 3:CK * hi:4], pcol(P3), None, OP.add), s)
+        for e in range(lo + 1, hi + 1):
+            listed[e] = s
+
+    def by_token(h, d):
+        o = NP + NT * h
+        d = [act(CK, lambda m=m: A.activation(T.cm[:, o + m:o + NT:4], T.cl[:, NT * h + m:NT * h + NT:4], AF.Copy, scale=T.mcol[:, m:m + 1]), d, c_scales) for m in range(4)]
+        d = [vec(128, lambda lo=lo: V.tensor_tensor_scan(T.cq[:, lo:lo + 128], T.reset4[:, 0:128], T.cm[:, lo:lo + 128], 0.0, OP.mult, OP.add), d, c_reset4) for lo in range(o, o + NT, 128)]
+        return vec(CK, lambda: V.tensor_scalar(T.offc[:, o // 4:(o + NT) // 4], T.cq[:, o + 3:o + NT:4], pcol(P3), None, OP.add), d)
+
+    part[0] += 1
+    v_before = by_token(0, d)
+    part[0] += 1
+    v_last = by_token(1, add("v", strewn(CK), lambda q, b: V.tensor_copy(table(LAST, 1), T.slots[:, 0:CK]), c_cl[1], c_slots, single[LAST]))
+
+    def slot(e):
+        return 4 * (1 + CK * e)
+
+    got = {}
+    for grp in UNPACKED[me]:
+        part[0] = 30 + grp[0]
+        n = CK * len(grp)
+        skip = PAD if n == CK and ("first", grp[0]) not in at and (grp != [me] or len(TOGETHER[me][own]) == 1) else 0
+        deps = [results[own] if e == me else ("r%d" % e, 16) for e in grp] + [results[at["rpad", e]] for e in grp if ("rpad", e) in at]
+        name, o = ("gg", 4) if grp == [LAST] else ("aa", slot(grp[0]))
+        d = [reader(n, lambda q, b, i=i, name=name, o=o, n=n, skip=skip: copy(q, T[name][:, o + i:o + 4 * n:4], T.pp[:, 512 * b + skip:512 * b + skip + n]), p)
+             for i, p in enumerate(products("qe", "pe", "rc", "rs", at["rl", grp[0]] - skip, max(n, 128), v_qe, deps))]
+        for e in grp:
+            got[e] = d
+    part[0] = 40
+    chain = [got[0], c_aa]
+    for e in range(1, LAST):
+        chain = add("v", picked(4 * CK), lambda q, b, e=e: V.tensor_tensor(T.aa[:, slot(e):slot(e + 1)], T.aa[:, 0:slot(e)].indirect(T.offc[:, 24 * e - 24:24 * e]),
+                                                                            T.aa[:, slot(e):slot(e + 1)], OP.add), chain, got[e], listed[e])
+
+    lo = 0
+    for n in PIECES:
+        def piece(lo=lo, n=n):
+            return T.yy[:, 16 * lo:16 * (lo + n)]
+
+        def offsets(h, lo=lo, n=n):
+            return T.offc[:, (NP + NT * h) // 4 + lo:(NP + NT * h) // 4 + lo + n]
+
+        d = add("va", picked(16 * n), lambda q, b, piece=piece, offsets=offsets: copy(q, piece(), T.gg[:].indirect(offsets(1))), got[LAST], v_last, c_gg)
+        d = add("v", picked(16 * n), lambda q, b, piece=piece, offsets=offsets: V.tensor_tensor(piece(), T.aa[:].indirect(offsets(0)), piece(), OP.add), chain, v_before, d)
+        add("s", 0.05, lambda q, b, lo=lo, n=n, piece=piece: g.sync.dma_start(T.y[:, 16 * lo:16 * (lo + n)], piece()), d, sem=("sty", 16), engines="y", moves=STORE * n,
+            due=STORE * (NT // 4 - lo - n))
+        lo += n
+    return tasks, readers
+
+
+def slot_in(taken, s, n):
+    i = 0
+    while i < len(taken) and taken[i][1] <= s:
+        i += 1
+    while i < len(taken) and taken[i][0] < s + n - 1e-9:
+        s = max(s, taken[i][1])
+        i += 1
+    taken.insert(i, (s, s + n))
+    return s + n
+
+
+def plan(graphs):
+    key = [(r, i) for r, (tasks, _) in enumerate(graphs) for i in range(len(tasks))]
+    number = {k: j for j, k in enumerate(key)}
+    task = [graphs[r][0][i] for r, i in key]
+    n, paces, lines = len(key), range(len(PACES)), [(r, q) for r in range(N) for q in "vatps"]
+    sent = {}
+    for j, t in enumerate(task):
+        sent.setdefault(t.get("to"), []).append(j)
+    wants = [[x for d in task[j]["deps"] for x in (sent[key[j][0], d[0]] if isinstance(d, tuple) else [number[key[j][0], d]])] for j in range(n)]
+    behind = [None if task[j].get("behind") is None else number[key[j][0], task[j]["behind"]] for j in range(n)]
+    feeds, leads = [[] for j in range(n)], [[] for j in range(n)]
+    for j in range(n):
+        for d in wants[j]:
+            feeds[d].append(j)
+        if behind[j] is not None:
+            leads[behind[j]].append(j)
+    moves = [None if "moves" not in t else [m[t["moves"][0]][t["moves"][1]] if "to" in t else t["moves"] for m in PACES] for t in task]
+    lands, begins = [t.get("lands") for t in task], [m["start"] for m in PACES]
+    lasts = [[m["issue"] if "to" in t else t["cost"][0] * (m["tensor"] if t["q"] == "t" else 1.0 if "moves" in t or "lands" in t else m["all"])
+              + m["all"] * CYC * (t["cost"][1] * m["gather"] + t["cost"][2] * m["scatter"]) for m in PACES] for t in task]
+    wakes, scales = [m["wake"] for m in PACES], [m["scale"] * len(PACES) for m in PACES]
+    lane = [(key[j][0], task[j].get("engines")) for j in range(n)]
+    reader = [number[key[j][0], task[j]["reader"]] if "bank" in task[j] else None for j in range(n)]
+    scores = {(r, b): [number[r, t] for t in graphs[r][1][b]] for r in range(N) for b in range(8)}
+
+    def forwards(ahead):
+        cost, wake = [c[0] for c in lasts], wakes[0]
+        left = [len(wants[j]) + (behind[j] is not None) for j in range(n)]
+        can, free, line = {w: {} for w in lines}, {w: 0.0 for w in lines}, {w: [] for w in lines}
+        end, busy, done, banks, turn = {}, {}, [], dict(scores), [4] * N
+
+        def offer(j, t):
+            for q in task[j]["q"]:
+                can[key[j][0], q][j] = t
+
+        def starts(w):
+            last = banks[w[0], turn[w[0]]] if w[1] == "t" else []
+            bank = max([end.get(t, 1e9) + wake for t in last] + [0.0])
+            return {j: max(t, free[w], 0.0 if reader[j] is None else bank) for j, t in can[w].items()}
+
+        for j in range(n):
+            if not left[j]:
+                offer(j, 0.0)
+        while len(done) < n:
+            now, where = min((min(starts(w).values()), w) for w in lines if can[w])
+            r, q = where
+            c = starts(where)
+            if q == "v":
+                c = {j: t for j, t in c.items() if task[j]["q"] == "v" or free[r, "a"] > t + GRAB * cost[j]}
+                if not c or min(c.values()) > now:
+                    free[where] = min(list(c.values()) + [max(now, free[r, "a"]) + 1e-6])
+                    continue
+            for j in sorted((j for j in c if c[j] <= now), key=lambda j: -ahead[j]):
+                if all(now + cost[j] + ahead[u] <= max(s + ahead[u], s + cost[u] + ahead[j]) + 1e-9 for u, s in c.items() if now < s < now + cost[j] and ahead[u] > ahead[j]):
+                    break
+            else:
+                free[where] = min(s for s in c.values() if s > now)
+                continue
+            for p in task[j]["q"]:
+                del can[r, p][j]
+            line[where].append(j)
+            done.append(j)
+            free[where] = now + cost[j]
+            end[j] = now + cost[j] if lands[j] is None else lands[j]
+            if moves[j] is not None:
+                end[j] = busy[lane[j]] = max(now + begins[0] + (0.0 if r in busy else FIRST), busy.get(lane[j], 0.0)) + moves[j][0]
+                busy[r] = True
+            if reader[j] is not None:
+                banks[r, turn[r]] = [reader[j]]
+                turn[r] = (turn[r] + 1) % 8
+            for u in feeds[j] + leads[j]:
+                left[u] -= 1
+                if not left[u]:
+                    offer(u, max([end[d] + wake for d in wants[u]] + [0.0]))
+        return line, done
+
+    def backwards(done, where):
+        taken, late = {}, [0.0] * n
+        for j in done[::-1]:
+            s = max([task[j].get("due") or 0.0] + [wakes[0] + late[u] for u in feeds[j] + leads[j]])
+            if moves[j] is not None:
+                s = (slot_in(taken.setdefault(lane[j], []), s, moves[j][0]) if where else s + moves[j][0]) + begins[0] - lasts[j][0]
+            late[j] = slot_in(taken.setdefault(where[j], []), s + (lands[j] or 0.0), lasts[j][0]) if where else s + (lands[j] or 0.0) + lasts[j][0]
+        return late
+
+    def run(line):
+        more, extra, left = {}, {}, [len(w) for w in wants]
+        for r in range(N):
+            last, b = {b: scores[r, b] for b in range(8)}, 4
+            for j in line[r, "t"]:
+                if reader[j] is not None:
+                    extra[j] = (b, last[b])
+                    for d in last[b]:
+                        more.setdefault(d, []).append(j)
+                    left[j] += len(last[b])
+                    last[b] = [reader[j]]
+                    b = (b + 1) % 8
+        where, pos = [None] * n, {w: 0 for w in line}
+        for w, l in line.items():
+            for j in l:
+                where[j] = w
+        ready, end, why = [[0.0] * n for p in paces], [[0.0] * n for p in paces], [[None] * n for p in paces]
+        free, busy, seen = {}, {}, [False] * n
+        todo = [l[0] for l in line.values() if l and not left[l[0]]]
+        while todo:
+            j = todo.pop()
+            w = where[j]
+            if behind[j] is not None and not seen[behind[j]]:
+                return None
+            seen[j] = True
+            f, b, held = free.get(w), busy.get(lane[j]), []
+            for p in paces:
+                s = ready[p][j]
+                if f is not None and f[1][p] >= s:
+                    s, why[p][j] = f[1][p], (f[0], True)
+                e = s + lasts[j][p]
+                held.append(e)
+                if moves[j] is not None:
+                    e = s + begins[p] + (0.0 if w[0] in busy else FIRST)
+                    if b is not None and end[p][b] > e:
+                        e, why[p][j] = end[p][b], (b, True)
+                    e += moves[j][p]
+                end[p][j] = e if lands[j] is None else lands[j]
+            if moves[j] is not None:
+                busy[lane[j]] = busy[w[0]] = j
+            free[w] = (j, held)
+            pos[w] += 1
+            if pos[w] < len(line[w]) and not left[line[w][pos[w]]]:
+                todo.append(line[w][pos[w]])
+            for u in feeds[j] + more.get(j, []):
+                for p in paces:
+                    t = end[p][j] + wakes[p]
+                    if t > ready[p][u]:
+                        ready[p][u], why[p][u] = t, (j, False)
+                left[u] -= 1
+                if not left[u] and line[where[u]][pos[where[u]]] == u:
+                    todo.append(u)
+        if not all(seen):
+            return None
+        tails = [[end[p][line[r, "s"][-1]] for r in range(N)] for p in paces]
+        return sum((max(t) + EVEN * sum(t) / N) / scales[p] for p, t in enumerate(tails)) / (1 + EVEN), end, why, where, extra, tails
+
+    left = [len(wants[j]) + (behind[j] is not None) for j in range(n)]
+    done = [j for j in range(n) if not left[j]]
+    for j in done:
+        for u in feeds[j] + leads[j]:
+            left[u] -= 1
+            if not left[u]:
+                done.append(u)
+    top, where = None, None
+    for turn in range(TURNS):
+        line, done = forwards(backwards(done, where))
+        now = run(line)
+        where = now[3]
+        if top is None or now[0] < top[0][0]:
+            top = now, line
+
+    tally, named, names = {}, {}, []
+    for j in range(n):
+        name = (key[j][0], task[j]["part"], task[j]["q"])
+        tally[name] = tally.get(name, 0) + 1
+        names.append(name[1:] + (tally[name],))
+        named[key[j][0], names[j]] = j
+    alike = [[named.get((r, names[j])) for r in range(N)] for j in range(n)]
+    now, line, state = top[0], dict(top[1]), [SEED]
+
+    def draw(m):
+        state[0] = (state[0] * 1103515245 + 12345) % 2 ** 31
+        return state[0] // 64 % m
+
+    for turn in range(MENDS):
+        total, end, why, where, extra, tails = now
+        p = draw(len(PACES))
+        r = max(range(N), key=lambda r: tails[p][r]) if draw(3) else draw(N)
+        j, held = line[r, "s"][-1], []
+        while why[p][j] is not None:
+            i, same = why[p][j]
+            if same and where[i] == where[j] and i not in wants[j]:
+                held.append((i, j))
+            j = i
+        i, j = held[draw(len(held))]
+        kind, far, lag, old = draw(8), draw(4) if draw(2) else 0, 0.1 * draw(4), dict(line)
+        either = [x for x in (0, 1) if len(task[(i, j)[x]]["q"]) > 1]
+        x = either[draw(len(either))] if either else None
+        for i, j in [(i, j)] if draw(3) == 0 else zip(alike[i], alike[j]):
+            if i is None or j is None or where[i] != where[j]:
+                continue
+            w = where[j]
+            l = line[w] = list(line[w])
+            if kind < 2 and either:
+                y, o = (i, j)[x], (w[0], "a" if w[1] == "v" else "v")
+                l.remove(y)
+                m = line[o] = list(line[o])
+                s = max([end[p][d] for d in wants[y]] + [0.0]) + lag
+                m.insert(len([1 for u in m if end[p][u] <= s]), y)
+            elif l.index(i) < l.index(j) and kind < 5:
+                a = l.index(i)
+                l.remove(j)
+                l.insert(max(0, a - far), j)
+            elif l.index(i) < l.index(j):
+                l.remove(i)
+                l.insert(l.index(j) + 1 + far, i)
+        new = run(line)
+        if new is not None and new[0] <= total + HEAT * (1.0 - turn / MENDS) * draw(100) / 100.0:
+            now = new
+            if new[0] < top[0][0]:
+                top = new, dict(line)
+        else:
+            line = old
+    return {w: [key[j][1] for j in l] for w, l in top[1].items()}, {key[j]: (b, [key[d][1] for d in ds]) for j, (b, ds) in top[0][4].items()}, top[0][0]
+
+
+PLANS = {}
 
 
 def rank_program(g, core, T, topo):
@@ -55,601 +711,40 @@ def rank_program(g, core, T, topo):
     if me is None:
         return
     cores = list(T.cores)
-
-    def far_of(r):
-        return [k for k in range(N) if topo.chip(cores[k]) != topo.chip(cores[r])]
-
-    def near_of(r):
-        return [k for k in range(N) if k != r and topo.chip(cores[k]) == topo.chip(cores[r])]
-
-    def coming(r):
-        return COMING[r]
-
-    far, near = far_of(me), near_of(me)
-    order = ORDER[me] or [e for part in (range(4), range(4, N)) for e in far + near + [me] if e in part]
-    idx = {e: i for i, e in enumerate(order)}
-
-    Q = {"v": (g.vector, "sv"), "a": (g.scalar, "sa"), "t": (g.tensor, "sten"), "p": (g, None), "s": (g.sync, None)}
-    count = {"sv": 0, "sa": 0, "sten": 0}
-    seen = {}
-
-    def need(q, deps):
-        for d in deps:
-            if d is not None and seen.get((q, d[0]), 0) < d[1]:
-                Q[q][0].wait_ge(T.sem[d[0]], d[1])
-                seen[(q, d[0])] = d[1]
-
-    def done(q, ins):
-        s = Q[q][1]
-        if q == "p":
-            s = "sp%d" % sum(1 for c in count if c.startswith("sp"))
-            count[s] = 0
-        ins.then_inc(T.sem[s], 1)
-        count[s] += 1
-        return (s, count[s])
-
-    V, A, TE = g.vector, g.scalar, g.tensor
-    R1, R2 = ROUNDS
-
-    g.sync.dma_start(T.xsb[:, 0:4 * HALF], T.x[:, 0:4 * HALF]).then_inc(T.sem["ldx"], 16)
-    g.scalar.dma_start(T.wgs[:], T.wg[:, 0:32]).then_inc(T.sem["ldg"], 16)
-    g.sync.dma_start(T.xsb[:, 4 * HALF:4 * NT], T.x[:, 4 * HALF:4 * NT]).then_inc(T.sem["ldx2"], 16)
-    g.sync.dma_start(T.w1s[:], T.w1[:]).then_inc(T.sem["ldw"], 16)
-    LDX, LDX2, LDG, LDW = ("ldx", 16), ("ldx2", 16), ("ldg", 16), ("ldw", 16)
-
-    def iota(name, pattern, base=0):
-        return done("p", g.iota(T[name][:], pattern, base, 0, allow_small_or_imprecise_dtypes=True))
-
-    c_pi = done("p", g.iota(T.pi[:], [[0, 2]], 0, 1))
-    c_k = {"1": iota("k1", [[0, 12], [1, 16]])}
-    c_tokf = {"1": iota("tokf1", [[1, HALF]])}
-    c_k["2"] = iota("k2", [[0, 6], [1, 32]])
-    c_im4 = iota("im4", [[0, 6], [1, 4], [0, 4]])
-    c_tokf["2"] = iota("tokf2", [[32, 6], [1, 16]])
-
-    c_zero = {"1": done("v", V.memset(T.wga1[:], 0.0))}
-    for i in range(4):
-        done("v", V.memset(T.offwf[:, 4 * i:4 * i + 4], float(4 * order[i])))
-    P3, P15, P31, P16, PM, H1, H2 = range(7)
-    need("v", [c_pi])
-    for k, m in enumerate((3, 15, 31, 16)):
-        done("v", V.tensor_scalar(T.pci[:, k:k + 1], T.pi[:, 0:1], m, None, OP.bitwise_and))
-    for k, m, s in ((PM, 15, 2), (H1, 16, 4), (H2, 64, 6)):
-        d = done("v", V.tensor_scalar(T.pci[:, k:k + 1], T.pi[:, 0:1], m, s, OP.bitwise_and, OP.logical_shift_right))
-    for i in (4, 5):
-        c_offwf = done("v", V.memset(T.offwf[:, 8 * i - 16:8 * i - 8], float(4 * order[i])))
-    need("v", [d])
-    c_pc = done("v", V.tensor_copy(T.pc[:, 0:7], T.pci[:, 0:7]))
-    c_ones = done("v", V.memset(T.reset4[:], 1.0))
-
-    def pcol(k, lo=0, hi=128):
-        return T.pc[lo:hi, k:k + 1]
-
-    need("v", [c_offwf, c_pc])
-    c_offw = done("v", V.tensor_scalar(T.offw[:], T.offwf[:], pcol(P3), None, OP.add))
-    need("v", [c_ones])
-    c_ones = c_reset4 = done("v", V.memset(T.reset4[:, 0:516:4], 0.0))
-    c_zero["2"] = None
-
-    SGN, KC, TOK, MB, CV = 0, 2, 4, 6, 8
-    need("a", [c_pc])
-    done("a", A.activation(T.pd[:, MB:MB + 2], T.pc[:, P15:P15 + 2], AF.Copy, scale=-STEP))
-    done("a", A.activation(T.pd[:, SGN:SGN + 2], T.pc[:, H1:H1 + 2], AF.Copy, bias=1.0, scale=-2.0))
-    done("a", A.activation(T.pd[:, KC:KC + 2], T.pc[:, H1:H1 + 2], AF.Copy, bias=CK + 1.0, scale=CK - 3.0))
-    done("a", A.activation(T.pd[:, TOK:TOK + 1], pcol(H1), AF.Copy, scale=float(HALF)))
-    done("a", A.activation(T.pd[:, TOK + 1:TOK + 2], pcol(H2), AF.Identity, bias=pcol(P16), scale=float(HALF)))
-    c_pd = done("a", A.activation(T.pd[:, CV:CV + 1], pcol(H1), AF.Copy, bias=float(HALF), scale=-(CK + 1.0)))
-
-    def dcol(j, R):
-        j += ROUNDS.index(R)
-        return T.pd[:, j:j + 1]
-
-    def copy(q, out, in_):
-        return done(q, A.activation(out, in_, AF.Copy) if q == "a" else V.tensor_copy(out, in_))
-
-    def gate(q, R, col, lo, n):
-        k = R["k"]
-        need(q, [c_offw, LDG, c_zero[k]])
-        return copy(q, T["wga" + k][:, 4 * col:4 * col + 16 * n], T.wgs[:, 0:32].indirect(T.offw[:, lo:lo + n]))
-
-    c_reset, c_rr, c_m3, c_tok, c_kc = {}, {}, {}, {}, {}
-
-    def windows(R):
-        k = R["k"]
-        need("a", [c_k[k], c_pd])
-        if R is R2:
-            d = done("a", A.activation(T.m32[:], T.k2[:], AF.Abs, bias=dcol(MB, R), scale=STEP))
-            need("a", [d])
-            c_reset[k] = done("a", A.activation(T.reset2[:], T.m32[:], AF.Sign))
-            return
-        c_reset[k] = done("a", A.activation(T["reset" + k][:], T["k" + k][:], AF.Sign))
-        c_m3[k] = done("a", A.activation(T["m3" + k][:], T["k" + k][:], AF.Abs, bias=dcol(MB, R), scale=STEP))
-        need("a", [c_reset[k]])
-        c_rr[k] = done("a", A.activation(T["rr" + k][:], T["reset" + k][:], AF.Copy, bias=-BIG, scale=BIG))
-
-    def tokens(R):
-        k, W, ns = R["k"], R["W"], R["NS"]
-        o = 0 if R is R1 else 4 * R1["NS"]
-        need("a", [c_tokf[k], c_tokf["1"], c_pd])
-        c_tok[k] = done("a", A.activation(T["tok" + k][:], T["tokf" + k][:], AF.Identity, bias=dcol(TOK, R)))
-        ends = T.tokf1[:, W - 1:W * ns:W]
-        done("a", A.activation(T["akk" + k][:, 3:4 * ns:4], ends, AF.Identity, bias=dcol(KC, R), scale=dcol(SGN, R)))
-        c_kc[k] = done("a", A.activation(T.akm[:, o + 3:o + 4 * ns:4], ends, AF.Identity, bias=dcol(SGN, R), scale=0.0))
-
-    a_g1 = [gate("a", R1, 16 + 32 * i, 4 * i, 4) for i in (2, 3)][-1]
-    windows(R1)
-    a_g2 = [gate("a", R2, 64 + 32 * i, 16 + 8 * i, 8) for i in (0, 1)][-1]
-    tokens(R1)
-    windows(R2)
-
-    v_g1 = [gate("v", R1, 16 + 32 * i, 4 * i, 4) for i in (0, 1)][-1]
-    d = [done("v", V.memset(T.wga2[:, o:o + 256], 0.0)) for o in (0, 512)][-1]
-    need("v", [v_g1, a_g1])
-    done("v", V.quantize_mx(T.qg1[:], T.pg1[:], T.wga1[:]))
-    need("v", [LDX])
-    v_qx0 = done("v", V.quantize_mx(T.qx[:, 0:HALF], T.px[:, 0:HALF], T.xsb[:, 0:4 * HALF]))
-    c_akm = [done("v", V.memset(T.akm[:, j:44:4], c)) for j, c in enumerate((0.0, 1.0, -1.0))][-1]
-    need("v", [LDX2])
-    v_qx1 = done("v", V.quantize_mx(T.qx[:, HALF:NT], T.px[:, HALF:NT], T.xsb[:, 4 * HALF:4 * NT]))
-    need("v", [a_g2, d])
-    v_qg2 = done("v", V.quantize_mx(T.qg2[:], T.pg2[:], T.wga2[:]))
-    need("v", [c_im4, c_k["1"]])
-    c_masks = done("v", V.tensor_scalar(T.mk[:], T.im4[:], pcol(PM), 4.0, OP.is_equal, OP.mult))
-    t_z = {}
-
-    def z(R, other, lo=0, hi=HALF):
-        o = 512 * (R["bank"] + other)
-        return T.pp[:, o + lo:o + hi]
-
-    for R, deps in ((R1, (v_qx0, v_qx1)), (R2, (v_qg2, v_qg2))):
-        k = R["k"]
-        for h in (0, 1):
-            need("t", [deps[h]])
-            s, c = slice(R["views"][h], R["views"][h] + 128), slice(HALF * h, HALF * h + HALF)
-            t_z[k] = [done("t", TE.matmul_mx(z(R, b), T["qg" + k][:, s], T["pg" + k][:, s], T.qx[:, c], T.px[:, c], h == 0, h == 1)) for b in (0, 1)]
-
-    need("p", [c_ones])
-    c_et = [done("p", g.affine_select(T.et[:, 512 * b:512 * b + 512], T.reset4[:, o:o + 512], [[-1, 512]], OP.is_equal, 0.0, b, 4)) for b, o in enumerate((2, 0, 0, 0))]
-
-    def zeros(ap, n):
-        return done("p", g.iota(ap, [[0, n]], 0, 0, allow_small_or_imprecise_dtypes=True))
-
-    c_pad, c_last = zeros(T.xt[:, 0:4 * PAD], 4 * PAD), zeros(T.akk2[:, 22:23], 1)
-    c_win = [zeros(T.win2[:, o + CK:o + 2 * CK], CK) for o in (0, WIN)]
-    c_slots = iota("slots", [[16, 36], [1, 4], [4, 4]], 1)
-    c_rt, c_aa = zeros(T.rt[:, 0:4 * PAD], 4 * PAD), zeros(T.aa[:, 0:4], 4)
-
-    v_md, v_sc = {}, {}
-
-    def own_mask(R, lo, hi):
-        k = R["k"]
-        need("v", [t_z[k][0], c_m3[k]])
-        v_md[k, lo] = done("v", V.tensor_tensor(T["md" + k][:, lo:hi], z(R, 0, lo, hi), T["m3" + k][:, lo:hi], OP.subtract))
-
-    def own_scan(R, lo, hi):
-        k = R["k"]
-        need("v", [v_md[k, lo], c_rr[k]])
-        v_sc[k, lo] = done("v", V.tensor_tensor_scan(T["sc" + k][:, lo:hi], T["rr" + k][:, lo:hi], T["md" + k][:, lo:hi], 0.0, OP.add, OP.max))
-
-    v_tie = {}
-
-    def equal(R, lo, hi):
-        k = R["k"]
-        need("v", [d for (j, _), d in v_sc.items() if j == k])
-        v_tie[k] = done("v", V.tensor_tensor(T["eqw" + k][:, lo:hi], z(R, 0, lo, hi), T["sc" + k][:, lo:hi], OP.is_equal))
-
-    def ties(R):
-        k = R["k"]
-        need("v", [v_tie[k], c_reset[k]])
-        v_tie[k] = done("v", V.tensor_tensor_scan(T["corr" + k][:], T["reset" + k][:], T["eqw" + k][:], 0.0, OP.mult, OP.add))
-
-    def ties_out(R):
-        k, W, ns = R["k"], R["W"], R["NS"]
-        need("v", [v_tie[k]])
-        v_tie[k] = copy("v", T["akk" + k][:, 0:4 * ns:4], T["corr" + k][:, W - 1:W * ns:W])
-
-    a_acc, a_zs = {}, {}
-
-    def scores_out(R):
-        k = R["k"]
-        need("a", [t_z[k][1]])
-        a_zs[k] = copy("a", T["zs" + k][:], z(R, 1))
-
-    def scalar_ranks(R):
-        k, W, ns = R["k"], R["W"], R["NS"]
-        need("a", [t_z[k][1], v_sc[k, 0]])
-        cmp, akk, signs = T["cmp" + k], T["akk" + k], []
-        for q in range(ns + 1):
-            if q < ns:
-                signs.append(done("a", A.activation(cmp[:, HALF * q:HALF * q + HALF], z(R, 1), AF.Sign, bias=T["sc" + k][:, W * q + W - 1:W * q + W], scale=-1.0)))
-            if q:
-                j, c = q - 1, HALF * (q - 1)
-                lower = cmp[:, c:c + W * q]
-                need("a", [signs[j]])
-                a_acc[k] = done("a", A.activation(lower, lower, AF.Relu, accum_out=akk[:, 4 * j + 1:4 * j + 2]))
-                if W * q < HALF:
-                    higher = cmp[:, c + W * q:c + HALF]
-                    a_acc[k] = done("a", A.activation(higher, higher, AF.Relu, scale=-1.0, accum_out=akk[:, 4 * j + 2:4 * j + 3]))
-
-    def scalar_places(R, fill):
-        k, ns = R["k"], R["NS"]
-        o = 0 if R is R1 else 4 * R1["NS"]
-        need("v", [a_acc[k], v_tie[k], c_kc[k], c_akm])
-        d = done("v", V.tensor_tensor_scan(T["akq" + k][:], T.akm[:, o:o + 4 * ns], T["akk" + k][:], 0.0, OP.mult, OP.add))
-        fill()
-        need("v", [d])
-        return copy("v", T["offr" + k][:, 0:ns], T["akq" + k][:, 3:4 * ns:4])
-
-    def vector_ranks(R, steps):
-        k, W, ns, n = R["k"], R["W"], R["NS"], R["n"]
-        cmp, sc = T["cmp" + k], T["sc" + k]
-        late = []
-
-        def total():
-            q, d = late.pop(0)
-            o, c = CK * (q - ns), HALF * q
-            need("v", [d])
-            return done("v", V.tensor_tensor_scan(T.sums[:, o:o + CK], cmp[:, c:c + CK], cmp[:, c + CK:c + HALF], T.first[:, q:q + 1], OP.add, OP.add))
-
-        equal(R, 0, HALF)
-        for q in range(ns, n):
-            s = sc[:, W * q + W - 1:W * q + W]
-            cut, c = W * q + W, HALF * q
-            d = done("v", V.tensor_scalar(cmp[:, c:c + cut], z(R, 0, 0, cut), s, None, OP.is_ge))
-            if cut < HALF:
-                d = done("v", V.tensor_scalar(cmp[:, c + cut:c + HALF], z(R, 0, cut, HALF), s, None, OP.is_gt))
-            late.append((q, d))
-            if q == ns:
-                ties(R)
-            elif q == ns + 1:
-                need("v", [v_tie[k]])
-                done("v", V.tensor_scalar(T.first[:], T["corr" + k][:, W - 1:HALF:W], -1.0, -float(CK), OP.mult, OP.add))
-                ties_out(R)
-            else:
-                need("v", [v_tie[k]])
-                total()
-        total()
-        v_sum = total()
-
-        def places():
-            steps[0]()
-            need("v", [v_sum, c_pd])
-            done("v", V.tensor_scalar(T["offr" + k][:, ns:n], T.sums[:, CK - 1:CK * (n - ns):CK], dcol(SGN, R), T.pd[:, CV:CV + 1], OP.mult, OP.add))
-        return scalar_places(R, places)
-
-    off = {}
-
-    def lists(R, v_offr, scores, deps, fill):
-        k, n, P = R["k"], R["n"], R["P"]
-        win, t1, pick, offr = T["win" + k], T["t1" + k], T["pick" + k], T["offr" + k]
-        fill()
-        need("v", [v_offr, c_tok[k]] + deps)
-        e = copy("v", win[:, WIN:2 * WIN].indirect(offr[:, 0:n]), T["tok" + k][:])
-        if R is R2:
-            fill()
-        d = copy("v", win[:, 0:WIN].indirect(offr[:, 0:n]), scores)
-        need("v", [e])
-        e = done("v", V.transpose(t1[:, CK:2 * CK], win[:, WIN + CK:WIN + 2 * CK]))
-        need("v", [d])
-        d = done("v", V.transpose(t1[:, 0:CK], win[:, CK:2 * CK]))
-        if R is R1:
-            src, step, other = t1, 32, 16
-        else:
-            fill()
-            need("v", [d])
-            for h in (0, 1):
-                d = e = done("v", V.tensor_tensor(T.s6[0:64, 6 * h:6 * h + 6], t1[64 * h:64 * h + 64, 0:2 * CK:32], t1[64 * h:64 * h + 64, 16:2 * CK:32], OP.add))
-            fill()
-            src, step, other = T.s6, 1, 6
-        need("v", [e])
-        o = 3 * step
-        d = done("v", V.tensor_tensor(pick[0:P, 3:6], src[0:P, o:2 * o:step], src[0:P, o + other:2 * o + other - step + 1:step], OP.subtract))
-        fill()
-        need("v", [d])
-        picks = []
-        for u in range(3):
-            c = u * step
-            picks.append(done("v", V.tensor_scalar(pick[0:P, 6 + u:7 + u], src[0:P, c:c + 1], src[0:P, c + other:c + other + 1], pick[0:P, 3 + u:4 + u], OP.is_lt, OP.mult)))
-        for u in range(3):
-            c = o + u * step
-            need("v", [picks[u]])
-            d = done("v", V.tensor_scalar(T["wa" + k][0:P, 32 * u:32 * u + 32], T.mask4[0:P, :], src[0:P, c:c + 1], pick[0:P, 6 + u:7 + u], OP.add, OP.subtract))
-        fill()
-        need("v", [d])
-        d = done("v", V.transpose(T["t2" + k][0:P, :], T["wa" + k][0:P, :]))
-        fill()
-        need("v", [d, c_rr4])
-        d = done("v", V.tensor_tensor_scan(T["s4" + k][0:P, :], T.rr4[0:P, :], T["t2" + k][0:P, :], 0.0, OP.add, OP.max))
-        off["list"] = d
-        if R is R1:
-            fill()
-            need("v", [d])
-
-    def spread(lo, hi):
-        need("a", [off["list"]])
-        for i in range(lo, hi):
-            k, block = ("1", i) if i < 4 else ("2", i - 4)
-            for b in (0, 1):
-                d = copy("a", T.tokr[32 * b:32 * b + 32, 24 * i:24 * i + 24], T["s4" + k][32 * block:32 * block + 32, 3:CK:4])
-        need("a", [d])
-        off["spread"] = copy("a", T.tokr[64:128, 24 * lo:24 * hi], T.tokr[0:64, 24 * lo:24 * hi])
-
-    def offsets(lo, hi):
-        need("v", [off["spread"]])
-        d = done("v", V.tensor_scalar(T.off4[:, 24 * lo:24 * hi], T.tokr[:, 24 * lo:24 * hi], 4.0, pcol(P3), OP.mult, OP.add))
-        for i in range(lo, hi):
-            off[i] = d
-
-    def gather(q, lo, hi):
-        need(q, [off[lo // 24], LDX, LDX2])
-        return copy(q, T.xt[:, 4 * PAD + 16 * lo:4 * PAD + 16 * hi], T.xsb[:, 0:4 * NT].indirect(T.off4[:, lo:hi]))
-
-    def pack(src, lo, n, qc, qs, there, deps):
-        need("v", deps)
-        return done("v", V.quantize_mx(T[qc][:, there:there + n], T[qs][:, there:there + n], T[src][:, 4 * lo:4 * (lo + n)]))
-
-    local = [0]
-    tk = {"last": None, "step": 0}
-
-    def transfer(r, es, bits, src, lo, dst, there, rsem):
-        src, dst = T[src][:, lo:lo + CK], T[dst][:, there:there + CK]
-        if bits:
-            src, dst = src.bitcast(dt.uint8), dst.bitcast(dt.uint8)
-        ad = topo.addr(cores[r])
-        local[0] += len(es)
-        return RemoteDMATransfer(dst_ids=[DstId(rid=ad[0], pnc=ad[1])], dma_engine_mask=sum(1 << k for k in es), remote_sem=T.sem[rsem], src=src, dst=dst)
-
-    def dispatch(i, deps):
-        r = order[i]
-        d = pack("xt", CK * i, 128, "ct", "cs", 128 * i, deps)
-        if r == me:
-            tk["codes"] = d
-            return
-        isfar = r in far
-        there = (far_of(r)[::-1 if BACKWARD[r] else 1] if isfar else near_of(r)).index(me) * CK
-        need("p", [d])
-        for bits, src, dst in ((True, "ct", "rxf" if isfar else "rxn"), (False, "cs", "rxfs" if isfar else "rxns")):
-            g.remote_dma_fused([transfer(r, topo.engines(core, cores[r])[-8:], bits, src, 128 * i + PAD, dst, there, "df" if isfar else "dn")], local_sem=T.sem["loc"])
-
-    def answer(ranks, lo, dep):
-        need("p", [dep])
-        n = len(ranks)
-        for bits, name in ((True, "rc"), (False, "rs")):
-            g.remote_dma_fused([transfer(r, topo.engines(core, cores[r])[-8:][i::n], bits, name, lo + CK * i, name, LAND0 + CK * coming(r).index(me), "r%d" % me)
-                                for i, r in enumerate(ranks)], local_sem=T.sem["loc"])
-
-    def qweight(i):
-        return pack("w1s", 128 * i, 128, "qw", "pw", 128 * i, [LDW])
-
-    def qunpack(i):
-        return pack("et", 128 * i, 128, "qe", "pe", 128 * i, [c_et[i]])
-
-    def filler(steps):
-        steps = list(steps)
-
-        def fill(n=1):
-            for _ in range(min(n, len(steps))):
-                steps.pop(0)()
-        return fill
-
-    s1 = R1["W"] * R1["NS"]
-    own_mask(R1, 0, s1)
-    own_mask(R1, s1, HALF)
-    own_scan(R1, 0, s1)
-    own_scan(R1, s1, HALF)
-    scores_out(R1)
-    scalar_ranks(R1)
-
-    def own_turned():
-        need("v", [t_z["2"][0]])
-        v_sc["2", 0] = done("v", V.transpose(T.sc2[:], z(R2, 0)))
-
-    v_offr = vector_ranks(R1, [own_turned])
-    scores_out(R2)
-    tokens(R2)
-    need("a", [c_reset4])
-    c_rr4 = done("a", A.activation(T.rr4[:], T.reset4[:, 0:CK], AF.Copy, bias=-BIG, scale=BIG))
-    c_cl = [done("a", A.activation(T.cl[:, NP + o:NP + o + HALF], T.k1[:], AF.Copy, scale=0.0)) for o in (0, HALF)][-1]
-    later = {}
-
-    scalar_ranks(R2)
-
-    def window_offsets():
-        done("v", V.tensor_scalar(T.mask4[:], T.im4[:, 0:32], pcol(P3), -BIG, OP.not_equal, OP.mult))
-        need("v", [c_tokf["1"]])
-        later["offz"] = done("v", V.tensor_scalar(T.offz[:], T.tokf1[:, 0:HALF:32], pcol(P31), None, OP.add))
-
-    def scales():
-        done("v", V.tensor_scalar(T.mcol[:, 0:4], T.k1[:, 0:4], pcol(PM), 4.0, OP.is_equal, OP.mult))
-        later["scales"] = done("v", V.tensor_scalar(T.mcol[:, 4:8], T.k1[:, 0:4], pcol(P3), None, OP.is_equal))
-
-    fill = filler([window_offsets, lambda: equal(R2, 0, CK), lambda: equal(R2, CK, HALF), lambda: ties(R2), scales, lambda: ties_out(R2)])
-    lists(R1, v_offr, T.zs1[:], [a_zs["1"]], fill)
-    for b in range(4):
-        off[0] = done("v", V.tensor_scalar(T.off4[32 * b:32 * b + 32, 0:24], T.s41[0:32, 3:CK:4], 4.0, pcol(P3, 32 * b, 32 * b + 32), OP.mult, OP.add))
-    need("a", [later["offz"], a_zs["2"]])
-    a_zc = copy("a", T.zc[:], T.zs2[:].indirect(T.offz[:]))
-    a_x = [gather("a", 0, 12)]
-    fill()
-    v_x = gather("v", 12, 24)
-    spread(0, 4)
-    fill(8)
-    dispatch(0, [a_x[0], v_x, c_pad])
-
-    def other_gathers():
-        offsets(1, 4)
-        a_x.extend(gather("a", 24 * i, 24 * i + 24) for i in (1, 2, 3))
-
-    def singles(lo, hi):
-        need("a", [off["spread"], later["scales"]])
-        for m in range(4):
-            tk["one"] = done("a", A.activation(T.one[:, 24 * lo + m:24 * hi:4], T.tokr[:, 24 * lo + m:24 * hi:4], AF.Copy, scale=T.mcol[:, 4 + m:5 + m]))
-
-    def singles_sum(lo, hi):
-        need("v", [tk["one"], c_reset4])
-        tk["one"] = done("v", V.tensor_tensor_scan(T.one[:, 24 * (N + lo):24 * (N + hi)], T.reset4[:, 0:24 * (hi - lo)], T.one[:, 24 * lo:24 * hi], 0.0, OP.mult, OP.add))
-
-    def singles_out(lo, hi):
-        need("v", [tk["one"]])
-        d = copy("v", T.off16[:, 6 * lo:6 * hi], T.one[:, 24 * (N + lo) + 3:24 * (N + hi):4])
-        for i in range(lo, hi):
-            tk["single", i] = d
-
-    singles(0, 4)
-
-    v_qw = []
-    weights = [lambda i=i: v_qw.append(qweight(i)) for i in range(4)]
-    sends = [lambda i=i: dispatch(i, [a_x[i]]) for i in range(N)]
-    steps = {"g": other_gathers, "u": lambda: qunpack(0), "v": lambda: qunpack(1), "w": lambda: qunpack(2), "1": sends[1], "2": sends[2], "3": sends[3],
-             "a": weights[0], "b": weights[1], "c": weights[2], "d": weights[3], "s": lambda: singles_sum(0, 4), "t": lambda: singles_out(0, 4)}
-    fill = filler([steps[s] for s in SECOND])
-    need("v", [c_last])
-    v_offr = scalar_places(R2, fill)
-    lists(R2, v_offr, T.zc[:], [a_zc] + c_win, fill)
-    spread(4, 6)
-    fill(8)
-
-    free = {0: [a_acc["2"], v_tie["2"]], 4: []}
-
-    def products(stat, plane, codes, planes, lo, n, bank, deps):
-        need("t", deps + free[bank])
-        r = []
-        for i in range(4):
-            c = slice(128 * i, 128 * i + 128)
-            o = 512 * (bank + i)
-            r.append(done("t", TE.matmul_mx(T.pp[:, o:o + n], T[stat][:, c], T[plane][:, c], T[codes][:, lo:lo + n], T[planes][:, lo:lo + n], True, True)))
-        return r
-
-    def relus(lo, n, bank, col, deps, both):
-        last = {}
-        for i in range(4):
-            q = "v" if both and i % 2 == 0 else "a"
-            need(q, [deps[i]])
-            o = 512 * (bank + i) + col
-            out, src = T.rt[:, 4 * lo + i:4 * (lo + n):4], T.pp[:, o:o + n]
-            last[q] = done(q, A.activation(out, src, AF.Relu, scale=0.05) if q == "a" else V.tensor_scalar(out, src, 0.0, 0.05, OP.max, OP.mult))
-        free[bank] = list(last.values())
-        return free[bank]
-
-    def slot(e):
-        return 4 * (1 + CK * e)
-
-    def unpack(e, bank, deps):
-        for b in range(4):
-            need("a", [deps[b]])
-            o = 512 * (bank + b) + PAD
-            d = copy("a", T.aa[:, slot(e) + b:slot(e) + 4 * CK:4], T.pp[:, o:o + CK])
-        free[bank] = got[e] = [d]
-
-    table = T.cl[:, NP:NP + NT]
-    got = {}
-
-    def tab():
-        k = tk["step"]
-        tk["step"] += 1
-        e = (k + 1) // 2
-        o16 = T.off16[:, 6 * idx[e]:6 * idx[e] + 6]
-        need("v", [tk["last"], tk["single", idx[e]], c_cl, c_slots])
-        if k % 2:
-            tk["last"] = tk["prev"] = done("v", V.tensor_tensor(T.cm[:, CK * (e - 1):CK * e], table.indirect(o16), T.mk[:], OP.mult))
-        else:
-            tk["last"] = copy("v", table.indirect(o16), T.slots[:, CK * e:CK * e + CK])
-
-    def previous(lo, hi):
-        need("v", [tk["prev"]])
-        sums = [done("v", V.tensor_tensor_scan(T.cq[:, CK * lo + b:CK * hi:4], T.reset4[:, 0:24 * (hi - lo)], T.cm[:, CK * lo + b:CK * hi:4], 0.0, OP.mult, OP.add)) for b in range(4)]
-        for b in range(4):
-            need("v", [sums[b]])
-            d = done("v", V.tensor_scalar(T.offc[:, 24 * lo + b:24 * hi:4], T.cq[:, CK * lo + 12 + b:CK * hi:16], pcol(P3), None, OP.add))
-        for e in range(lo + 1, hi + 1):
-            tk["list", e] = d
-
-    def masked_last():
-        need("a", [tk["last"]])
-        for m in range(4):
-            tk["masked"] = done("a", A.activation(T.cm[:, NP + m:NP + NT:4], T.cl[:, NP + m:NP + NT:4], AF.Copy, scale=T.mcol[:, m:m + 1]))
-
-    def summed(lo, hi):
-        need("v", [tk["masked"]])
-        tk["sum"] = done("v", V.tensor_tensor_scan(T.cq[:, lo:hi], T.reset4[:, 0:hi - lo], T.cm[:, lo:hi], 0.0, OP.mult, OP.add))
-
-    def last_list():
-        need("v", [tk["sum"]])
-        tk["out"] = done("v", V.tensor_scalar(T.offc[:, NP // 4:(NP + NT) // 4], T.cq[:, NP + 3:NP + NT:4], pcol(P3), None, OP.add))
-
-    def far_products():
-        tk["far"] = [products("qw", "pw", "rxf", "rxfs", 0, 128, 4, [("df", 48), v_qw[-1]]), products("qw", "pw", "rxf", "rxfs", CK, 2 * CK, 0, [])]
-        far_relus(0)
-
-    def far_relus(i):
-        tk["relu"] = relus(FAR0 + CK * i, CK, 0 if i else 4, CK * (i - 1) if i else 0, tk["far"][min(i, 1)], i < HELP[me])
-
-    def far_answer(i):
-        answer([far[2 - i if BACKWARD[me] else i]], 128 * i + PAD, pack("rt", CK * i, 128, "rc", "rs", 128 * i, tk["relu"] + [c_rt]))
-
-    def near_products(both):
-        tk["near"] = relus(NEAR0, 2 * CK, 4, 0, products("qw", "pw", "rxn", "rxns", 0, 2 * CK, 4, [("dn", 32), v_qw[-1]]), both)
-
-    def own_products():
-        tk["own"] = relus(OWN0, 128, 0, 0, products("qw", "pw", "ct", "cs", 128 * idx[me], 128, 0, [tk["codes"], v_qw[-1]]), False)
-
-    def own_results():
-        d = pack("rt", OWN0, 128, "rc", "rs", OWNC, tk["own"])
-        unpack(me, 4, products("qe", "pe", "rc", "rs", OWNC, 128, 4, [d, tk["qe"]]))
-
-    def last_unpack():
-        tk["qe"] = qunpack(3)
-
-    todo = list(coming(me))
-
-    def back():
-        e = todo.pop(0)
-        j = coming(me).index(e)
-        bank = 4 * (j % 2)
-        return e, bank, products("qe", "pe", "rc", "rs", LAND0 + CK * j - PAD, 128, bank, [("r%d" % e, 16 if e in far else 8)] + got[me])
-
-    def sums_so_far(e, lo, hi):
-        return T.aa[:, 0:slot(e)].indirect(T.offc[:, 24 * (e - 1) + lo:24 * (e - 1) + hi])
-
-    def chain(e):
-        ready = [tk["list", e], c_aa, tk.get("chain")] + got[0]
-        if e in got:
-            need("v", ready + got[e])
-            s = slice(slot(e), slot(e) + 4 * CK)
-            tk["chain"] = done("v", V.tensor_tensor(T.aa[:, s], sums_so_far(e, 0, 24), T.aa[:, s], OP.add))
-            return
-        need("a", ready)
-        d = copy("a", T.gg[:, 192:384], sums_so_far(e, 12, 24))
-        need("v", ready)
-        need("v", [d, copy("v", T.gg[:, 0:192], sums_so_far(e, 0, 12))])
-        _, bank, u = back()
-        for b in range(4):
-            need("v", [u[b]])
-            o = 512 * (bank + b) + PAD
-            tk["chain"] = done("v", V.tensor_tensor(T.aa[:, slot(e) + b:slot(e) + 4 * CK:4], T.gg[:, b:4 * CK:4], T.pp[:, o:o + CK], OP.add))
-        free[bank] = [tk["chain"]]
-
-    work = {"s": lambda: singles(4, N), "t": lambda: singles_sum(4, N), "u": lambda: singles_out(4, N), ".": tab,
-            "W": lambda: previous(0, N - 1), "w": lambda: previous(0, 3), "x": lambda: previous(3, N - 1), "e": lambda: offsets(4, N),
-            "y": masked_last, "k": lambda: summed(NP, NP + 128), "l": lambda: summed(NP + 128, NP + 256), "L": lambda: summed(NP + 256, NP + NT), "m": last_list,
-            "d": sends[4], "G": lambda: a_x.append(gather("a", 96, 120)), "g": lambda: a_x.append(gather("a", 120, 144)), "c": sends[5], "o": own_products, "O": own_results,
-            "f": far_products, "h": lambda: far_relus(1), "j": lambda: far_relus(2),
-            "F": lambda: far_answer(0), "H": lambda: far_answer(1), "J": lambda: far_answer(2),
-            "n": lambda: near_products(False), "p": lambda: near_products(True),
-            "N": lambda: answer(near, NEARC, pack("rt", NEAR0, 2 * CK, "rc", "rs", NEARC, tk["near"])),
-            "a": lambda: qunpack(2), "A": lambda: qunpack(1), "b": last_unpack, "U": lambda: unpack(*back())}
-    work.update({str(e): lambda e=e: chain(e) for e in range(1, N)})
-    for step in PLAN[me] + SUM[me]:
-        work[step]()
-
-    win = T.aa[:, 0:slot(N)]
-    for k in range(4):
-        q = "va"[k % 2]
-        need(q, [tk["chain"], tk["out"]])
-        need("s", [copy(q, T.yy[:, NT * k:NT * k + NT], win.indirect(T.offc[:, NP // 4 + 24 * k:NP // 4 + 24 * k + 24]))])
-        g.sync.dma_start(T.y[:, NT * k:NT * k + NT], T.yy[:, NT * k:NT * k + NT]).then_inc(T.sem["sty"], 16)
-
-    g.wait_ge(T.sem["loc"], local[0])
-    for s in count:
-        g.wait_ge(T.sem[s], count[s])
-    g.wait_ge(T.sem["sty"], 64)
+    if not PLANS:
+        PLANS["plan"] = plan([graph(r, cores, topo, T, g) for r in range(N)])
+    order, extra, _ = PLANS["plan"]
+    tasks = graph(me, cores, topo, T, g)[0]
+    queue = {"v": g.vector, "a": g.scalar, "t": g.tensor, "p": g, "s": g.sync}
+
+    token, count = {}, {}
+    for q in queue:
+        for i in order[me, q]:
+            t = tasks[i]
+            if "to" in t:
+                count["loc"] = count.get("loc", 0) + 8
+                continue
+            s, n = t["sem"] if "sem" in t else ("sp%d" % sum(1 for c in count if c.startswith("sp")) if q == "p" else "s" + q, 1)
+            count[s] = count.get(s, 0) + n
+            token[i] = (s, count[s])
+    for q in queue:
+        seen = {}
+        for i in order[me, q]:
+            t = tasks[i]
+            bank, freed = extra.get((me, i), (None, []))
+            if "of" in t:
+                bank = extra[me, t["of"]][0]
+            want = {}
+            for d in t["deps"] + freed:
+                s, n = d if isinstance(d, tuple) else token[d]
+                want[s] = max(want.get(s, 0), n)
+            for s, n in want.items():
+                if seen.get(s, 0) < n:
+                    queue[q].wait_ge(T.sem[s], n)
+                    seen[s] = n
+            ins = t["call"](q, bank)
+            if i in token:
+                ins.then_inc(T.sem[token[i][0]], t["sem"][1] if "sem" in t else 1)
+
+    for s, n in count.items():
+        g.wait_ge(T.sem[s], n)

from concourse.bass import DstId, RemoteDMATransfer
from concourse.mybir import dt, AluOpType, ActivationFunctionType

OP = AluOpType
AF = ActivationFunctionType
NT, CK, N = 384, 96, 6
BIG = 1e29
STEP = 2.0 ** 90
UNIT = 2.0 ** 75
F8, U8, F32, BF, U16, I32 = "float8_e4m3fn_x4", "uint8", "float32", "bfloat16", "uint16", "int32"

PAD = 128 - CK
HALF = NT // 2
WIN = HALF + CK
NP = CK * (N - 1)
LAST = N - 1
ROUNDS = ({"k": "1", "W": 16, "NS": 5, "bank": 0, "G": 144, "views": (16, 0), "P": 128},
          {"k": "2", "W": 32, "NS": 6, "bank": 2, "G": 192, "views": (64, 0), "P": 64})
XW, RW = NT + 128 * N + NP, 128 * N + NP

SHAPES = {
    BF: {"xsb": 4 * NT, "x2": 4 * NT, "wgs": 32, "w1s": 2048, "et": 516, "reset4": 516, "xt": 4 * (PAD + N * CK), "rt": 4 * 128 * N},
    F8: {"xc": XW, "qw": 512, "qe": 512, "rc": RW},
    U8: {"xs": XW, "pw": 512, "pe": 512, "rs": RW},
    I32: {"pi": 2, "pci": 12},
    U16: {"offw": 8 * N, "offx": 6 * N, "offy": 6 * N, "off1": 6 * N, "offm": 2, "offc": (NP + 2 * NT) // 4, "offz": 6},
    F32: {"pc": 12, "pd": 24, "offwf": 8 * N, "offmf": 2, "im4": CK, "slots": NP, "mk": CK, "mcol": 4, "both": 32, "tokr": 6 * N, "zs": HALF, "m31": HALF, "m32": HALF,
          "rr1": HALF, "md1": HALF, "cl": 2 * NT, "cm": NP + 2 * NT, "cq": NP + 2 * NT, "aa": 4 + 4 * NP, "gg": 4 + 4 * CK, "yy": 4 * NT},
}
for R in ROUNDS:
    k, n = R["k"], HALF // R["W"]
    R["n"] = n
    SHAPES[BF].update({"wga" + k: 4 * R["G"], "cmp" + k: n * HALF, "reset" + k: HALF, "eqw" + k: HALF, "corr" + k: HALF, "sums" + k: n * CK})
    SHAPES[F8].update({"qg" + k: R["G"]})
    SHAPES[U8].update({"pg" + k: R["G"]})
    SHAPES[U16].update({"offr" + k: n})
    SHAPES[F32].update({"k" + k: HALF, "sc" + k: HALF, "akk" + k: 4 * n, "akq" + k: 4 * n, "akm" + k: 4 * n, "first" + k: n, "tok" + k: 16 * n, "tokf" + k: 16 * n,
                        "sin" + k: 16 * n, "win" + k: WIN, "t1" + k: CK + 128, "pair" + k: 32, "pick" + k: 16, "s4" + k: 16})
SCRATCH = {name: ("sbuf", [128, n], kind) for kind in SHAPES for name, n in SHAPES[kind].items()}
SCRATCH["pp"] = ("psum", [128, 4096], F32)
SEMAPHORES = (["sv", "sa", "st", "ldx", "ldx2", "ldg", "ldw", "ld2", "sty", "loc"] + ["x%d" % e for e in range(N)] + ["r%d" % e for e in range(N)]
              + ["sp%d" % i for i in range(28)])

SERVED = [[3, 1, 4, 2, 5, 0], [2, 4, 5, 0, 3, 1], [0, 5, 1, 3, 4, 2], [0, 2, 1, 4, 3, 5], [1, 2, 0, 3, 5, 4], [0, 1, 2, 3, 4, 5]]
RUNS = ((0,), (1,), (2, 3), (4,), (5,))
TOGETHER = [[[3], [4], [1], [5, 2], [0]], [[4], [5], [3], [1, 2], [0]], [[5, 3], [4, 1], [0], [2]], [[0], [1], [2], [3, 4], [5]], [[1], [5], [0], [3, 2], [4]],
            [[5], [0], [1], [3, 4], [2]]]
UNPACKED = [[[e] for e in range(N)] for s in range(N)]
PIECES = (12, 24, 24, 24, 12)
PREVIOUS = ((0, 2), (2, 4))
DIRECT = (1, 0)

CYC, LEAST, FIRST, STORE = 0.83e-3, 64, 1.0, 0.62 / 24
LOADS = {"ldg": 1.45, "ldx": 2.0, "ldx2": 2.6, "ldw": 5.6, "ld2": 6.7}
PACES = [{"all": 1.0, "tensor": 1.3, "gather": 1.5, "scatter": 3.0, "wake": 0.17, "issue": 0.15, "start": 1.3, "far": (0.42, 0.2), "near": (0.42, 0.2), "scale": 1.0},
         {"all": 1.2, "tensor": 1.5, "gather": 1.6, "scatter": 3.8, "wake": 0.15, "issue": 0.3, "start": 1.5, "far": (0.95, 0.55), "near": (0.7, 0.35), "scale": 1.2},
         {"all": 1.4, "tensor": 1.8, "gather": 1.8, "scatter": 4.8, "wake": 0.16, "issue": 0.15, "start": 1.3, "far": (0.55, 0.3), "near": (0.42, 0.2), "scale": 1.35}]
DUE, FEED = (16.5, 16.2, 15.4, 15.0, 14.2, 13.8), 23.4
GRAB, TURNS, MENDS, EVEN, HEAT, SEED = 0.3, 4, 4000, 0.5, 0.02, 1


def cyc(n):
    return max(LEAST, n) * CYC


def layout(r):
    at, col = {}, 0
    mine = [grp for grp in TOGETHER[r] if r in grp][0]
    singles = [grp[0] for grp in TOGETHER[r] if len(grp) == 1 and grp != mine]
    for tile in (("q0",), ("q1",)) + RUNS:
        col += HALF if tile[0] in ("q0", "q1") else max(128, CK * len(tile))
        for i, t in enumerate(tile):
            at["x", t] = col - (HALF if t in ("q0", "q1") else CK * (len(tile) - i))
        if tile[-1] == SERVED[r].index(r) and len(mine) > 1:
            for s in mine[1:]:
                at["xl", s] = col
                col += CK
        elif singles:
            at["xl", singles[0]], at["xpad", singles[0]] = col, tile[-1]
            singles.pop(0)
            col += CK
    for s in [s for grp in TOGETHER[r] if len(grp) > 1 and grp != mine for s in grp]:
        at["xl", s] = col
        col += CK
    col = o = 0
    singles = [grp[0] for grp in UNPACKED[r] if len(grp) == 1 and grp != [r]]
    for j, grp in enumerate(TOGETHER[r]):
        sides = [singles.pop(0) for _ in range(2) if singles]
        for e in sides[:1]:
            at["rl", e], at["rpad", e], at["first", e] = col, j, True
            col += CK
        at["r", j], at["rt", j] = col, o
        col, o = col + max(128, CK * len(grp)), o + max(128, CK * len(grp))
        for i, s in enumerate(grp):
            at["rc", s] = col - CK * (len(grp) - i)
        for e in sides[1:]:
            at["rl", e], at["rpad", e] = col, j
            col += CK
    for e in [e for grp in UNPACKED[r] if len(grp) > 1 for e in grp]:
        at["rl", e] = col
        col += CK
    at["rl", r] = at["rc", r]
    return at


def graph(me, cores, topo, T, g):
    core = cores[me]
    at = layout(me)
    order = SERVED[me]
    idx = {e: i for i, e in enumerate(order)}
    tasks, part = [], [0]
    V, A, TE = g.vector, g.scalar, g.tensor
    R1, R2 = ROUNDS

    def flat(deps):
        out = []
        for d in deps:
            if isinstance(d, list):
                out.extend(flat(d))
            elif d is not None:
                out.append(d)
        return out

    def add(q, cost, call, *deps, **more):
        tasks.append(dict(q=q, part=part[0], cost=cost if isinstance(cost, tuple) else (cost, 0, 0), call=call, deps=flat(list(deps)), **more))
        return len(tasks) - 1

    def vec(n, call, *deps):
        return add("v", cyc(n), lambda q, b: call(), *deps)

    def act(n, call, *deps):
        return add("a", cyc(n), lambda q, b: call(), *deps)

    def pool(fixed, n, call, *deps):
        return add("p", fixed + 2 * n * CYC, lambda q, b: call(), *deps)

    def copy(q, out, in_):
        return A.activation(out, in_, AF.Copy) if q == "a" else V.tensor_copy(out, in_)

    def picked(n):
        return (0.055, n, 0)

    def strewn(n):
        return (0.05, 0, n)

    def pack(src, lo, n, qc, qs, there, *deps):
        return add("v", 0.012 + 0.88e-3 * n, lambda q, b: V.quantize_mx(T[qc][:, there:there + n], T[qs][:, there:there + n], T[src][:, lo:lo + 4 * n]), *deps)

    def load(q, sem, out, in_, behind=None, *deps):
        return add(q, 0.05, lambda q, b: (g.sync if q == "s" else A).dma_start(out(), in_()), *deps, sem=(sem, 16), lands=LOADS[sem], behind=behind)

    LDX = load("s", "ldx", lambda: T.xsb[:, 0:4 * HALF], lambda: T.x[:, 0:4 * HALF])
    LDG = load("a", "ldg", lambda: T.wgs[:], lambda: T.wg[:, 0:32])
    LDX2 = load("s", "ldx2", lambda: T.xsb[:, 4 * HALF:4 * NT], lambda: T.x[:, 4 * HALF:4 * NT], LDX)
    LDW = load("s", "ldw", lambda: T.w1s[:], lambda: T.w1[:], LDX2, LDX2)
    LD2 = load("s", "ld2", lambda: T.x2[:, 0:4 * NT - 2], lambda: T.x[:, 2:4 * NT], LDW)

    def iota(name, pattern, n, base=0, lo=0):
        return pool(0.13, n, lambda: g.iota(T[name][:, lo:lo + n], pattern, base, 0, allow_small_or_imprecise_dtypes=True))

    def zeros(name, lo, n):
        return iota(name, [[0, n]], n, 0, lo)

    def fill(name, cols, value, n=1, *deps):
        return vec(n, lambda: V.memset(T[name][:, cols], value), *deps)

    c_pi = pool(0.13, 2, lambda: g.iota(T.pi[:], [[0, 2]], 0, 1))
    c_k = {"1": iota("k1", [[0, 12], [1, 16]], HALF), "2": iota("k2", [[0, 6], [1, 32]], HALF)}
    c_tokf = {"1": iota("tokf1", [[1, HALF]], HALF), "2": iota("tokf2", [[32, 6], [1, 16]], CK)}
    c_im4, c_offmf, c_offwf = iota("im4", [[0, 24], [1, 4]], CK), iota("offmf", [[8, 2]], 2), iota("offwf", [[4, N], [0, 8]], 8 * N)
    c_slots = iota("slots", [[1, NP]], NP, 1)
    c_pad, c_aa, c_gg = zeros("xt", 0, 4 * PAD), zeros("aa", 0, 4), zeros("gg", 0, 4)
    c_win = {"1": [zeros("win1", CK - 16, 16), zeros("win1", HALF, 16)], "2": zeros("win2", CK - 16, 128)}
    c_pick = {R["k"]: zeros("pick" + R["k"], 0, 16) for R in ROUNDS}
    c_cl = [zeros("cl", o, NT) for o in (0, NT)]

    c_zero = {"1": [fill("wga1", slice(None), 0.0, 288)], "2": [fill("wga2", slice(o, o + 256), 0.0, 128) for o in (0, 512)]}
    P3, P15, P31, P16, PM, H1, H2, FT, P14, P2, P1 = range(11)

    def bits(k, m, s):
        return vec(1, lambda: V.tensor_scalar(T.pci[:, k:k + 1], T.pi[:, 0:1], m, s, OP.bitwise_and, OP.logical_shift_right), c_pi)

    c_pc = vec(8, lambda: V.tensor_copy(T.pc[:, 0:8], T.pci[:, 0:8]),
               [bits(*x) for x in ((P3, 3, 0), (P15, 15, 0), (P31, 31, 0), (P16, 16, 0), (H1, 16, 4), (H2, 64, 6), (FT, 8, 3), (PM, 15, 2))])
    c_pc2 = vec(3, lambda: V.tensor_copy(T.pc[:, 8:11], T.pci[:, 8:11]), [bits(*x) for x in ((P14, 14, 1), (P2, 2, 1), (P1, 1, 0))])
    c_reset4 = fill("reset4", slice(0, 516, 4), 0.0, 65, fill("reset4", slice(None), 1.0, 258))

    def pcol(k):
        return T.pc[:, k:k + 1]

    c_offw = vec(8 * N, lambda: V.tensor_scalar(T.offw[:], T.offwf[:], pcol(P3), None, OP.add), c_offwf, c_pc)

    SGN, KC, TOK, MB, CV, BIAS, TU, TB, LOW, MA, MC = range(0, 22, 2)

    def two(j):
        return T.pd[:, j:j + 2]

    def one(j):
        return T.pd[:, j:j + 1]

    def dcol(j, R):
        return one(j + ROUNDS.index(R))

    c_mb = act(2, lambda: A.activation(two(MB), T.pc[:, P15:P15 + 2], AF.Copy, scale=-STEP), c_pc)
    c_sgn = act(2, lambda: A.activation(two(SGN), T.pc[:, H1:H1 + 2], AF.Copy, bias=1.0, scale=-2.0), c_pc)
    c_kc0 = act(2, lambda: A.activation(two(KC), T.pc[:, H1:H1 + 2], AF.Copy, bias=CK + 1.0, scale=CK - 3.0), c_pc)
    c_cv = act(2, lambda: A.activation(two(CV), T.pc[:, H1:H1 + 2], AF.Copy, bias=float(HALF), scale=-(CK + 1.0)), c_pc)
    d = [act(1, lambda: A.activation(one(TOK), pcol(H1), AF.Copy, scale=float(HALF)), c_pc),
         act(1, lambda: A.activation(one(TOK + 1), pcol(H2), AF.Identity, bias=pcol(P16), scale=float(HALF)), c_pc),
         act(1, lambda: A.activation(one(TU), pcol(FT), AF.Copy, scale=4.0 * UNIT), c_pc),
         act(1, lambda: A.activation(one(LOW), pcol(FT), AF.Copy, bias=-BIG, scale=BIG), c_pc)]
    d = [act(1, lambda: A.activation(one(TB), pcol(FT), AF.Identity, bias=one(LOW), scale=UNIT), d), d]
    c_bias = act(2, lambda: A.activation(two(BIAS), two(TOK), AF.Identity, bias=one(TB), scale=one(TU)), d)
    d = [vec(1, lambda: V.tensor_scalar(one(MA), pcol(H1), -224.0, 112.0, OP.mult, OP.add), c_pc),
         vec(1, lambda: V.tensor_scalar(one(MA + 1), pcol(P14), pcol(P1), 16.0, OP.subtract, OP.mult), c_pc2)]
    d = [vec(1, lambda: V.tensor_scalar(one(MC), one(MA), pcol(P2), one(MA + 1), OP.mult, OP.add), d),
         vec(1, lambda: V.tensor_scalar(one(MC + 1), pcol(H1), 96.0, 16.0, OP.mult, OP.add), c_pc)]
    d = vec(2, lambda: V.tensor_scalar(T.offmf[:], T.offmf[:], one(MC), one(MC + 1), OP.add, OP.add), d, c_offmf)
    c_offm = vec(2, lambda: V.tensor_scalar(T.offm[:], T.offmf[:], CK + 127.0, None, OP.min), d)

    def gate(R, col, e, n):
        k = R["k"]
        return add("va", picked(16 * n), lambda q, b: copy(q, T["wga" + k][:, 4 * col:4 * col + 16 * n], T.wgs[:, 0:32].indirect(T.offw[:, 8 * e:8 * e + n])),
                   c_offw, LDG, c_zero[k] if R is R1 else None)

    c_reset, c_tok, c_kc = {}, {}, {}
    c_reset["1"] = act(HALF, lambda: A.activation(T.reset1[:], T.k1[:], AF.Sign), c_k["1"])
    c_m3 = act(HALF, lambda: A.activation(T.m31[:], T.k1[:], AF.Abs, bias=dcol(MB, R1), scale=STEP), c_k["1"], c_mb)
    c_rr = act(HALF, lambda: A.activation(T.rr1[:], T.reset1[:], AF.Copy, bias=-BIG, scale=BIG), c_reset["1"])
    d = act(HALF, lambda: A.activation(T.m32[:], T.k2[:], AF.Abs, bias=dcol(MB, R2), scale=STEP), c_k["2"], c_mb)
    c_reset["2"] = act(HALF, lambda: A.activation(T.reset2[:], T.m32[:], AF.Sign), d)

    def tokens(R):
        k, W, ns = R["k"], R["W"], R["NS"]
        c_tok[k] = act(16 * R["n"], lambda: A.activation(T["tok" + k][:], T["tokf" + k][:], AF.Identity, bias=dcol(BIAS, R), scale=one(TU)), c_tokf[k], c_bias)
        ends = lambda: T.tokf1[:, W - 1:W * ns:W]
        c_kc[k] = [act(ns, lambda: A.activation(T["akk" + k][:, 3:4 * ns:4], ends(), AF.Identity, bias=dcol(KC, R), scale=dcol(SGN, R)), c_tokf["1"], c_sgn, c_kc0),
                   act(ns, lambda: A.activation(T["akm" + k][:, 3:4 * ns:4], ends(), AF.Identity, bias=dcol(SGN, R), scale=0.0), c_tokf["1"], c_sgn,
                       iota("akm" + k, [[0, ns], [-1, 2], [1, 2]], 4 * ns)),
                   zeros("akk" + k, 4 * ns - 2, 1) if W * ns == HALF else None]

    tokens(R1)
    tokens(R2)
    c_masks = vec(CK, lambda: V.tensor_scalar(T.mk[:], T.im4[:], pcol(PM), 4.0, OP.is_equal, OP.mult), c_im4, c_pc)
    c_offz = vec(6, lambda: V.tensor_scalar(T.offz[:], T.tokf1[:, 0:HALF:32], pcol(P31), None, OP.add), c_tokf["1"], c_pc)
    c_scales = vec(4, lambda: V.tensor_scalar(T.mcol[:], T.k1[:, 0:4], pcol(PM), 4.0, OP.is_equal, OP.mult), c_k["1"], c_pc)
    c_et = pool(0.17, 516, lambda: g.affine_select(T.et[:, 0:515], T.reset4[:, 0:515], [[-1, 515]], OP.is_equal, 0.0, 3, 4), c_reset4)
    v_qe = [pack("et", 3 - b, 128, "qe", "pe", 128 * b, c_et) for b in range(4)]
    v_qw = [pack("w1s", 512 * i, 128, "qw", "pw", 128 * i, LDW) for i in range(4)]

    part[0] += 1
    v_qg = {"1": pack("wga1", 0, R1["G"], "qg1", "pg1", 0, [gate(R1, 16 + 32 * i, order[i], 4) for i in range(4)]),
            "2": pack("wga2", 0, R2["G"], "qg2", "pg2", 0, [gate(R2, 64 + 32 * i, order[4 + i], 8) for i in (0, 1)], c_zero["2"])}
    made = {"q0": pack("xsb", 0, HALF, "xc", "xs", at["x", "q0"], LDX), "q1": pack("xsb", 4 * HALF, HALF, "xc", "xs", at["x", "q1"], LDX2)}

    def z(R, other, lo=0, hi=HALF):
        o = 512 * (R["bank"] + other)
        return T.pp[:, o + lo:o + hi]

    def score(R, other, h, before):
        k, s, c = R["k"], R["views"][h], at["x", "q%d" % h]
        return add("t", (HALF + 16) * CYC, lambda q, b: TE.matmul_mx(z(R, other), T["qg" + k][:, s:s + 128], T["pg" + k][:, s:s + 128],
                                                                      T.xc[:, c:c + HALF], T.xs[:, c:c + HALF], h == 0, h == 1), v_qg[k], made["q%d" % h], behind=before)

    t_z = {R["k"]: [score(R, b, 1, score(R, b, 0, None)) for b in (0, 1)] for R in ROUNDS}
    readers = {b: [] for b in range(8)}

    def reads(R, other, t):
        readers[R["bank"] + other].append(t)
        return t

    part[0] += 1
    s1 = R1["W"] * R1["NS"]
    v_sc = {"1": [], "2": [reads(R2, 0, vec(HALF, lambda: V.transpose(T.sc2[:], z(R2, 0)), t_z["2"][0]))]}
    tasks[v_sc["2"][0]]["due"] = FEED
    for lo, hi in ((0, s1), (s1, HALF)):
        d = reads(R1, 0, vec(hi - lo, lambda lo=lo, hi=hi: V.tensor_tensor(T.md1[:, lo:hi], z(R1, 0, lo, hi), T.m31[:, lo:hi], OP.subtract), t_z["1"][0], c_m3))
        v_sc["1"].append(vec(hi - lo, lambda lo=lo, hi=hi: V.tensor_tensor_scan(T.sc1[:, lo:hi], T.rr1[:, lo:hi], T.md1[:, lo:hi], 0.0, OP.add, OP.max), d, c_rr))

    def ranks(R):
        k, W, ns, n = R["k"], R["W"], R["NS"], R["n"]
        cmp, sc, akk, offr = (lambda lo, hi: T["cmp" + k][:, lo:hi]), (lambda q: T["sc" + k][:, W * q + W - 1:W * q + W]), "akk" + k, "offr" + k
        d = [reads(R, 0, vec(CK, lambda lo=lo: V.tensor_tensor(T["eqw" + k][:, lo:lo + CK], z(R, 0, lo, lo + CK), T["sc" + k][:, lo:lo + CK], OP.is_equal), v_sc[k], t_z[k][0]))
             for lo in (0, CK)]
        tie = vec(CK, lambda: V.tensor_tensor_scan(T["corr" + k][:], T["reset" + k][:], T["eqw" + k][:], 0.0, OP.mult, OP.add), d, c_reset[k])
        acc = [add("va", cyc(ns), lambda q, b: copy(q, T[akk][:, 0:4 * ns:4], T["corr" + k][:, W - 1:W * ns:W]), tie)]
        for j in range(ns):
            c, cut = HALF * j, W * j + W
            d = reads(R, 1, act(HALF, lambda j=j, c=c: A.activation(cmp(c, c + HALF), z(R, 1), AF.Sign, bias=sc(j), scale=-1.0), t_z[k][1], v_sc[k][0]))
            acc.append(act(max(cut, LEAST) + 24, lambda j=j, c=c, cut=cut: A.activation(cmp(c, c + cut), cmp(c, c + cut), AF.Relu, accum_out=T[akk][:, 4 * j + 1:4 * j + 2]), d))
            if cut < HALF:
                acc.append(act(max(HALF - cut, LEAST) + 24, lambda j=j, c=c, cut=cut: A.activation(cmp(c + cut, c + HALF), cmp(c + cut, c + HALF), AF.Relu, scale=-1.0,
                                                                                                   accum_out=T[akk][:, 4 * j + 2:4 * j + 3]), d))
        d = vec(4 * ns, lambda: V.tensor_tensor_scan(T["akq" + k][:, 0:4 * ns], T["akm" + k][:, 0:4 * ns], T[akk][:, 0:4 * ns], 0.0, OP.mult, OP.add), acc, c_kc[k])
        places = [vec(ns, lambda: V.tensor_copy(T[offr][:, 0:ns], T["akq" + k][:, 3:4 * ns:4]), d)]
        if ns == n:
            return places
        first = vec(n, lambda: V.tensor_scalar(T["first" + k][:], T["corr" + k][:, W - 1:HALF:W], -1.0, -float(CK), OP.mult, OP.add), tie)
        sums = []
        for j in range(ns, n):
            c, cut, o = HALF * j, W * j + W, CK * (j - ns)
            d = [reads(R, 0, vec(cut, lambda j=j, c=c, cut=cut: V.tensor_scalar(cmp(c, c + cut), z(R, 0, 0, cut), sc(j), None, OP.is_ge), t_z[k][0], v_sc[k][-1]))]
            if cut < HALF:
                d.append(reads(R, 0, vec(HALF - cut, lambda j=j, c=c, cut=cut: V.tensor_scalar(cmp(c + cut, c + HALF), z(R, 0, cut, HALF), sc(j), None, OP.is_gt), t_z[k][0], v_sc[k][-1])))
            sums.append(vec(CK // 2, lambda j=j, c=c, o=o: V.tensor_tensor_scan(T["sums" + k][:, o:o + CK], cmp(c, c + CK), cmp(c + CK, c + HALF), T["first" + k][:, j:j + 1], OP.add, OP.add),
                            d, first))
        return places + [vec(n, lambda: V.tensor_scalar(T[offr][:, ns:n], T["sums" + k][:, CK - 1:CK * (n - ns):CK], dcol(SGN, R), dcol(CV, R), OP.mult, OP.add), sums, c_sgn, c_cv)]

    part[0] += 1
    a_zs = reads(R2, 1, act(HALF, lambda: copy("a", T.zs[:], z(R2, 1)), t_z["2"][1]))
    v_sin = {"1": reads(R1, 0, vec(HALF, lambda: V.tensor_tensor(T.sin1[:], z(R1, 0), T.tok1[:], OP.max), t_z["1"][0], c_tok["1"])),
             "2": add("v", picked(CK), lambda q, b: V.tensor_tensor(T.sin2[:], T.zs[:].indirect(T.offz[:]), T.tok2[:], OP.max), a_zs, c_offz, c_tok["2"])}

    def lists(R):
        k, n, P = R["k"], R["n"], R["P"]
        win, t1, pair, pick = "win" + k, "t1" + k, "pair" + k, "pick" + k
        part[0] += 1
        d = add("v", strewn(16 * n), lambda q, b: V.tensor_copy(T[win][:].indirect(T["offr" + k][:]), T["sin" + k][:]), ranks(R), v_sin[k], c_win[k])
        part[0] += 1
        d = [vec(CK, lambda: V.transpose(T[t1][:, 0:CK], T[win][:, CK:2 * CK]), d), vec(128, lambda: V.transpose(T[t1][:, CK:CK + 128], T[win][:, CK - 16:CK + 112]), d)]
        if R is R1:
            d = add("v", picked(32), lambda q, b: V.tensor_copy(T[pair][:], T[t1][:].indirect(T.offm[:])), d, c_offm)
        else:
            d = add("va", picked(32), lambda q, b: copy(q, T.both[:], T[t1][:].indirect(T.offm[:])), d, c_offm)
            d = [vec(32, lambda h=h: V.tensor_tensor(T[pair][0:64, 1 - h:32:2], T.both[64 * h:64 * h + 64, 0:32:2], T.both[64 * h:64 * h + 64, 1:32:2], OP.add), d) for h in (0, 1)]
        d = vec(16, lambda: V.tensor_tensor(T[pick][0:P, 1:16:2], T[pair][0:P, 1:16:2], T[pair][0:P, 0:16:2], OP.is_lt), d, c_pick[k])
        return vec(16, lambda: V.tensor_tensor_scan(T["s4" + k][0:P, :], T[pick][0:P, :], T[pair][0:P, 16:32], 0.0, OP.mult, OP.max), d)

    off, odd, single = {}, {}, {}

    def spread(R, lo, hi):
        k, done = R["k"], lists(R)
        mid = lo + DIRECT[ROUNDS.index(R)]

        def found(i):
            return T["s4" + k][32 * (i - lo):32 * (i - lo) + 32, 1:12:2]

        for i in range(lo, mid):
            off[i] = [vec(6, lambda i=i, b=b: V.tensor_scalar(T.offx[32 * b:32 * b + 32, 6 * i:6 * i + 6], found(i), 1.0 / UNIT, -1.0, OP.mult, OP.add), done) for b in range(4)]
        part[0] += 1
        if mid < hi:
            d = [act(6, lambda i=i, b=b: A.activation(T.tokr[32 * b:32 * b + 32, 6 * i:6 * i + 6], found(i), AF.Copy, bias=-1.0, scale=1.0 / UNIT), done)
                 for i in range(mid, hi) for b in (0, 1)]
            d = [vec(6, lambda h=h: V.tensor_copy(T.offx[64 * h:64 * h + 64, 6 * mid:6 * hi], T.tokr[0:64, 6 * mid:6 * hi]), d) for h in (0, 1)]
            for i in range(mid, hi):
                off[i] = d
        for a, b in ((lo, mid), (mid, hi)):
            if a < b:
                d = vec(6, lambda a=a, b=b: V.tensor_scalar(T.offy[:, 6 * a:6 * b], T.offx[:, 6 * a:6 * b], 1.0, None, OP.add), [off[i] for i in range(a, b)])
                for i in range(a, b):
                    odd[i] = d
        d = vec(6, lambda: V.tensor_scalar(T.off1[:, 6 * lo:6 * hi], T.offx[:, 6 * lo:6 * hi], 0.25, None, OP.mult), [off[i] for i in range(lo, hi)])
        for i in range(lo, hi):
            single[order[i]] = d

    spread(R1, 0, 4)
    spread(R2, 4, N)

    def send(r, names, lo, there, sem, dep, due=None):
        es = topo.engines(core, cores[r])[-8:]
        ad = topo.addr(cores[r])

        def call(name, bits):
            src, dst = T[name][:, lo:lo + CK], T[name][:, there:there + CK]
            if bits:
                src, dst = src.bitcast(dt.uint8), dst.bitcast(dt.uint8)
            return g.remote_dma_fused([RemoteDMATransfer(dst_ids=[DstId(rid=ad[0], pnc=ad[1])], dma_engine_mask=sum(1 << e for e in es), remote_sem=T.sem[sem], src=src, dst=dst)],
                                      local_sem=T.sem["loc"])

        for name, bits in zip(names, (True, False)):
            add("p", 0.0, lambda q, b, name=name, bits=bits: call(name, bits), dep, to=(r, sem), engines=es[0],
                moves=("near" if topo.chip(core) == topo.chip(cores[r]) else "far", 1 - bits), due=due)

    before = c_pad
    for run in RUNS:
        part[0] += 1
        lo, hi = run[0], run[-1] + 1
        d = [add("va", picked(CK * len(run)), lambda q, b, lo=lo, hi=hi, t=t: copy(q, T.xt[:, 4 * (PAD + CK * lo) + t:4 * (PAD + CK * hi):4],
                                                                                   T[("xsb", "x2")[t // 2]][:, 0:4 * NT - 2].indirect(T[("offx", "offy")[t % 2]][:, 6 * lo:6 * hi])),
                 [(off, odd)[t % 2][i] for i in run], LD2 if t > 1 else [LDX, LDX2]) for t in range(4)]
        skip = PAD if len(run) == 1 else 0
        t = pack("xt", 4 * (PAD + CK * lo - skip), CK * len(run) + skip, "xc", "xs", at["x", lo] - skip, d, before if skip else None)
        before = d
        for i in run:
            made[i] = t
            if order[i] != me:
                send(order[i], ("xc", "xs"), at["x", i], layout(order[i])["xl", me], "x%d" % me, t, DUE[i])

    def products(stat, plane, codes, planes, lo, n, packed, deps):
        return [add("t", (n + 16) * CYC, lambda q, b, i=i: TE.matmul_mx(T.pp[:, 512 * b:512 * b + n], T[stat][:, 128 * i:128 * i + 128], T[plane][:, 128 * i:128 * i + 128],
                                                                         T[codes][:, lo:lo + n], T[planes][:, lo:lo + n], True, True), packed[i], deps, bank=True)
                for i in range(4)]

    def reader(n, call, product):
        tasks[product]["reader"] = add("va", cyc(n), call, product, of=product)
        return tasks[product]["reader"]

    results = {}
    for j, grp in enumerate(TOGETHER[me]):
        part[0] += 1
        n = CK * len(grp)
        skip = max(0, 128 - n)
        deps = [made[idx[me]] if s == me else ("x%d" % s, 16) for s in grp] + [made[at["xpad", s]] for s in grp if ("xpad", s) in at]
        lo, o = (at["x", idx[me]] if grp[0] == me else at["xl", grp[0]]) - skip, 4 * at["rt", j]

        def relu(q, b, i, o=o, n=n, skip=skip):
            out, src = T.rt[:, o + 4 * skip + i:o + 4 * (skip + n):4], T.pp[:, 512 * b + skip:512 * b + skip + n]
            return A.activation(out, src, AF.Relu, scale=0.05) if q == "a" else V.tensor_scalar(out, src, 0.0, 0.05, OP.max, OP.mult)

        d = [reader(n, lambda q, b, i=i, relu=relu: relu(q, b, i), p) for i, p in enumerate(products("qw", "pw", "xc", "xs", lo, n + skip, v_qw, deps))]
        results[j] = pack("rt", o, n + skip, "rc", "rs", at["r", j], d, zeros("rt", o, 4 * skip) if skip else None)
        for s in grp:
            if s != me:
                send(s, ("rc", "rs"), at["rc", s], layout(s)["rl", me], "r%d" % me, results[j])
    own = [j for j, grp in enumerate(TOGETHER[me]) if me in grp][0]

    part[0] = 20

    def table(e, h):
        return T.cl[:, NT * h:NT * h + NT].indirect(T.off1[:, 6 * idx[e]:6 * idx[e] + 6])

    d, prev = [c_cl[0], c_slots], {}
    for e in range(LAST):
        if e:
            d = prev[e] = add("v", picked(CK), lambda q, b, e=e: V.tensor_tensor(T.cm[:, CK * (e - 1):CK * e], table(e, 0), T.mk[:], OP.mult), d, single[e], c_masks)
        d = add("v", strewn(CK), lambda q, b, e=e: V.tensor_copy(table(e, 0), T.slots[:, CK * e:CK * e + CK]), d, single[e])
    part[0] += 1
    listed = {}
    for lo, hi in PREVIOUS:
        s = vec(CK * (hi - lo), lambda lo=lo, hi=hi: V.tensor_tensor_scan(T.cq[:, CK * lo:CK * hi], T.reset4[:, 0:CK * (hi - lo)], T.cm[:, CK * lo:CK * hi], 0.0, OP.mult, OP.add),
                [prev[e] for e in range(lo + 1, hi + 1)], c_reset4)
        s = vec(24 * (hi - lo), lambda lo=lo, hi=hi: V.tensor_scalar(T.offc[:, 24 * lo:24 * hi], T.cq[:, CK * lo + 3:CK * hi:4], pcol(P3), None, OP.add), s)
        for e in range(lo + 1, hi + 1):
            listed[e] = s

    def by_token(h, d):
        o = NP + NT * h
        d = [act(CK, lambda m=m: A.activation(T.cm[:, o + m:o + NT:4], T.cl[:, NT * h + m:NT * h + NT:4], AF.Copy, scale=T.mcol[:, m:m + 1]), d, c_scales) for m in range(4)]
        d = [vec(128, lambda lo=lo: V.tensor_tensor_scan(T.cq[:, lo:lo + 128], T.reset4[:, 0:128], T.cm[:, lo:lo + 128], 0.0, OP.mult, OP.add), d, c_reset4) for lo in range(o, o + NT, 128)]
        return vec(CK, lambda: V.tensor_scalar(T.offc[:, o // 4:(o + NT) // 4], T.cq[:, o + 3:o + NT:4], pcol(P3), None, OP.add), d)

    part[0] += 1
    v_before = by_token(0, d)
    part[0] += 1
    v_last = by_token(1, add("v", strewn(CK), lambda q, b: V.tensor_copy(table(LAST, 1), T.slots[:, 0:CK]), c_cl[1], c_slots, single[LAST]))

    def slot(e):
        return 4 * (1 + CK * e)

    got = {}
    for grp in UNPACKED[me]:
        part[0] = 30 + grp[0]
        n = CK * len(grp)
        skip = PAD if n == CK and ("first", grp[0]) not in at and (grp != [me] or len(TOGETHER[me][own]) == 1) else 0
        deps = [results[own] if e == me else ("r%d" % e, 16) for e in grp] + [results[at["rpad", e]] for e in grp if ("rpad", e) in at]
        name, o = ("gg", 4) if grp == [LAST] else ("aa", slot(grp[0]))
        d = [reader(n, lambda q, b, i=i, name=name, o=o, n=n, skip=skip: copy(q, T[name][:, o + i:o + 4 * n:4], T.pp[:, 512 * b + skip:512 * b + skip + n]), p)
             for i, p in enumerate(products("qe", "pe", "rc", "rs", at["rl", grp[0]] - skip, max(n, 128), v_qe, deps))]
        for e in grp:
            got[e] = d
    part[0] = 40
    chain = [got[0], c_aa]
    for e in range(1, LAST):
        chain = add("v", picked(4 * CK), lambda q, b, e=e: V.tensor_tensor(T.aa[:, slot(e):slot(e + 1)], T.aa[:, 0:slot(e)].indirect(T.offc[:, 24 * e - 24:24 * e]),
                                                                            T.aa[:, slot(e):slot(e + 1)], OP.add), chain, got[e], listed[e])

    lo = 0
    for n in PIECES:
        def piece(lo=lo, n=n):
            return T.yy[:, 16 * lo:16 * (lo + n)]

        def offsets(h, lo=lo, n=n):
            return T.offc[:, (NP + NT * h) // 4 + lo:(NP + NT * h) // 4 + lo + n]

        d = add("va", picked(16 * n), lambda q, b, piece=piece, offsets=offsets: copy(q, piece(), T.gg[:].indirect(offsets(1))), got[LAST], v_last, c_gg)
        d = add("v", picked(16 * n), lambda q, b, piece=piece, offsets=offsets: V.tensor_tensor(piece(), T.aa[:].indirect(offsets(0)), piece(), OP.add), chain, v_before, d)
        add("s", 0.05, lambda q, b, lo=lo, n=n, piece=piece: g.sync.dma_start(T.y[:, 16 * lo:16 * (lo + n)], piece()), d, sem=("sty", 16), engines="y", moves=STORE * n,
            due=STORE * (NT // 4 - lo - n))
        lo += n
    return tasks, readers


def slot_in(taken, s, n):
    i = 0
    while i < len(taken) and taken[i][1] <= s:
        i += 1
    while i < len(taken) and taken[i][0] < s + n - 1e-9:
        s = max(s, taken[i][1])
        i += 1
    taken.insert(i, (s, s + n))
    return s + n


def plan(graphs):
    key = [(r, i) for r, (tasks, _) in enumerate(graphs) for i in range(len(tasks))]
    number = {k: j for j, k in enumerate(key)}
    task = [graphs[r][0][i] for r, i in key]
    n, paces, lines = len(key), range(len(PACES)), [(r, q) for r in range(N) for q in "vatps"]
    sent = {}
    for j, t in enumerate(task):
        sent.setdefault(t.get("to"), []).append(j)
    wants = [[x for d in task[j]["deps"] for x in (sent[key[j][0], d[0]] if isinstance(d, tuple) else [number[key[j][0], d]])] for j in range(n)]
    behind = [None if task[j].get("behind") is None else number[key[j][0], task[j]["behind"]] for j in range(n)]
    feeds, leads = [[] for j in range(n)], [[] for j in range(n)]
    for j in range(n):
        for d in wants[j]:
            feeds[d].append(j)
        if behind[j] is not None:
            leads[behind[j]].append(j)
    moves = [None if "moves" not in t else [m[t["moves"][0]][t["moves"][1]] if "to" in t else t["moves"] for m in PACES] for t in task]
    lands, begins = [t.get("lands") for t in task], [m["start"] for m in PACES]
    lasts = [[m["issue"] if "to" in t else t["cost"][0] * (m["tensor"] if t["q"] == "t" else 1.0 if "moves" in t or "lands" in t else m["all"])
              + m["all"] * CYC * (t["cost"][1] * m["gather"] + t["cost"][2] * m["scatter"]) for m in PACES] for t in task]
    wakes, scales = [m["wake"] for m in PACES], [m["scale"] * len(PACES) for m in PACES]
    lane = [(key[j][0], task[j].get("engines")) for j in range(n)]
    reader = [number[key[j][0], task[j]["reader"]] if "bank" in task[j] else None for j in range(n)]
    scores = {(r, b): [number[r, t] for t in graphs[r][1][b]] for r in range(N) for b in range(8)}

    def forwards(ahead):
        cost, wake = [c[0] for c in lasts], wakes[0]
        left = [len(wants[j]) + (behind[j] is not None) for j in range(n)]
        can, free, line = {w: {} for w in lines}, {w: 0.0 for w in lines}, {w: [] for w in lines}
        end, busy, done, banks, turn = {}, {}, [], dict(scores), [4] * N

        def offer(j, t):
            for q in task[j]["q"]:
                can[key[j][0], q][j] = t

        def starts(w):
            last = banks[w[0], turn[w[0]]] if w[1] == "t" else []
            bank = max([end.get(t, 1e9) + wake for t in last] + [0.0])
            return {j: max(t, free[w], 0.0 if reader[j] is None else bank) for j, t in can[w].items()}

        for j in range(n):
            if not left[j]:
                offer(j, 0.0)
        while len(done) < n:
            now, where = min((min(starts(w).values()), w) for w in lines if can[w])
            r, q = where
            c = starts(where)
            if q == "v":
                c = {j: t for j, t in c.items() if task[j]["q"] == "v" or free[r, "a"] > t + GRAB * cost[j]}
                if not c or min(c.values()) > now:
                    free[where] = min(list(c.values()) + [max(now, free[r, "a"]) + 1e-6])
                    continue
            for j in sorted((j for j in c if c[j] <= now), key=lambda j: -ahead[j]):
                if all(now + cost[j] + ahead[u] <= max(s + ahead[u], s + cost[u] + ahead[j]) + 1e-9 for u, s in c.items() if now < s < now + cost[j] and ahead[u] > ahead[j]):
                    break
            else:
                free[where] = min(s for s in c.values() if s > now)
                continue
            for p in task[j]["q"]:
                del can[r, p][j]
            line[where].append(j)
            done.append(j)
            free[where] = now + cost[j]
            end[j] = now + cost[j] if lands[j] is None else lands[j]
            if moves[j] is not None:
                end[j] = busy[lane[j]] = max(now + begins[0] + (0.0 if r in busy else FIRST), busy.get(lane[j], 0.0)) + moves[j][0]
                busy[r] = True
            if reader[j] is not None:
                banks[r, turn[r]] = [reader[j]]
                turn[r] = (turn[r] + 1) % 8
            for u in feeds[j] + leads[j]:
                left[u] -= 1
                if not left[u]:
                    offer(u, max([end[d] + wake for d in wants[u]] + [0.0]))
        return line, done

    def backwards(done, where):
        taken, late = {}, [0.0] * n
        for j in done[::-1]:
            s = max([task[j].get("due") or 0.0] + [wakes[0] + late[u] for u in feeds[j] + leads[j]])
            if moves[j] is not None:
                s = (slot_in(taken.setdefault(lane[j], []), s, moves[j][0]) if where else s + moves[j][0]) + begins[0] - lasts[j][0]
            late[j] = slot_in(taken.setdefault(where[j], []), s + (lands[j] or 0.0), lasts[j][0]) if where else s + (lands[j] or 0.0) + lasts[j][0]
        return late

    def run(line):
        more, extra, left = {}, {}, [len(w) for w in wants]
        for r in range(N):
            last, b = {b: scores[r, b] for b in range(8)}, 4
            for j in line[r, "t"]:
                if reader[j] is not None:
                    extra[j] = (b, last[b])
                    for d in last[b]:
                        more.setdefault(d, []).append(j)
                    left[j] += len(last[b])
                    last[b] = [reader[j]]
                    b = (b + 1) % 8
        where, pos = [None] * n, {w: 0 for w in line}
        for w, l in line.items():
            for j in l:
                where[j] = w
        ready, end, why = [[0.0] * n for p in paces], [[0.0] * n for p in paces], [[None] * n for p in paces]
        free, busy, seen = {}, {}, [False] * n
        todo = [l[0] for l in line.values() if l and not left[l[0]]]
        while todo:
            j = todo.pop()
            w = where[j]
            if behind[j] is not None and not seen[behind[j]]:
                return None
            seen[j] = True
            f, b, held = free.get(w), busy.get(lane[j]), []
            for p in paces:
                s = ready[p][j]
                if f is not None and f[1][p] >= s:
                    s, why[p][j] = f[1][p], (f[0], True)
                e = s + lasts[j][p]
                held.append(e)
                if moves[j] is not None:
                    e = s + begins[p] + (0.0 if w[0] in busy else FIRST)
                    if b is not None and end[p][b] > e:
                        e, why[p][j] = end[p][b], (b, True)
                    e += moves[j][p]
                end[p][j] = e if lands[j] is None else lands[j]
            if moves[j] is not None:
                busy[lane[j]] = busy[w[0]] = j
            free[w] = (j, held)
            pos[w] += 1
            if pos[w] < len(line[w]) and not left[line[w][pos[w]]]:
                todo.append(line[w][pos[w]])
            for u in feeds[j] + more.get(j, []):
                for p in paces:
                    t = end[p][j] + wakes[p]
                    if t > ready[p][u]:
                        ready[p][u], why[p][u] = t, (j, False)
                left[u] -= 1
                if not left[u] and line[where[u]][pos[where[u]]] == u:
                    todo.append(u)
        if not all(seen):
            return None
        tails = [[end[p][line[r, "s"][-1]] for r in range(N)] for p in paces]
        return sum((max(t) + EVEN * sum(t) / N) / scales[p] for p, t in enumerate(tails)) / (1 + EVEN), end, why, where, extra, tails

    left = [len(wants[j]) + (behind[j] is not None) for j in range(n)]
    done = [j for j in range(n) if not left[j]]
    for j in done:
        for u in feeds[j] + leads[j]:
            left[u] -= 1
            if not left[u]:
                done.append(u)
    top, where = None, None
    for turn in range(TURNS):
        line, done = forwards(backwards(done, where))
        now = run(line)
        where = now[3]
        if top is None or now[0] < top[0][0]:
            top = now, line

    tally, named, names = {}, {}, []
    for j in range(n):
        name = (key[j][0], task[j]["part"], task[j]["q"])
        tally[name] = tally.get(name, 0) + 1
        names.append(name[1:] + (tally[name],))
        named[key[j][0], names[j]] = j
    alike = [[named.get((r, names[j])) for r in range(N)] for j in range(n)]
    now, line, state = top[0], dict(top[1]), [SEED]

    def draw(m):
        state[0] = (state[0] * 1103515245 + 12345) % 2 ** 31
        return state[0] // 64 % m

    for turn in range(MENDS):
        total, end, why, where, extra, tails = now
        p = draw(len(PACES))
        r = max(range(N), key=lambda r: tails[p][r]) if draw(3) else draw(N)
        j, held = line[r, "s"][-1], []
        while why[p][j] is not None:
            i, same = why[p][j]
            if same and where[i] == where[j] and i not in wants[j]:
                held.append((i, j))
            j = i
        i, j = held[draw(len(held))]
        kind, far, lag, old = draw(8), draw(4) if draw(2) else 0, 0.1 * draw(4), dict(line)
        either = [x for x in (0, 1) if len(task[(i, j)[x]]["q"]) > 1]
        x = either[draw(len(either))] if either else None
        for i, j in [(i, j)] if draw(3) == 0 else zip(alike[i], alike[j]):
            if i is None or j is None or where[i] != where[j]:
                continue
            w = where[j]
            l = line[w] = list(line[w])
            if kind < 2 and either:
                y, o = (i, j)[x], (w[0], "a" if w[1] == "v" else "v")
                l.remove(y)
                m = line[o] = list(line[o])
                s = max([end[p][d] for d in wants[y]] + [0.0]) + lag
                m.insert(len([1 for u in m if end[p][u] <= s]), y)
            elif l.index(i) < l.index(j) and kind < 5:
                a = l.index(i)
                l.remove(j)
                l.insert(max(0, a - far), j)
            elif l.index(i) < l.index(j):
                l.remove(i)
                l.insert(l.index(j) + 1 + far, i)
        new = run(line)
        if new is not None and new[0] <= total + HEAT * (1.0 - turn / MENDS) * draw(100) / 100.0:
            now = new
            if new[0] < top[0][0]:
                top = new, dict(line)
        else:
            line = old
    return {w: [key[j][1] for j in l] for w, l in top[1].items()}, {key[j]: (b, [key[d][1] for d in ds]) for j, (b, ds) in top[0][4].items()}, top[0][0]


PLANS = {}


def rank_program(g, core, T, topo):
    me = T.rank_of(core)
    if me is None:
        return
    cores = list(T.cores)
    if not PLANS:
        PLANS["plan"] = plan([graph(r, cores, topo, T, g) for r in range(N)])
    order, extra, _ = PLANS["plan"]
    tasks = graph(me, cores, topo, T, g)[0]
    queue = {"v": g.vector, "a": g.scalar, "t": g.tensor, "p": g, "s": g.sync}

    token, count = {}, {}
    for q in queue:
        for i in order[me, q]:
            t = tasks[i]
            if "to" in t:
                count["loc"] = count.get("loc", 0) + 8
                continue
            s, n = t["sem"] if "sem" in t else ("sp%d" % sum(1 for c in count if c.startswith("sp")) if q == "p" else "s" + q, 1)
            count[s] = count.get(s, 0) + n
            token[i] = (s, count[s])
    for q in queue:
        seen = {}
        for i in order[me, q]:
            t = tasks[i]
            bank, freed = extra.get((me, i), (None, []))
            if "of" in t:
                bank = extra[me, t["of"]][0]
            want = {}
            for d in t["deps"] + freed:
                s, n = d if isinstance(d, tuple) else token[d]
                want[s] = max(want.get(s, 0), n)
            for s, n in want.items():
                if seen.get(s, 0) < n:
                    queue[q].wait_ge(T.sem[s], n)
                    seen[s] = n
            ins = t["call"](q, bank)
            if i in token:
                ins.then_inc(T.sem[token[i][0]], t["sem"][1] if "sem" in t else 1)

    for s, n in count.items():
        g.wait_ge(T.sem[s], n)
